import numpy as np, ml_dtypes
CORES = [1,5,17,21,33,37,49,53]
N = 8
BF = ml_dtypes.bfloat16
def gentries(a):
    return np.ascontiguousarray(a.reshape(8, 16, -1).transpose(0, 2, 1)).reshape(8, -1)
def gtable(e):
    e = np.asarray(e); return np.ascontiguousarray(e.reshape(8, -1, 16).transpose(0, 2, 1)).reshape(128, -1).astype(np.int32)
L, V, W, RO, MP = 256, 1024, 4096, 3, 5
HN, HZ = [1, 3, 6], [7, 2, 5]
def parts(rng):
    return (rng.integers(0, 256, (N, 8, 16, W)), rng.integers(0, W, (N, 8, 16, V)), rng.integers(0, 256, (N, 8, 16, L)),
            rng.integers(0, V, (N, 8, L)), rng.integers(1, 4096, (N, 8, 16, 1)), rng.integers(0, 256, (N, 8, RO)))
def pack(x, b, z, v, w, t):
    return {"xt": np.ascontiguousarray(x.reshape(N, 128, W)).astype(np.float32).astype(BF), "bag": np.ascontiguousarray(b.reshape(N, 128, V)).astype(np.int32),
            "z0": np.ascontiguousarray(z.reshape(N, 128, L)).astype(np.float32).astype(BF), "v0": np.stack([gtable(a) for a in v]),
            "uw": np.ascontiguousarray(w.reshape(N, 128, 1)).astype(np.int32), "bt": np.ascontiguousarray(t).astype(np.int32)}
def setup_inputs(rng):
    return pack(*parts(rng))
def setup_inputs_spread(rng):
    x, b, z, v, w, t = parts(rng)
    x = np.minimum((np.exp2(8 * rng.random((N, 8, 1, W))) * rng.random(x.shape) * 1.2).astype(np.int64), 255)
    z = np.minimum((np.exp2(8 * rng.random((N, 8, 1, L))) * rng.random(z.shape) * 1.2).astype(np.int64), 255)
    p = rng.choice(np.array([1, 2, 3, 5]), (N, 8, 1, 1))
    b = np.minimum((W * rng.random(b.shape) ** p).astype(np.int64), W - 1); v = np.minimum((V * rng.random(v.shape) ** p[..., 0]).astype(np.int64), V - 1)
    w = np.minimum(np.maximum(np.exp2(12 * rng.random(w.shape)).astype(np.int64), 1), 4095); t = np.minimum(np.exp2(8 * rng.random(t.shape)).astype(np.int64) - 1, 255)
    return pack(x, b, z, v, w, t)
def twos(rng, n):
    a = rng.integers(0, 2, (N, 8, 16, n))
    return 255 * np.where(rng.random((N, 8, 1, n)) < 0.5, a[:, :, :1], a)
def setup_inputs_ends(rng):
    x, b, z, v, w, t = parts(rng)
    x = twos(rng, W); z = twos(rng, L); x[:, 1::2, :, 0] = 0; x[:, 1::2, :, W - 1] = 255
    eb = (W - 1) * rng.integers(0, 2, b.shape); ev = (V - 1) * rng.integers(0, 2, v.shape)
    kb = rng.random(b.shape) < 0.7; kv = rng.random(v.shape) < 0.7; kb[:, 3::4] = True; kv[:, 3::4] = True
    b = np.where(kb, eb, b); v = np.where(kv, ev, v)
    b[:, 7, :, V - 1] = W - 1; b[:, 7, 0, V - 1] = 0
    b[:, 7, :, 0] = W - 1; b[:, 7, 1::2, 0] = 0
    v[:, :, 0] = 0; v[:, :, L - 1] = V - 1; v[:, 7, 4] = V - 1; v[:, 7, 7] = 0
    z[:, 7, :, L - 1] = 255; z[:, 7, :, 4] = 255; z[:, 7, :, 7] = 0; z[:, 6, :, L - 1] = 255; z[:, 6, :, 2] = 0
    w = np.where(rng.random(w.shape) < 0.5, 1, 4095); w[:, 7] = 4095; w[:, 6] = 1
    t = 255 * rng.integers(0, 2, t.shape); t[:, 7, 0] = 255; t[:, 6, 0] = 0
    return pack(x, b, z, v, w, t)
def setup_inputs_corners(rng):
    x, b, z, v, w, t = parts(rng); lane = np.arange(L)
    for g in range(3):
        h = 5 * g + 1; x[:, g] = 0; x[:, g, h] = np.arange(W) & 255; z[:, g] = 0
        be = rng.integers(0, 61, N); be[0] = (0, 1, 60)[g]; be[N - 1] = (60, 0, 1)[g]; t[:, g, 0] = be
        v[:, g] = np.argsort(rng.random((N, V)), axis=1)[:, :L]
        for r in range(N):
            e = int(be[r]); m = rng.integers(100, 180, (L, 1)); c = np.array([0, max(e - 1, 0), e, e + 1])
            q = np.concatenate([m - rng.choice(c, (L, MP - 1)), m, m + rng.choice(c, (L, 15 - MP))], axis=1)
            q = np.concatenate([np.zeros((L, 1), np.int64), rng.permuted(q, axis=1)], axis=1)
            b[r, g, :, v[r, g]] = q + 256 * rng.integers(0, W // 256, (L, 16))
            z[r, g, h] = m[:, 0] + rng.choice(np.array([-e - 1, -e, -1, 0, e, e + 1]), L)
    v[:, 3] = lane; t[:, 3] = 255
    v[:, 4] = np.where(rng.random((N, L)) < 0.5, rng.choice(np.array([0, V - 1, V // 2 - 1, V // 2]), (N, L)), lane); t[:, 4] = 0
    v[:, 5] = (lane >> 1) + V // 2 * (lane & 1); b[:, 5, :, V // 2:] = b[:, 5, :, :V // 2]
    b[:, 6] = np.where(rng.random((N, 1, V)) < 0.5, b[:, 6, :1], b[:, 6])
    p0 = np.take_along_axis(b[:, 6, 0], v[:, 6], 1); z[:, 6, :, ::2] = np.take_along_axis(x[:, 6], p0[:, None, :], 2)[:, :, ::2]
    own = 16 * ((V - 1 - np.arange(V)) & (L - 1)) + rng.integers(0, 16, (N, 16, V))
    b[:, 7] = np.where(rng.random((N, 16, V)) < 0.7, own, rng.choice(np.array([0, W - 1]), (N, 16, V))); v[:, 7] = V - 1 - lane
    z[:, 7] = 255 * rng.integers(0, 2, (N, 1, L)); w[:, 7] = rng.choice(np.array([1, 4095]), (N, 16, 1))
    return pack(x, b, z, v, w, t)
def setup_inputs_crowd(rng):
    x, b, z, v, w, t = parts(rng); lane = np.arange(L)
    for g in range(8):
        p = int(rng.integers(1, V // 2 - 2)) if g != 7 else V - 1; c = int(rng.integers(0, W)); q = int(rng.integers(0, L - 1))
        x[:, g, :, c] = 0; b[:, g, 0, p] = c; v[:, g] = p
        small = rng.integers(0, 21, (N, 16, L))
        if g in (0, 1, 2, 7): z[:, g] = small
        if g in (3, 4): z[:, g] = 255 - small
        if g == 1: v[:, g, q] = p + 1
        if g == 2: v[:, g] = p + V // 2 * (lane & 1); b[:, g, :, p + V // 2] = b[:, g, :, p]
        if g == 4: z[:, g, :, q] = small[:, :, q]
        if g == 5: v[:, g] = rng.choice(np.array([p, 0, V - 1]), (N, L)); b[:, g] = rng.choice(np.array([0, c, W // 2, W // 2 + 5, W - 1]), (N, 16, V))
        if g == 7: v[:, g, L - 1] = 0
    return pack(x, b, z, v, w, t)
def check_inputs(d):
    bad = []
    for k, lo, hi in (("xt", 0, 255), ("bag", 0, W - 1), ("z0", 0, 255), ("v0", 0, V - 1), ("uw", 1, 4095), ("bt", 0, 255)):
        a = np.asarray(d[k]).astype(np.float64)
        if not np.all((a >= lo) & (a <= hi)): bad.append("range of " + k)
        elif not np.all(a == np.floor(a)): bad.append("whole numbers of " + k)
    return bad
def reference(xt, bag, z0, v0, uw, bt):
    X = xt.astype(np.float32).astype(np.int64).reshape(N, 8, 16, W); B = bag.astype(np.int64).reshape(N, 8, 16, V)
    z = z0.astype(np.float32).astype(np.int64).reshape(N, 8, 16, L); v = np.stack([gentries(a) for a in v0]).astype(np.int64)
    wt = uw.astype(np.int64).reshape(N, 8, 16, 1); bands = bt.astype(np.int64); A = np.zeros((N, 8, L), np.int64)
    lane = np.arange(L); k = np.arange(16).reshape(1, 1, 16, 1); ri = np.arange(N).reshape(N, 1, 1); gi = np.arange(8).reshape(1, 8, 1)
    u = np.add.reduce(wt * z, axis=2) & (W - 1)
    for t in range(RO):
        P = np.take_along_axis(B, v[:, :, None, :], 3)
        flat = np.ascontiguousarray(P.transpose(0, 1, 3, 2)).reshape(N, 8, 1, 16 * L)
        x = np.take_along_axis(X, flat, 3).reshape(N, 8, 16, L, 16)
        D = np.add.reduce(np.abs(x - x[..., :1]), axis=2)
        o = np.argsort(D, axis=3, kind="stable")
        m = np.take_along_axis(D, o[..., MP:MP + 1], 3)[..., 0]; e = o[..., 15][:, :, None, :]
        beta = bands[:, :, t][:, :, None] + 32 * A; q = np.add.reduce(np.abs(z - x[..., 0]), axis=2)
        far = q >= m; amb = np.abs(q - m) <= beta
        D = D.transpose(0, 1, 3, 2); m = m[:, :, None]; be = beta[:, :, None]
        M = np.where(np.abs(D - m) <= be, P, -1)
        sn = [(r - HN[t]) % N for r in range(N)]; sz = [(r - HZ[t]) % N for r in range(N)]
        M2 = M[sn]; z2 = z[sz]; a2 = amb[sz]
        side = np.where(far[:, :, None], D > m + be, D < m - be)
        F = np.where(side, P, np.where(M2 >= 0, M2, (P + (2 * k + 1) * u[:, :, None]) & (W - 1)))
        fe = np.take_along_axis(F, e, 2); F = np.where(k == e, F[:, :, :1], np.where(k == 0, fe, F))
        w = (2 * v + 1 + far) & (V - 1)
        top = np.full((N, 8, V), -1, np.int64); np.maximum.at(top, (ri, gi, w), np.broadcast_to(lane, w.shape))
        r_, g_, i_ = np.nonzero(np.take_along_axis(top, w, 2) == lane)
        B[r_, g_, :, w[r_, g_, i_]] = F[r_, g_, :, i_]
        c = np.broadcast_to((16 * lane + (u & 15))[:, :, None, :], z.shape)
        np.put_along_axis(X, c, (np.take_along_axis(X, c, 3) + z) & 255, 3)
        z = np.where(a2[:, :, None], (z + z2) >> 1, z); u = np.add.reduce(wt * z, axis=2) & (W - 1)
        v = np.where(a2, u & (V - 1), w); A = amb.astype(np.int64)
    return {"yx": X.reshape(N, 128, W).astype(np.float32).astype(BF), "yb": (B[..., :V // 2] + W * B[..., V // 2:]).reshape(N, 128, V // 2).astype(np.float32),
            "yz": z.reshape(N, 128, L).astype(np.float32).astype(BF), "yv": np.stack([gtable(a) for a in v]).astype(np.float32)}

@@ -1,0 +1,671 @@
+import numpy as np
+from concourse.bass import DstId, RemoteDMATransfer
+from concourse.mybir import AluOpType as Alu, ActivationFunctionType as Act
+
+N, L, NV, W, RO = 8, 256, 1024, 4096, 3
+HN, HZ = [1, 3, 6], [7, 2, 5]
+BIG = 8192.0
+SB = 16384.0
+NB, NF = 12, 16
+F32, BF, F16, I32, U16 = "float32", "bfloat16", "float16", "int32", "uint16"
+
+SCRATCH = {}
+
+
+def _sb(name, shape, dt):
+    SCRATCH[name] = ("sbuf", [128] + shape, dt)
+
+
+for _n, _s, _d in [
+    ("X", [W], BF), ("bagi", [NV], I32), ("B", [NV + L], F32), ("v0i", [16], I32), ("uwi", [4], I32), ("bti", [4], I32),
+    ("xg", [16 * L], BF), ("mx", [16, L], BF), ("Poff", [L], U16), ("Pc", [L], F16),
+    ("Dc", [L], F16), ("cs", [7, L], BF), ("cl", [L], F16), ("mask2", [L], BF), ("hi", [L], BF), ("lo", [L], BF),
+    ("sg", [L], BF), ("sq", [L], BF), ("Gs", [L], F32), ("Lt", [L], F32), ("scn", [L], F32), ("A32", [L], BF), ("vm", [L], BF),
+    ("yi", [L], I32), ("Fi", [L], I32), ("Fc", [L], F32), ("tF", [L], F16), ("t2", [L], F32), ("junk", [32, L], BF),
+    ("zm", [L], BF), ("xs", [L], BF), ("xm", [L], BF), ("pk", [NV // 2], F32),
+    ("ZZ0", [2 * L], BF), ("ZZ1", [2 * L], BF), ("ZZ2", [2 * L], BF), ("ZZ3", [L], BF),
+    ("ik", [16], F32), ("pci", [2], I32), ("ci", [8], I32), ("col", [32], F32), ("cb", [32], BF), ("bl", [48], F32), ("aq", [48], F32), ("li", [48], F32), ("T4", [NV], BF), ("jr", [L], BF), ("jr0", [L], BF),
+    ("ff", [16, 7], F32), ("gg", [16, 7], F32), ("kk", [16, 7], F32), ("ix", [144], F32), ("ms", [4, 144], BF),
+    ("pb", [16, NB], BF), ("pf", [16, NF], F16), ("BDb", [128, NB], BF), ("BDf", [128, NF], F16),
+    ("gm", [8], F32), ("gmb", [16], BF), ("DTs", [L], F16), ("mw", [144], F16), ("km1", [16], F32), ("dg", [16], F32), ("r0", [16], F32), ("wi", [48], I32), ("thr", [16], F32),
+    ("sc0", [128], F32), ("sc1", [128], F32), ("sc2", [128], F32), ("cst", [4, L], BF), ("btb", [4], BF), ("btc", [8], F32), ("uf", [4], F32),
+    ("base", [48], F32), ("dlt", [48], F32), ("prd", [48], F32), ("res", [48], F32), ("offs", [48], U16), ("aoff", [16], U16), ("woff", [16], U16),
+    ("ti", [96], I32), ("tf", [160], F32), ("N1", [16], F32), ("N2", [16], F32),
+]:
+    _sb(_n, _s, _d)
+for _t in range(RO):
+    _sb("Pc%d" % _t, [L], F16); _sb("pr%d" % _t, [L], F16); _sb("zr%d" % _t, [L], BF)
+    _sb("hl%d" % _t, [2 * L], BF); _sb("hr%d" % _t, [2 * L], BF)
+    _sb("as%d" % _t, [48], F32); _sb("ar%d" % _t, [48], F32)
+for _b in range(8):
+    SCRATCH["p%d" % _b] = ("psum", [128, 512], F32)
+
+SEMAPHORES = ["eV", "eS", "eP", "eG", "sent"] + ["d%d" % i for i in range(24)] + ["r%d" % i for i in range(24)]
+
+FIG = {"cy": 1.04e-3, "gam": 1.62e-3, "sca": 3.95e-3, "pcy": 0.5e-3, "iss": 0.5, "hop": 3.0, "sync": 0.07}
+CFG = {"CH": [(0, 128), (128, 256)],
+       "MS": [(0, 128), (128, 256)],
+       "SC": [(0, 128), (128, 256)],
+       "UN": [(0, 64, 32), (64, 128, 0), (128, 192, 16), (192, 256, 0)],
+       "TG": [(0, 128), (128, 256)],
+       "NS": [4, 4, 4], "PS": [64], "XS": 1, "LO": "SVVV", "M2P": 1, "NG": [(0, 128), (128, 256)], "DT": [1, 1, 1], "Q2": 0, "SW": 1.0, "SEED": 0, "JIT": 0.0, "IT": 3}
+BIAS = {'Scol_17': -4.4, 'SN2_0': 0.4, 'Pp2_8': -3.3, 'Vscn_128': 1.4, 'Vcl_0': -1.4, 'Vmx_1_192': 0.7, 'Pp0_0': -3.0, 'Pp2_13': 2.7, 'Vxg_0': 0.6,
+        'SN2_4': -4.0, 'Pp7_384': -4.5, 'Voffs_16': -1.9, 'SA_0': -2.6, 'Vmx_8_192': 1.4, 'SN2_6': 1.6, 'Vtf_152': -2.4, 'Vcs_5_0': -2.7,
+        'Smask_0': -0.5, 'Vas_0': 0.5, 'Vti_48': 1.0, 'VtF_128': 0.5, 'Scs_0_128': -0.6, 'Vci_1': 4.0, 'VBDb_96_0': 3.7, 'Gsc_0': -2.7,
+        'Vcs_4_128': -0.6, 'Shl_0': -1.2, 'Pp1_256': 0.6, 'Vtf_128': 0.8, 'Vcs_4_0': -2.8, 'Vpf_0_0': 2.5, 'Scs_2_128': -0.9,
+        'SN2_0': -3.8, 'SN2_4': -3.2, 'Vmx_8_192': 2.0, 'Scs_0_128': -0.5, 'Sxg_512': 5.9, 'VBDf_32_0': 0.1, 'Scol_16': 3.9, 'Scol_12': -0.7, 'Vci_0': -1.4,
+        'Vmx_1_0': 0.6, 'Vti_40': 0.8, 'Vti_56': 5.1, 'SN2_12': -0.9, 'Pp5_384': 1.5, 'Gjr_0': -2.4, 'Vsc_0': 0.5, 'Spk_256': -1.7, 'Vbti_0': -0.3,
+        'Scol_6': -2.7, 'Vcol_0': 2.4, 'SN2_2': -1.3, 'Spb_0_8': -1.0, 'Pp4_0': 5.6, 'Ssg_0': -1.4, 'VPoff_0': -0.1, 'Vti_16': 1.1, 'Rhr_256': 0.1,
+        'Scs_3_0': 0.1, 'Vmw_0': -0.1, 'Vjr_0': 2.2, 'VBDb_80_0': 3.7, 'Vres_0': -0.3, 'Scol_15': -0.4, 'Gff_0_0': -1.0, 'Vt_128': -5.1,
+        'Smask_128': -0.6, 'Pp7_256': 0.1, 'Scb_16': 0.6, 'Pp6_256': -1.8}
+
+
+class Ap(tuple):
+    pass
+
+
+def ap(buf, *idx, part=None):
+    shape = SCRATCH[buf][1][1:]
+    idx = list(idx) + [slice(None)] * (len(shape) - len(idx))
+    reg, cnt = [], 1
+    for i, n in zip(idx, shape):
+        if isinstance(i, slice):
+            r = range(*i.indices(n)); reg.append((r[0], r[-1] + 1)); cnt *= len(r)
+        else:
+            reg.append((i, i + 1))
+    return Ap((buf, tuple(idx), tuple(reg), cnt, part, None))
+
+
+def ind(win, off):
+    return Ap((win[0], win[1], win[2], off[3] * 16, None, off))
+
+
+def s_(a, b, c=None):
+    return slice(a, b, c)
+
+
+def build(cfg=CFG):
+    ops = []; tab = []; stage = [0.0]; tail = {}
+    CH, MS, SC, UNS = cfg["CH"], cfg["MS"], cfg["SC"], cfg["UN"]
+
+    def add(eng, kind, args, reads, writes, cost, lat=0.0):
+        rd, wr = [], []
+        for a in reads:
+            if isinstance(a, Ap):
+                rd.append((a[0], a[2]))
+                if a[5] is not None: rd.append((a[5][0], a[5][2]))
+        for a in writes:
+            if isinstance(a, Ap):
+                wr.append((a[0], a[2]))
+                if a[5] is not None: rd.append((a[5][0], a[5][2]))
+            else:
+                wr.append(a)
+        banks = set(b for b, _ in rd + wr if b in SCRATCH and SCRATCH[b][0] == "psum")
+        ops.append({"eng": eng, "kind": kind, "args": args, "rd": rd, "wr": wr, "cost": cost, "lat": lat, "banks": banks, "after": [], "soft": [], "bias": stage[0]})
+        return len(ops) - 1
+
+    def chain(key, i):
+        if key in tail: ops[i]["soft"].append(tail[key])
+        if ops[i]["kind"] == "load": ops[i]["bias"] = 100.0 - i
+        tail[key] = i
+
+    def two(*a):
+        return all(SCRATCH[x[0]][2] in (BF, F16, U16) for x in a)
+
+    def vcost(out, in0, per):
+        if in0[5] is not None: return (0.05, in0[3], "gam")
+        if out[5] is not None: return (0.05, out[3], "sca")
+        return (0.0, max(64, out[3] * per), "cy")
+
+    def ts(out, in0, s1, s2, op0, op1=None):
+        return add("V", "ts", (out, in0, s1, s2, op0, op1), [in0, s1, s2], [out], vcost(out, in0, 0.5 if two(out, in0) else 1))
+
+    def tt(out, in0, in1, op):
+        ps = SCRATCH[in0[0]][0] == "psum" or SCRATCH[in1[0]][0] == "psum"
+        return add("V", "tt", (out, in0, in1, op), [in0, in1], [out], vcost(out, in0, 1 if ps else 2))
+
+    def tts(items):
+        return add("V", "tts", items, [x for a in items for x in a[1:3]], [a[0] for a in items], (0.0, sum(max(64, a[0][3]) for a in items), "cy"))
+
+    def cp(out, in0):
+        return add("V", "cp", (out, in0), [in0], [out], vcost(out, in0, 0.5 if two(out, in0) else 1))
+
+    def mset(out, v):
+        return add("V", "mset", (out, v), [], [out], vcost(out, out, 0.5 if two(out) else 1))
+
+    def scan(out, d0, d1):
+        return add("V", "scan", (out, d0, d1), [d0, d1], [out], vcost(out, out, 1))
+
+    def act(out, in0, fn, bias=0.0, scale=1.0, acc=None):
+        c = (0.065, in0[3], "gam") if in0[5] is not None else (0.02 if acc else 0.0, max(64, in0[3]), "cy")
+        if fn == Act.Sigmoid and not tab:
+            tab.append(1); c = (1.3, c[1], c[2])
+        return add("S", "act", (out, in0, fn, bias, scale, acc), [in0, bias, scale], [out] if acc is None else [acc], c)
+
+    def acts(items):
+        i = add("S", "acts", items, [x for a in items for x in (a[1], a[3])], [a[5] for a in items] + [a[0] for a in items],
+                (0.02 * len(items), sum(max(64, a[1][3]) for a in items), "cy"))
+        return i
+
+    def aff(out, in0, bias, scale, eng):
+        if eng == "S": return act(out, in0, Act.Identity, bias, scale)
+        return ts(out, in0, scale, bias, Alu.mult, Alu.add)
+
+    def mm(items, start=True, stop=True):
+        outs = [i[0] for i in items]
+        wr = outs + [("open" + o[0], ((0, 1),)) for o in outs if o[0] in ("p2", "p3")]
+        return add("P", "mm", items, [i[1] for i in items] + [i[2] for i in items], wr, (0.03, sum(max(64, i[2][3]) for i in items), "pcy"))
+
+    def grp(out, pairs, start=True, stop=True):
+        return [(out, a, b, start and i == 0, stop and i == len(pairs) - 1) for i, (a, b) in enumerate(pairs)]
+
+    def iota(out, pat, base, cm):
+        return add("G", "iota", (out, pat, base, cm), [], [out], (0.13, 2 * out[3], "cy"))
+
+    def load(q, buf, name, idx, us):
+        return add(q, "load", (buf, name, idx), [], [buf], (0.06, 0, "cy"), 1.6 + us)
+
+    def store(q, buf, name, idx, us):
+        return add(q, "store", (buf, name, idx), [buf], [], (0.06, 0, "cy"), 1.6 + us)
+
+    def send(*trs):
+        i = add("G", "send", trs, [x[0] for x in trs], [], (0.0, 1, "iss"))
+        j = add("R", "recv", trs, [], [x[1] for x in trs], (0.0, 1, "hop"))
+        ops[j]["after"].append(i)
+        return j
+
+    A = ap
+    C = lambda j: A("col", s_(j, j + 1))
+    mb = lambda m: A("BDb", s_(None, None), m)
+    mf = lambda m: A("BDf", s_(None, None), m)
+    pb = lambda m: A("pb", s_(None, None), m)
+    pf = lambda m: A("pf", s_(None, None), m)
+    sel = lambda m, r: A("ms", m, s_(15 - r, 143 - r))
+    ik = A("ik")
+
+    chain("ly", load("Y", A("bagi"), "bag", None, 1.5))
+    chain("ls", load("S", A("v0i"), "v0", None, 0.0))
+    chain("ls", load("S", A("ZZ0", s_(0, L)), "z0", None, 0.5))
+    chain("ls", load("S", A("uwi", s_(0, 1)), "uw", None, 0.5))
+    chain("ly", load("Y", A("X"), "xt", None, 3.5))
+    mset(A("bti"), 0)
+    chain("ly", load("Y", A("bti", s_(0, 3), part=s_(0, 128, 16)), "bt", None, 3.5))
+
+    iota(A("pci", s_(0, 1)), [[1, 1]], 0, 1)
+    iota(ik, [[1, 16]], 0, 0)
+    iota(A("ix"), [[1, 144]], 0, 0)
+    iota(A("ff"), [[1, 16], [1, 7]], 1, 0)
+    iota(A("gg"), [[-1, 16], [1, 7]], 1, 0)
+    iota(A("kk"), [[1, 16], [0, 7]], 0, 0)
+    iota(A("sc0"), [[0, 8], [1, 16]], 0, 0)
+    iota(A("jr0"), [[1, L]], 0, 0)
+    iota(A("T4"), [[0, 2], [4, 512]], -1024, 0)
+    J, GC, MC, NJ, PJ, J0, JG, NJG, C7, C6, NC6, NJ0, R13, R16, OFF, HALF, JB, NJB, JP, UH, UL, NOFF = range(22)
+    pci = A("pci", s_(0, 1))
+    ts(A("ci", s_(0, 1)), pci, 15, None, Alu.bitwise_and); cp(C(J), A("ci", s_(0, 1)))
+    ts(A("ci", s_(1, 2)), pci, 4, None, Alu.arith_shift_right); cp(C(GC), A("ci", s_(1, 2)))
+    ts(C(J0), C(J), 0.0, None, Alu.is_equal)
+    idn = Act.Identity
+    act(C(30), C(J), idn, -400 * 15.5, 400.0)
+    act(A("cb", s_(0, 7)), A("ik", s_(1, 8)), Act.Sigmoid, C(30), 400.0)
+    aff(C(MC), C(GC), 15.0, 16.0, "V")
+    aff(C(NJ), C(J), -7.5, -1.0, "V"); aff(C(PJ), C(J), -7.5, 1.0, "V")
+    for c, b, s in [(JG, 1.0, -1.0), (NJG, -1.0, 1.0), (C7, -1.0, 7.0), (C6, -1.0, 6.0), (NC6, 1.0, -6.0), (NJ0, 0.0, -1.0),
+                    (R13, 0.0, -13 * BIG), (R16, 0.0, 16 * BIG), (HALF, 0.5, -1.0), (JB, BIG, -BIG), (NJB, -BIG, BIG)]:
+        act(C(c), C(J0), idn, b, s)
+    ts(C(OFF), C(J), 14.5, SB, Alu.is_lt, Alu.mult)
+    act(C(NOFF), C(OFF), idn, 0.0, -1.0); act(C(29), C(OFF), idn, 200.0, -400.0)
+    ts(A("tf", s_(0, 1)), C(J), 1.0, None, Alu.add)
+    ts(C(JP), C(J), 14.5, A("tf", s_(0, 1)), Alu.is_lt, Alu.mult)
+    ts(A("gm"), A("ik", s_(0, 8)), C(GC), None, Alu.is_equal)
+    act(A("gmb", s_(0, 8)), A("gm"), idn, 0.0, 2.0); act(A("gmb", s_(8, 16)), A("gm"), idn, 0.0, -1.0)
+    ts(A("km1"), ik, 1.0, None, Alu.min)
+    ts(A("dg"), ik, C(J), None, Alu.is_equal)
+    ts(A("li", s_(0, 16)), ik, 16.0, C(J), Alu.mult, Alu.add)
+    act(A("li", s_(16, 32)), A("li", s_(0, 16)), idn, 1024.0, 1.0)
+    act(A("li", s_(32, 48)), A("li", s_(0, 16)), idn, 0.0, 16.0)
+    act(A("tf", s_(16, 32)), A("li", s_(0, 16)), idn, 255.0 / 128, -1.0 / 128)
+    act(A("base", s_(32, 48)), A("li", s_(0, 16)), idn)
+    mset(A("dlt", s_(32, 48)), 256.0)
+    ts(A("jr"), A("jr0"), 1.0 / 128, None, Alu.mult)
+    for m, v in enumerate([2048.0, -0.25, -2.0 ** 26, 10240.0]):
+        mset(A("cst", m), v)
+    mset(A("B", s_(NV, NV + L)), 0.0)
+    cp(A("uf", s_(0, 1)), A("uwi", s_(0, 1)))
+    act(A("tf", s_(32, 48)), ik, idn, 1.0, 2.0)
+    ts(A("wi", s_(0, 16)), A("tf", s_(32, 48)), A("uf", s_(0, 1)), 2048.0, Alu.mult, Alu.add)
+    ts(A("wi", s_(16, 32)), A("wi", s_(0, 16)), W - 1, None, Alu.bitwise_and)
+    ts(pf(15), A("wi", s_(16, 32)), -2048.0, None, Alu.add)
+    ts(C(UH), A("wi", s_(16, 17)), -2048.0, None, Alu.add)
+    ts(A("mw"), A("ix"), C(MC), C(UH), Alu.is_equal, Alu.mult)
+    if not all(cfg["DT"][:len(CH)]):
+        for m, v in enumerate([2.0, -1.0]):
+            ts(A("ms", m), A("ix"), C(MC), v, Alu.is_equal, Alu.mult)
+    dg = A("dg")
+    for m, v in [(7, 1.0), (8, -1.0), (10, -2.0 ** 25), (11, 0.5)]:
+        act(pb(m), dg, idn, 0.0, v)
+    act(pb(9), dg, idn, -1.0, 0.0)
+    for nm, bias, neg, pos, dst in [("ff", NJ, NJG, JG, A("pf", s_(None, None), s_(0, 7))), ("gg", PJ, NJB, JB, A("pb", s_(None, None), s_(0, 7)))]:
+        act(A(nm), A(nm), Act.Square, C(bias))
+        ts(A(nm), A(nm), 56.25, C(neg), Alu.is_equal, Alu.mult)
+        mset(A(nm, 0), 0.0)
+        if nm == "ff":
+            ts(A("kk"), A("kk"), C(J), C(JG), Alu.is_equal, Alu.mult)
+        else:
+            ts(A("kk"), A("kk"), BIG, None, Alu.mult)
+            ts(A("r0"), A("km1"), C(R13), C(R16), Alu.mult, Alu.add)
+            tt(A(nm, s_(None, None), 0), A(nm, s_(None, None), 0), A("r0"), Alu.add)
+        tt(dst, A(nm), A("kk"), Alu.add)
+    for m, v in [(7, C(JG)), (8, C(NJG)), (14, 1.0)]:
+        ts(pf(m), dg, v, None, Alu.mult)
+    ts(pf(9), ik, 0.0, C(J0), Alu.mult, Alu.add)
+    ts(pf(12), ik, 0.0, C(C7), Alu.mult, Alu.add)
+    ts(pf(10), A("km1"), C(J0), C(C6), Alu.mult, Alu.add)
+    ts(pf(11), A("km1"), C(NJ0), C(NC6), Alu.mult, Alu.add)
+    ts(pf(13), dg, -2.0, 1.0, Alu.mult, Alu.add)
+    for gq in range(8):
+        ts(A("BDb", s_(16 * gq, 16 * gq + 16)), A("pb"), A("gm", s_(gq, gq + 1)), None, Alu.mult)
+    for gq in range(8):
+        ts(A("BDf", s_(16 * gq, 16 * gq + 16)), A("pf"), A("gm", s_(gq, gq + 1)), None, Alu.mult)
+    IB, NI, NONE, MI, HI = mb(7), mb(8), mb(9), mb(10), mb(11)
+    ts(A("thr", s_(0, 7)), A("cb", s_(0, 7)), -1.0, C(HALF), Alu.mult, Alu.add)
+    act(A("thr", s_(8, 15)), A("thr", s_(0, 7)), idn, 0.0, -400.0)
+    ts(A("sc1"), A("sc0"), C(J), -3 * SB, Alu.is_equal, Alu.mult)
+    ts(A("sc2"), A("sc0"), C(JP), SB, Alu.is_equal, Alu.mult)
+    tt(A("sc1"), A("sc1"), A("sc2"), Alu.add)
+    cp(A("btb"), A("bti"))
+    mm(grp(A("p7", s_(0, 4)), [(NONE, A("btb"))]))
+    act(A("btc", s_(0, 4)), A("p7", s_(0, 4)), idn, 0.0, -1.0)
+    act(A("btc", s_(4, 8)), A("p7", s_(0, 4)), idn, -200.0, 400.0)
+
+    def ulist(z, zo):
+        out = A("p4", s_(0, 16))
+        mm(grp(out, [(A("mw", s_(15 - r, 143 - r)), A(z, s_(zo + r, zo + L, 16))) for r in range(16)]))
+        cp(A("ti", s_(0, 16)), out)
+
+    cp(A("offs", s_(0, 16)), A("v0i")); cp(A("res", s_(0, 16)), A("v0i"))
+    ulist("ZZ0", 0)
+    ts(A("ti", s_(16, 32)), A("ti", s_(0, 16)), 15, None, Alu.bitwise_and)
+    tt(A("res", s_(16, 32)), A("ti", s_(16, 32)), A("li", s_(32, 48)), Alu.add)
+    cp(A("offs", s_(16, 32)), A("res", s_(16, 32)))
+
+    for t in range(RO):
+        Z = "ZZ%d" % t; z = A(Z, s_(0, L)); last = t == RO - 1
+        voff = A("offs", s_(0, 16)); coff = A("offs", s_(16, 32))
+        cut = [0] + (cfg["PS"] if t else []) + [L]
+        for a, b in zip(cut, cut[1:]):
+            vo = A("offs", s_(a // 16, b // 16))
+            if t == 0:
+                cp(A("Poff", s_(a, b)), ind(A("bagi"), vo))
+            else:
+                chain("vg", ts(A("Poff", s_(a, b)), ind(A("B", s_(0, NV)), vo), 2048.0, None, Alu.add))
+        Pn = "Pc%d" % t; HL = "hl%d" % t
+        ts(A(Pn), A("Poff"), -2048.0, None, Alu.add)
+        send((z, A("zr%d" % t), HZ[t]), (A(Pn), A("pr%d" % t), HN[t]))
+        act(A("vm"), ind(A("T4"), voff), Act.Copy)
+        act(A("tf", s_(64, 80)), A("res", s_(0, 16)), idn, 0.0, 2.0)
+        act(A("base", s_(16, 32)), A("res", s_(16, 32)), idn)
+        bl = A("bl")
+        if t == 0:
+            act(bl, A("li"), idn, A("btc", s_(0, 1)), 0.0)
+        else:
+            act(bl, A("as%d" % (t - 1)), idn, A("btc", s_(t, t + 1)), 32.0)
+        if cfg["XS"]:
+            act(A("zm"), ind(A("X"), coff), idn, -256.0, 1.0)
+            xp = A("p1", s_(128, 128 + L))
+            mm(grp(xp, [(IB, A("zm")), (IB, z)]))
+            act(A("xs"), xp, idn)
+        else:
+            act(A("zm"), z, idn, -256.0, 1.0)
+            tt(A("xs"), ind(A("X"), coff), A("zm"), Alu.add)
+        ts(A("xm"), A("xs"), 0.0, 256.0, Alu.is_lt, Alu.mult)
+        for c, (a, b) in enumerate(CH):
+            n = b - a; ln = s_(a, b); pd = "p%d" % (2 + c % 2)
+            xk = lambda p, q, k: A("xg", s_(16 * p + k, 16 * q, 16))
+            KL = ([1, 2, 3, 4, 5, 6, 7], [8, 9, 10, 11, 12], [13, 14, 15, 0])
+            for iu, (u0, u1, nv) in enumerate(UNS):
+                if u0 < a or u1 > b: continue
+                stage[0] = cfg["SW"] * (L - u1) / 64
+                UN = u1 - u0; lu = s_(u0, u1); x0 = A("p%d" % (iu % 2), s_(0, UN)); D = A(pd, s_(u0 - a, u1 - a)); um = u0 + nv
+                if um > u0:
+                    chain("vg", cp(A("xg", s_(16 * u0, 16 * um)), ind(A("X"), A("Poff", s_(u0, um)))))
+                if um < u1:
+                    chain("sg", act(A("xg", s_(16 * um, 16 * u1)), ind(A("X"), A("Poff", s_(um, u1))), Act.Copy))
+                dt_ = cfg["DT"][c]
+                mm(grp(x0, [(IB, xk(u0, u1, 0))]))
+                if not dt_:
+                    mm(grp(D, [(NONE, xk(u0, u1, 0)), (sel(1, 0), A(Z, lu))] + [(sel(1, k), xk(u0, u1, k)) for k in range(1, 16)], stop=False))
+                for kl in KL:
+                    chain("mx", tts([(A("mx", k, lu), xk(u0, u1, k) if k else A(Z, lu), x0, Alu.max) for k in kl]))
+                    if not dt_:
+                        mm(grp(D, [(sel(0, k), A("mx", k, lu)) for k in kl], start=False, stop=0 in kl))
+            Dc = A("Dc", ln); cl = A("cl", ln); tp = A(pd, s_(128, 128 + n))
+            if dt_:
+                pn = s_(0, n); DT = lambda k: A(pd, s_(k, 128, 16), part=pn)
+                two_, neg_ = A("gmb", s_(0, 8)), A("gmb", s_(8, 16))
+                mm([(A(pd, s_(0, 128), part=pn), xk(a, b, 0), NONE, True, False)]
+                   + [(DT(k), xk(a, b, k), neg_, False, False) for k in range(1, 16)] + [(DT(0), A(Z, ln), neg_, False, False)])
+                for kl in KL:
+                    mm([(DT(k), A("mx", k, ln), two_, False, k == 0) for k in kl])
+                DTs = A("DTs", s_(128 * (c % 2), 128 * (c % 2) + 128), part=pn)
+                ts(DTs, A(pd, s_(0, 128), part=pn), -2048.0, None, Alu.add)
+                mm(grp(A(pd, s_(384, 384 + n)), [(DTs, A("BDf", s_(0, n), 14, part=pn))]))
+                cp(Dc, A(pd, s_(384, 384 + n)))
+            else:
+                ts(Dc, A(pd, s_(0, n)), -2048.0, None, Alu.add)
+            ns = cfg["NS"][c]; nb = ns if 3 <= ns <= 4 or n <= 64 else 4
+            dif = lambda s: A("p4", s_(s * n, s * n + n)) if s < nb else A("p5", s_((s - nb) * n, (s - nb + 1) * n))
+            for r_ in (range(nb), range(nb, 7)):
+                if len(r_): mm([(dif(s), mf(s), Dc, True, True) for s in r_])
+            for s in range(7):
+                if s < ns:
+                    act(A("cs", s, ln), dif(s), Act.Sigmoid, A("thr", s_(8 + s, 9 + s)), 400.0)
+                else:
+                    ts(A("cs", s, ln), dif(s), A("thr", s_(s, s + 1)), None, Alu.is_gt)
+            so = sorted(range(7), key=lambda s: s if s < ns else s - ns + 0.5)
+            mm(grp(tp, [(mf(7), Dc)] + [(mb(s), A("cs", s, ln)) for s in so[:4]], stop=False))
+            mm(grp(tp, [(mb(s), A("cs", s, ln)) for s in so[4:]], start=False))
+            ts(cl, tp, -2048.0, 2048.0, Alu.max, Alu.min)
+            act(A("mask2", ln), tp, Act.Sigmoid, -9.5 * BIG, 1.0)
+            band = [(NI, A("A32", ln))] if t else []
+            E1, Q1 = A("p6", s_(2 * a, 2 * a + n)), A("p6", s_(2 * a + n, 2 * b))
+            E2, Q2 = A("p7", s_(2 * a, 2 * a + n)), A("p7", s_(2 * a + n, 2 * b))
+            mm(grp(E1, band + [(mf(7), Dc), (mf(10), cl)]))
+            mm(grp(E2, band + [(mf(8), Dc), (mf(11), cl)]))
+            if cfg["Q2"]: mm(grp(Q1, [(mf(9), Dc), (mf(12), cl)]))
+            else: Q1 = Q2
+            mm(grp(Q2, [(mf(9), Dc), (mf(12), cl)]))
+            act(A(HL, s_(2 * a, 2 * a + n)), E1, Act.Sigmoid, A("btc", s_(4 + t, 5 + t)), 400.0)
+            if cfg["LO"][c] == "V":
+                ts(A(HL, s_(2 * a + n, 2 * b)), E2, A("btc", s_(t, t + 1)), None, Alu.is_gt)
+            else:
+                act(A(HL, s_(2 * a + n, 2 * b)), E2, Act.Sigmoid, A("btc", s_(4 + t, 5 + t)), 400.0)
+            if cfg["M2P"]:
+                act(A(pd, s_(256, 256 + n)), tp, Act.Sigmoid, -9.5 * BIG, 1.0)
+            for (ma, mb_) in MS:
+                if mb_ == b: send((A(HL, s_(2 * ma, 2 * b)), A("hr%d" % t, s_(2 * ma, 2 * b)), HN[t]))
+            stage[0] = 0.0
+            act(A("sg", ln), Q1, Act.Sign, 0.5, 1.0)
+            scan(A("scn", ln), A("sc1", s_(0, n)), Q2)
+            for (ta, tb) in cfg["TG"]:
+                if tb != b: continue
+                o = lambda x: s_(x + ta // 16, x + tb // 16)
+                act(A("cb", o(16)), A("scn", s_(ta + 15, tb, 16)), Act.Sigmoid, C(29), 400.0)
+                tt(A("ti", o(32)), A("tf", o(64)), A("cb", o(16)), Alu.add)
+                ts(A("ti", o(48)), A("ti", o(32)), NV - 1, None, Alu.bitwise_and)
+                ts(A("tf", o(128)), A("ti", o(48)), -2.0, 1025.0 - 255.5 / 128, Alu.mult, Alu.add)
+                tt(A("tf", o(144)), A("tf", o(128)), A("tf", o(16)), Alu.add)
+                kp = lambda x, y: A("p6", s_(2 * ta + x - ta, 2 * ta + y - ta))
+                mm(grp(kp(ta, tb), [(IB, A(x, s_(ta, tb))) for x in ("vm", "jr", "sg")]))
+                for (sa, sb) in SC:
+                    if sa < ta or sb > tb: continue
+                    for h in range(sa // 16, sb // 16, 2):
+                        acts([(A("junk", kb - 128 + s, s_(0, sb - 16 * s)), kp(16 * s, sb), Act.Sign, A("tf", s_(kb + s, kb + s + 1)), 1.0, A(acc, s_(s, s + 1)))
+                              for s in (h, h + 1) for kb, acc in ((128, "N2"), (144, "N1"))])
+        if t == 0:
+            ts(A("B", s_(0, NV)), A("bagi"), -2048.0, None, Alu.add)
+        tt(ind(A("X"), coff), A("xs"), A("xm"), Alu.add)
+        ql = A("scn", s_(15, L, 16))
+        for e in range(3):
+            act(A("aq", s_(16 * e, 16 * e + 16)), ql, Act.Abs, C(NOFF))
+        tt(A("as%d" % t), A("aq"), bl, Alu.is_le)
+        send((A("as%d" % t), A("ar%d" % t), HZ[t]))
+        if last:
+            i = store("Y", A("X"), "yx", None, 5.0)
+            ops[i]["after"] += [j for j, o_ in enumerate(ops) if o_["kind"] == "send"]
+        ts(A("ti", s_(64, 80)), A("ti", s_(32, 48)), 1.0, None, Alu.add)
+        wl = A("ti", s_(80, 96))
+        ts(wl, A("ti", s_(64, 80)), NV - 1, None, Alu.bitwise_and)
+        cp(A("base", s_(0, 16)), wl)
+        up, Pt, Gp = A("p0", s_(0, L)), A("p0", s_(L, 2 * L)), A("p1", s_(0, L))
+        for (a, b) in CH:
+            mm(grp(A("p0", s_(a, b)), [(IB, A(HL, s_(2 * a, a + b))), (NI, A(HL, s_(a + b, 2 * b))), (IB, A("sg", s_(a, b)))]))
+        act(A("sq"), up, Act.Square, 0.0, 4096.0)
+        mm(grp(Gp, [(mf(15), z), (mf(14), A(Pn))]))
+        act(A("Gs"), Gp, idn, 2048.0 - 2.0 ** 23, 1.0)
+        mm(grp(Pt, [(IB, A("cst", 2)), (IB, A("sq")), (IB, A("cst", 3)), (mf(14), A(Pn))]))
+        tt(A("Lt"), A("Gs"), Pt, Alu.max)
+        for (a, b) in cfg["NG"]:
+            sl = s_(a // 16, b // 16); o = lambda x: s_(x + a // 16, x + b // 16)
+            tt(A("N1", sl), A("N1", sl), A("N2", sl), Alu.is_gt)
+            tt(A("N1", sl), A("N1", sl), A("li", o(16)), Alu.mult)
+            tt(A("N1", sl), A("N1", sl), A("base", o(0)), Alu.max)
+            cp(A("woff", sl), A("N1", sl))
+        if not last:
+            ts(A("aoff"), A("as%d" % t, s_(0, 16)), 8.0, 256.0, Alu.mult, Alu.add)
+            act(A("A32"), ind(A("T4"), A("aoff")), Act.Copy)
+        zp = A("p1", s_(L, 2 * L))
+        mm(grp(zp, [(IB, A("cst", 1)), (HI, z), (HI, A("zr%d" % t))]))
+        ts(A(Z, s_(L, 2 * L)), zp, 1.5 * 2 ** 23, 1.5 * 2 ** 23, Alu.add, Alu.subtract)
+        ulist(Z, L)
+        ts(A("ti", s_(16, 32)), A("ti", s_(0, 16)), NV - 1, None, Alu.bitwise_and)
+        tt(A("dlt", s_(0, 16)), A("ti", s_(16, 32)), A("base", s_(0, 16)), Alu.subtract)
+        if not last:
+            ts(A("wi", s_(0, 16)), A("ti", s_(0, 16)), 15, None, Alu.bitwise_and)
+            tt(A("wi", s_(16, 32)), A("wi", s_(0, 16)), A("li", s_(32, 48)), Alu.add)
+            tt(A("dlt", s_(16, 32)), A("wi", s_(16, 32)), A("base", s_(16, 32)), Alu.subtract)
+        for c, (a, b) in enumerate(MS):
+            ln = s_(a, b); pb_ = "p%d" % (3 - c % 2); Y, H = A(pb_, s_(0, b - a)), A("p5", s_(L + a, L + b))
+            for (ca, cb) in CH:
+                if ca < a or cb > b: continue
+                Yc = A(pb_, s_(ca - a, cb - a)); hr = "hr%d" % t
+                mm(grp(Yc, [(IB, A("cst", 0, s_(ca, cb))), (mf(14), A("pr%d" % t, s_(ca, cb)))], stop=False))
+                mm(grp(Yc, [(MI, A(hr, s_(2 * ca, ca + cb))), (MI, A(hr, s_(ca + cb, 2 * cb)))], start=False))
+            chain("po", tt(A("yi", ln), A("Lt", ln), Y, Alu.max))
+            ts(A("Fi", ln), A("yi", ln), W - 1, None, Alu.bitwise_and)
+            ts(A("Fc", ln), A("Fi", ln), -2048.0, None, Alu.add)
+            if cfg["M2P"]:
+                tt(A("tF", ln), A("Fc", ln), A("p%d" % (2 + c % 2), s_(256, 256 + b - a)), Alu.mult)
+            else:
+                tt(A("tF", ln), A("Fc", ln), A("mask2", ln), Alu.mult)
+            mm(grp(H, [(mf(13), A("tF", ln))]))
+            tt(A("t2", ln), A("mask2", ln), H, Alu.mult)
+            for (sa, sb) in SC:
+                if a <= sa and sb <= b:
+                    chain("po", tt(ind(A("B"), A("woff", s_(sa // 16, sb // 16))), A("Fc", s_(sa, sb)), A("t2", s_(sa, sb)), Alu.add))
+        tt(A("prd"), A("ar%d" % t), A("dlt"), Alu.mult)
+        tt(A("res"), A("prd"), A("base"), Alu.add)
+        cp(A("offs"), A("res"))
+        act(A("ZZ%d" % (t + 1), s_(0, L)), ind(A(Z), A("offs", s_(32, 48))), Act.Copy)
+    store("Y", A("res", s_(0, 16)), "yv", None, 0.0)
+    store("Y", A("ZZ3"), "yz", None, 0.3)
+    h = NV // 4
+    for e in range(2):
+        pp = A("p%d" % (6 + e), s_(0, h))
+        act(pp, A("B", s_(2 * h + e * h, 3 * h + e * h)), idn, 2048.0 * 4097, 4096.0)
+        tt(A("pk", s_(e * h, e * h + h)), A("B", s_(e * h, e * h + h)), pp, Alu.add)
+        store("YS"[e], A("pk", s_(e * h, e * h + h)), "yb", (e * h, e * h + h), 0.5)
+    return ops
+
+
+def overlap(a, b):
+    return all(x[0] < y[1] and y[0] < x[1] for x, y in zip(a, b))
+
+
+def deps(ops):
+    n = len(ops); pred = [set(o["after"]) for o in ops]
+    hist = {}
+    for i, o in enumerate(ops):
+        for b, r in o["rd"]:
+            for j, rj, w in hist.get(b, ()):
+                if w and overlap(r, rj): pred[i].add(j)
+        for b, r in o["wr"]:
+            for j, rj, w in hist.get(b, ()):
+                if overlap(r, rj): pred[i].add(j)
+        for b, r in o["wr"]:
+            hist[b] = [h for h in hist.get(b, []) if not all(x[0] <= y[0] and y[1] <= x[1] for x, y in zip(r, h[1]))] + [(i, r, True)]
+        for b, r in o["rd"]:
+            hist.setdefault(b, []).append((i, r, False))
+        pred[i].discard(i)
+    succ = [[] for _ in ops]
+    for i in range(n):
+        for j in pred[i] | set(ops[i]["soft"]): succ[j].append(i)
+    return pred, succ
+
+
+def tag(o):
+    b, r = (o["wr"] or o["rd"])[0]
+    return o["eng"] + (b if b[0] == "p" or b[0] == "N" else b.rstrip("0123")) + "_" + "_".join(str(x[0]) for x in r)
+
+
+def costs(ops, fig):
+    return [o["cost"][0] + o["cost"][1] * fig[o["cost"][2]] for o in ops]
+
+
+def place(ops, pred, succ, prio, fig, back=False):
+    n = len(ops); c = costs(ops, fig); sy = fig["sync"]
+    if back:
+        pred, succ = succ, [p | set(o["soft"]) for p, o in zip(pred, ops)]
+    left = [len(p) if back else len(p | set(o["soft"])) for p, o in zip(pred, ops)]; ready = [i for i in range(n) if not left[i]]
+    beg = [0.0] * n; fin = [0.0] * n; busy = {}; seq = []
+    while ready:
+        i = max(ready, key=lambda k: prio[k]); ready.remove(i); o = ops[i]; e = o["eng"]
+        t = max([fin[j] + (0.0 if e == "P" == ops[j]["eng"] else sy) for j in pred[i]] + [beg[j] + c[j] for j in o["soft"] if not back], default=0.0)
+        if back: t += o["lat"]
+        if e != "R":
+            iv = [(a, b) for a, b, _ in busy.get(e, ()) if b > t]
+            for k in o["banks"]:
+                iv += [(a - sy, b + sy) for a, b, f in busy.get(k, ()) if f != e and b + sy > t]
+            for a, b in sorted(iv):
+                if t + c[i] <= a + 1e-9: break
+                t = max(t, b)
+            for k in [e] + list(o["banks"]):
+                busy.setdefault(k, []).append((t, t + c[i], e))
+        beg[i] = t; fin[i] = t + c[i] + (0.0 if back else o["lat"]); seq.append(i)
+        for k in succ[i]:
+            left[k] -= 1
+            if not left[k]: ready.append(k)
+    if back: return fin
+    order = sorted(seq, key=lambda k: beg[k])
+    full = [set(p) for p in pred]; last = {}
+    for i in order:
+        e = ops[i]["eng"]
+        for k in ops[i]["banks"]:
+            d = last.setdefault(k, {})
+            full[i].update(j for f, j in d.items() if f != e)
+            d[e] = i
+    return order, full, beg, fin
+
+
+def replay(ops, order, full, fig):
+    c = costs(ops, fig); sy = fig["sync"]; free = {}; fin = {}; beg = {}
+    for i in order:
+        e = ops[i]["eng"]
+        t = max([fin[j] + (0.0 if e == "P" == ops[j]["eng"] else sy) for j in full[i]], default=0.0)
+        if e != "R":
+            t = max(t, free.get(e, 0.0)); free[e] = t + c[i]
+        beg[i] = t; fin[i] = t + c[i] + ops[i]["lat"]
+    return max(fin.values()), beg, fin
+
+
+def plan(ops, seed=None, dp=None, fig=FIG):
+    seed = CFG["SEED"] if seed is None else seed
+    pred, succ = dp or deps(ops)
+    n = len(ops); c = costs(ops, fig); prio = [0.0] * n
+    jit = np.random.RandomState(seed).uniform(1 - CFG["JIT"], 1 + CFG["JIT"], n)
+    for i in range(n - 1, -1, -1):
+        prio[i] = (c[i] + ops[i]["lat"] + fig["sync"]) * float(jit[i]) + max([prio[k] for k in succ[i]], default=0.0)
+    prio = [p + o["bias"] + BIAS.get(tag(o), 0.0) for p, o in zip(prio, ops)]
+    best = None
+    for _ in range(CFG["IT"]):
+        order, full, beg, fin = place(ops, pred, succ, prio, fig)
+        if best is None or max(fin) < max(best[3]): best = (order, full, beg, fin)
+        if CFG["IT"] > 1:
+            prio = place(ops, pred, succ, fin, fig, True)
+    return best
+
+
+PLAN = []
+
+
+def rank_program(g, core, T, topo):
+    rank = T.rank_of(core)
+    if rank is None:
+        return
+    if not PLAN:
+        o_ = build(); PLAN.append(o_); PLAN.append(plan(o_))
+    ops, (order, pred, _b, _f) = PLAN
+    Q = {"V": g.vector, "S": g.scalar, "P": g.tensor, "G": g, "Y": g.sync}
+    cores = T.cores
+    eng = [e for e in topo.engines(cores[0], cores[1]) if all(e in topo.engines(a, b) for a in cores for b in cores if a != b)]
+    mask = sum(1 << e for e in eng)
+    comp = ("ts", "tt", "tts", "cp", "mset", "scan", "act", "acts", "mm", "iota")
+    pos = {}; cnt = {}
+    for i in order:
+        e = ops[i]["eng"]; cnt[e] = cnt.get(e, 0) + 1; pos[i] = cnt[e]
+    seen = {}; waits = {}; need = set()
+    for i in order:
+        e = ops[i]["eng"]; w = []
+        if e == "R": continue
+        best = {}
+        for j in pred[i]:
+            oj = ops[j]
+            if oj["kind"] in comp:
+                if e == "P" and oj["eng"] == "P": continue
+                if pos[j] > seen.get((e, oj["eng"]), 0) and pos[j] > pos.get(best.get(oj["eng"]), 0): best[oj["eng"]] = j
+            elif oj["kind"] != "send" and (e, j) not in seen:
+                seen[(e, j)] = 1; w.append(j)
+        for f, j in best.items():
+            seen[(e, f)] = pos[j]; need.add(j); w.append(j)
+        waits[i] = w
+    semof = {}; num = {}; nd = 0; nr = 0
+    for i in order:
+        o = ops[i]
+        if o["kind"] in comp:
+            if i in need:
+                num[o["eng"]] = num.get(o["eng"], 0) + 1; semof[i] = (T.sem["e" + o["eng"]], num[o["eng"]])
+        elif o["kind"] in ("load", "store"):
+            semof[i] = (T.sem["d%d" % nd], 16); nd += 1
+        elif o["kind"] == "recv":
+            semof[i] = (T.sem["r%d" % nr], len(eng)); semof[o["after"][0]] = semof[i]; nr += 1
+
+    def R(a):
+        if not isinstance(a, Ap): return a
+        v = T[a[0]][(a[4] if a[4] is not None else slice(None),) + a[1]]
+        return v.indirect(R(a[5])) if a[5] is not None else v
+
+    def hbm(name, idx):
+        return T[name][:] if idx is None else T[name][:, idx[0]:idx[1]]
+
+    sent = 0
+    for i in order:
+        o = ops[i]; k = o["kind"]; a = o["args"]
+        if k == "recv": continue
+        q = Q[o["eng"]]
+        for j in waits[i]:
+            q.wait_ge(*semof[j])
+        if k == "ts":
+            ins = q.tensor_scalar(R(a[0]), R(a[1]), R(a[2]), R(a[3]), a[4]) if a[5] is None else q.tensor_scalar(R(a[0]), R(a[1]), R(a[2]), R(a[3]), a[4], a[5])
+        elif k == "tt": ins = q.tensor_tensor(R(a[0]), R(a[1]), R(a[2]), a[3])
+        elif k == "tts":
+            for m in a: ins = q.tensor_tensor(R(m[0]), R(m[1]), R(m[2]), m[3])
+        elif k == "cp": ins = q.tensor_copy(R(a[0]), R(a[1]))
+        elif k == "mset": ins = q.memset(R(a[0]), a[1])
+        elif k == "scan": ins = q.tensor_tensor_scan(R(a[0]), R(a[1]), R(a[2]), 0.0, Alu.add, Alu.max)
+        elif k == "act":
+            ins = q.activation(R(a[0]), R(a[1]), a[2], bias=R(a[3]), scale=R(a[4]), accum_out=R(a[5]))
+        elif k == "acts":
+            for m in a: ins = q.activation(R(m[0]), R(m[1]), m[2], bias=R(m[3]), scale=m[4], accum_out=R(m[5]))
+        elif k == "mm":
+            for m in a: ins = q.matmul(R(m[0]), R(m[1]), R(m[2]), m[3], m[4])
+        elif k == "iota":
+            if SCRATCH[a[0][0]][2] == I32: ins = q.iota(R(a[0]), a[1], a[2], a[3])
+            else: ins = q.iota(R(a[0]), a[1], a[2], a[3], allow_small_or_imprecise_dtypes=True)
+        elif k == "load":
+            q.dma_start(R(a[0]), hbm(a[1], a[2])).then_inc(semof[i][0], 16); continue
+        elif k == "store":
+            if o["after"]: q.wait_ge(T.sem.sent, len(eng) * len(o["after"]))
+            q.dma_start(hbm(a[1], a[2]), R(a[0])).then_inc(semof[i][0], 16); continue
+        else:
+            sent += len(eng); to = [topo.addr(cores[(rank + x[2]) % N]) for x in a]
+            if len(a) == 1:
+                g.remote_dma(R(a[0][1]), R(a[0][0]), semof[i][0], T.sem.sent, to[0][1], to[0][0], mask)
+            else:
+                m = len(eng) // len(a)
+                g.remote_dma_fused([RemoteDMATransfer(dst_ids=[DstId(rid=to[j][0], pnc=to[j][1])], dma_engine_mask=sum(1 << e for e in eng[j * m:j * m + m]),
+                                                      remote_sem=semof[i][0], src=R(x[0]), dst=R(x[1])) for j, x in enumerate(a)], local_sem=T.sem.sent)
+            continue
+        if i in need: ins.then_inc(semof[i][0], 1)
+    for i in order:
+        if ops[i]["kind"] == "store": g.sync.wait_ge(*semof[i])
+    g.wait_ge(T.sem.sent, sent)

@@ -4,9 +4,8 @@ from concourse.mybir import AluOpType as Alu, ActivationFunctionType as Act
 
 N, L, NV, W, RO = 8, 256, 1024, 4096, 3
 HN, HZ = [1, 3, 6], [7, 2, 5]
-BIG = 8192.0
-SB = 16384.0
-NB, NF = 12, 16
+BIG = 4096.0
+NF = 20
 F32, BF, F16, I32, U16 = "float32", "bfloat16", "float16", "int32", "uint16"
 
 SCRATCH = {}
@@ -18,46 +17,47 @@ def _sb(name, shape, dt):
 
 for _n, _s, _d in [
     ("X", [W], BF), ("bagi", [NV], I32), ("B", [NV + L], F32), ("v0i", [16], I32), ("uwi", [4], I32), ("bti", [4], I32),
-    ("xg", [16 * L], BF), ("mx", [16, L], BF), ("Poff", [L], U16), ("Pc", [L], F16),
-    ("Dc", [L], F16), ("cs", [7, L], BF), ("cl", [L], F16), ("mask2", [L], BF), ("hi", [L], BF), ("lo", [L], BF),
-    ("sg", [L], BF), ("sq", [L], BF), ("Gs", [L], F32), ("Lt", [L], F32), ("scn", [L], F32), ("A32", [L], BF), ("vm", [L], BF),
-    ("yi", [L], I32), ("Fi", [L], I32), ("Fc", [L], F32), ("tF", [L], F16), ("t2", [L], F32), ("junk", [32, L], BF),
+    ("xg", [16 * L], BF), ("mx", [16, L], BF), ("ab", [4, 512], BF), ("Poff", [L], U16),
+    ("Dc", [L], F16), ("cs", [4, 7 * 128], BF), ("cl", [L], F16), ("mask2", [L], BF),
+    ("sq", [L], BF), ("Gs", [L], F32), ("Lt", [L], F32),
+    ("yi", [L], I32), ("Fi", [L], I32), ("Fc", [L], F32), ("tF", [L], F32), ("t2", [L], F32),
     ("zm", [L], BF), ("xs", [L], BF), ("xm", [L], BF), ("pk", [NV // 2], F32),
     ("ZZ0", [2 * L], BF), ("ZZ1", [2 * L], BF), ("ZZ2", [2 * L], BF), ("ZZ3", [L], BF),
-    ("ik", [16], F32), ("pci", [2], I32), ("ci", [8], I32), ("col", [32], F32), ("cb", [32], BF), ("bl", [48], F32), ("aq", [48], F32), ("li", [48], F32), ("T4", [NV], BF), ("jr", [L], BF), ("jr0", [L], BF),
-    ("ff", [16, 7], F32), ("gg", [16, 7], F32), ("kk", [16, 7], F32), ("ix", [144], F32), ("ms", [4, 144], BF),
-    ("pb", [16, NB], BF), ("pf", [16, NF], F16), ("BDb", [128, NB], BF), ("BDf", [128, NF], F16),
-    ("gm", [8], F32), ("gmb", [16], BF), ("DTs", [L], F16), ("mw", [144], F16), ("km1", [16], F32), ("dg", [16], F32), ("r0", [16], F32), ("wi", [48], I32), ("thr", [16], F32),
-    ("sc0", [128], F32), ("sc1", [128], F32), ("sc2", [128], F32), ("cst", [4, L], BF), ("btb", [4], BF), ("btc", [8], F32), ("uf", [4], F32),
-    ("base", [48], F32), ("dlt", [48], F32), ("prd", [48], F32), ("res", [48], F32), ("offs", [48], U16), ("aoff", [16], U16), ("woff", [16], U16),
-    ("ti", [96], I32), ("tf", [160], F32), ("N1", [16], F32), ("N2", [16], F32),
+    ("ik", [16], F32), ("pci", [2], I32), ("ci", [8], I32), ("col", [40], F32), ("cb", [8], BF), ("li", [48], BF),
+    ("ff", [16, 7], F32), ("gg", [16, 7], F32), ("kk", [16, 7], F32), ("ix", [144], BF), ("gx", [128], BF), ("ms", [5, 144], BF),
+    ("pf", [16, NF], F16), ("BD", [128, NF], F16), ("M", [22, 128], F16), ("MB", [2, 128], BF), ("T4", [NV], BF), ("vm", [L], BF), ("junk", [16, 128], BF), ("SW", [128], F32),
+    ("gm", [8], F32), ("mw", [144], F16), ("km1", [16], F32), ("dg", [16], F32), ("dgs", [16], F32), ("r0", [16], F32), ("wi", [32], I32),
+    ("thr", [16], F32), ("gmb", [16], BF), ("DTs", [L], F16), ("tH", [L], F16), ("sx", [L], BF), ("DC", [L], BF), ("SP", [L], BF), ("sc", [L], F32),
+    ("SQ", [L], BF), ("DG", [L], BF), ("sd", [2, L], BF), ("zh", [L], F16),
+    ("cst", [2, L], BF), ("btb", [4], BF), ("btc", [20], F32), ("uf", [4], F32), ("tf", [32], F32),
+    ("ti", [32], I32), ("tj", [48], I32), ("nb", [48], F16), ("dlt", [32], F16), ("prd", [32], F16),
+    ("kb", [16], F32), ("kc", [16], F16), ("ka", [16], F32), ("ki", [2, 16], I32), ("vi", [2, 16], I32), ("fl", [4, 16], F32), ("lf", [16], F32), ("woff", [16], U16), ("res", [16], F32),
 ]:
     _sb(_n, _s, _d)
 for _t in range(RO):
     _sb("Pc%d" % _t, [L], F16); _sb("pr%d" % _t, [L], F16); _sb("zr%d" % _t, [L], BF)
-    _sb("hl%d" % _t, [2 * L], BF); _sb("hr%d" % _t, [2 * L], BF)
-    _sb("as%d" % _t, [48], F32); _sb("ar%d" % _t, [48], F32)
+    _sb("hl%d" % _t, [2 * L], BF); _sb("hr%d" % _t, [2 * L], BF); _sb("bits%d" % _t, [L], BF)
+    _sb("as%d" % _t, [32], BF); _sb("ar%d" % _t, [32], BF)
+for _t in range(RO + 1):
+    _sb("offs%d" % _t, [64], U16)
 for _b in range(8):
     SCRATCH["p%d" % _b] = ("psum", [128, 512], F32)
 
 SEMAPHORES = ["eV", "eS", "eP", "eG", "sent"] + ["d%d" % i for i in range(24)] + ["r%d" % i for i in range(24)]
 
-FIG = {"cy": 1.04e-3, "gam": 1.62e-3, "sca": 3.95e-3, "pcy": 0.5e-3, "iss": 0.5, "hop": 3.0, "sync": 0.07}
+FIG = {"cy": 0.83e-3, "gam": 1.3e-3, "sca": 3.15e-3, "pcy": 0.42e-3, "iss": 0.5, "hop": 2.7, "sync": 0.15, "own": 0.19, "ov": 0.018}
 CFG = {"CH": [(0, 128), (128, 256)],
-       "MS": [(0, 128), (128, 256)],
-       "SC": [(0, 128), (128, 256)],
-       "UN": [(0, 64, 32), (64, 128, 0), (128, 192, 16), (192, 256, 0)],
-       "TG": [(0, 128), (128, 256)],
-       "NS": [4, 4, 4], "PS": [64], "XS": 1, "LO": "SVVV", "M2P": 1, "NG": [(0, 128), (128, 256)], "DT": [1, 1, 1], "Q2": 0, "SW": 1.0, "SEED": 0, "JIT": 0.0, "IT": 3}
-BIAS = {'Scol_17': -4.4, 'SN2_0': 0.4, 'Pp2_8': -3.3, 'Vscn_128': 1.4, 'Vcl_0': -1.4, 'Vmx_1_192': 0.7, 'Pp0_0': -3.0, 'Pp2_13': 2.7, 'Vxg_0': 0.6,
-        'SN2_4': -4.0, 'Pp7_384': -4.5, 'Voffs_16': -1.9, 'SA_0': -2.6, 'Vmx_8_192': 1.4, 'SN2_6': 1.6, 'Vtf_152': -2.4, 'Vcs_5_0': -2.7,
-        'Smask_0': -0.5, 'Vas_0': 0.5, 'Vti_48': 1.0, 'VtF_128': 0.5, 'Scs_0_128': -0.6, 'Vci_1': 4.0, 'VBDb_96_0': 3.7, 'Gsc_0': -2.7,
-        'Vcs_4_128': -0.6, 'Shl_0': -1.2, 'Pp1_256': 0.6, 'Vtf_128': 0.8, 'Vcs_4_0': -2.8, 'Vpf_0_0': 2.5, 'Scs_2_128': -0.9,
-        'SN2_0': -3.8, 'SN2_4': -3.2, 'Vmx_8_192': 2.0, 'Scs_0_128': -0.5, 'Sxg_512': 5.9, 'VBDf_32_0': 0.1, 'Scol_16': 3.9, 'Scol_12': -0.7, 'Vci_0': -1.4,
-        'Vmx_1_0': 0.6, 'Vti_40': 0.8, 'Vti_56': 5.1, 'SN2_12': -0.9, 'Pp5_384': 1.5, 'Gjr_0': -2.4, 'Vsc_0': 0.5, 'Spk_256': -1.7, 'Vbti_0': -0.3,
-        'Scol_6': -2.7, 'Vcol_0': 2.4, 'SN2_2': -1.3, 'Spb_0_8': -1.0, 'Pp4_0': 5.6, 'Ssg_0': -1.4, 'VPoff_0': -0.1, 'Vti_16': 1.1, 'Rhr_256': 0.1,
-        'Scs_3_0': 0.1, 'Vmw_0': -0.1, 'Vjr_0': 2.2, 'VBDb_80_0': 3.7, 'Vres_0': -0.3, 'Scol_15': -0.4, 'Gff_0_0': -1.0, 'Vt_128': -5.1,
-        'Smask_128': -0.6, 'Pp7_256': 0.1, 'Scb_16': 0.6, 'Pp6_256': -1.8}
+       "PS": [64],
+       "GA": [("V", 0, 64), ("S", 64, 128), ("S", 128, 192), ("S", 192, 256)],
+       "UN": [(0, 128, 0), (128, 192, 0), (192, 256, 0)],
+       "PL": [{"D": ("p2", 0), "A": ("p4", 0), "B": ("p5", 0), "E": ("p6", 0), "U": ("p2", 384), "H": ("p0", 384)},
+              {"D": ("p3", 0), "A": ("p0", 0), "B": ("p1", 0), "E": ("p7", 0), "U": ("p3", 384), "H": ("p1", 384)}],
+       "DUE": [("V:xs:0", "V:mx:0"), ("V:X:0", "V:cs:512"), ("V:ZZ:256", "V:cl:128"), ("S:vm:0", "S:Dc:128"), ("V:tj:16", "V:sc:0"),
+               ("V:Lt:128", "V:sc:0"), ("V:Lt:0", "V:sd:0"), ("V:woff:0", "V:yi:128"), ("V:t:0", "V:yi:128"), ("S:B:0", "S:ka:0"),
+               ("V:dlt:0", "V:yi:128")],
+       "AB": "p7", "ZC": 0, "ZP": ("p4", 0),
+       "DT": ["S", 0], "RW": 9, "NS": ["SS", "SV"], "HF": [0, 1], "RB": [0.0, 0.0], "UB": 0.0, "XV": 1, "LX": 1, "ZS": 0,
+       "NA": 8, "KL": 2, "XP": 128, "XB": 0.0, "PO": 128, "DC": "SS", "TI": "S", "TU": 1, "SW": 0.5, "IT": 2, "MOVES": 8000, "SEEDS": 3, "JIT": 0.1}
 
 
 class Ap(tuple):
@@ -86,7 +86,7 @@ def s_(a, b, c=None):
 
 def build(cfg=CFG):
     ops = []; tab = []; stage = [0.0]; tail = {}
-    CH, MS, SC, UNS = cfg["CH"], cfg["MS"], cfg["SC"], cfg["UN"]
+    CH = cfg["CH"]
 
     def add(eng, kind, args, reads, writes, cost, lat=0.0):
         rd, wr = [], []
@@ -94,6 +94,8 @@ def build(cfg=CFG):
             if isinstance(a, Ap):
                 rd.append((a[0], a[2]))
                 if a[5] is not None: rd.append((a[5][0], a[5][2]))
+            elif isinstance(a, tuple):
+                rd.append(a)
         for a in writes:
             if isinstance(a, Ap):
                 wr.append((a[0], a[2]))
@@ -101,7 +103,7 @@ def build(cfg=CFG):
             else:
                 wr.append(a)
         banks = set(b for b, _ in rd + wr if b in SCRATCH and SCRATCH[b][0] == "psum")
-        ops.append({"eng": eng, "kind": kind, "args": args, "rd": rd, "wr": wr, "cost": cost, "lat": lat, "banks": banks, "after": [], "soft": [], "bias": stage[0]})
+        ops.append({"eng": eng, "kind": kind, "args": args, "rd": rd, "wr": wr, "cost": cost, "lat": lat, "banks": banks, "after": [], "soft": [], "due": [], "bias": stage[0]})
         return len(ops) - 1
 
     def chain(key, i):
@@ -133,28 +135,36 @@ def build(cfg=CFG):
     def mset(out, v):
         return add("V", "mset", (out, v), [], [out], vcost(out, out, 0.5 if two(out) else 1))
 
-    def scan(out, d0, d1):
-        return add("V", "scan", (out, d0, d1), [d0, d1], [out], vcost(out, out, 1))
+    def scan(out, d0, d1, op0, op1):
+        return add("V", "scan", (out, d0, d1, op0, op1), [d0, d1], [out], vcost(out, out, 1))
 
     def act(out, in0, fn, bias=0.0, scale=1.0, acc=None):
         c = (0.065, in0[3], "gam") if in0[5] is not None else (0.02 if acc else 0.0, max(64, in0[3]), "cy")
         if fn == Act.Sigmoid and not tab:
             tab.append(1); c = (1.3, c[1], c[2])
-        return add("S", "act", (out, in0, fn, bias, scale, acc), [in0, bias, scale], [out] if acc is None else [acc], c)
+        return add("S", "act", (out, in0, fn, bias, scale, acc), [in0, bias, scale], [acc, out] if acc else [out], c)
 
-    def acts(items):
-        i = add("S", "acts", items, [x for a in items for x in (a[1], a[3])], [a[5] for a in items] + [a[0] for a in items],
-                (0.02 * len(items), sum(max(64, a[1][3]) for a in items), "cy"))
-        return i
+    def many(ids):
+        part = [ops.pop() for _ in ids][::-1]; o = dict(part[0])
+        o.update(kind="many", args=part, rd=sum([p["rd"] for p in part], []), wr=sum([p["wr"] for p in part], []),
+                 cost=(sum(p["cost"][0] for p in part), sum(p["cost"][1] for p in part), "cy"), banks=set().union(*[p["banks"] for p in part]))
+        ops.append(o)
+        return len(ops) - 1
 
     def aff(out, in0, bias, scale, eng):
         if eng == "S": return act(out, in0, Act.Identity, bias, scale)
         return ts(out, in0, scale, bias, Alu.mult, Alu.add)
 
-    def mm(items, start=True, stop=True):
+    def mm(items, area=()):
         outs = [i[0] for i in items]
-        wr = outs + [("open" + o[0], ((0, 1),)) for o in outs if o[0] in ("p2", "p3")]
-        return add("P", "mm", items, [i[1] for i in items] + [i[2] for i in items], wr, (0.03, sum(max(64, i[2][3]) for i in items), "pcy"))
+        keys = [("open" + b, ((0, 1),)) for b in set(o[0] for o in outs)]
+        first, final = items[0][3], items[-1][4]
+        c = sum(max(64, i[2][3]) * (4 if SCRATCH[i[2][0]][2] == F32 else 1) for i in items)
+        rd = [i[1] for i in items] + [i[2] for i in items]
+        if first and final: rd, wr = rd + keys, outs
+        elif first or final: wr = outs + keys + list(area)
+        else: rd, wr = outs + rd + keys, []
+        return add("P", "mm", items, rd, wr, (0.03, c, "pcy"))
 
     def grp(out, pairs, start=True, stop=True):
         return [(out, a, b, start and i == 0, stop and i == len(pairs) - 1) for i, (a, b) in enumerate(pairs)]
@@ -172,16 +182,15 @@ def build(cfg=CFG):
         i = add("G", "send", trs, [x[0] for x in trs], [], (0.0, 1, "iss"))
         j = add("R", "recv", trs, [], [x[1] for x in trs], (0.0, 1, "hop"))
         ops[j]["after"].append(i)
-        return j
+        return i
 
     A = ap
     C = lambda j: A("col", s_(j, j + 1))
-    mb = lambda m: A("BDb", s_(None, None), m)
-    mf = lambda m: A("BDf", s_(None, None), m)
-    pb = lambda m: A("pb", s_(None, None), m)
+    bd = lambda m: A("BD", s_(None, None), m)
     pf = lambda m: A("pf", s_(None, None), m)
+    M = lambda m: A("M", m)
     sel = lambda m, r: A("ms", m, s_(15 - r, 143 - r))
-    ik = A("ik")
+    ik = A("ik"); idn = Act.Identity; sig = Act.Sigmoid
 
     chain("ly", load("Y", A("bagi"), "bag", None, 1.5))
     chain("ls", load("S", A("v0i"), "v0", None, 0.0))
@@ -194,58 +203,62 @@ def build(cfg=CFG):
     iota(A("pci", s_(0, 1)), [[1, 1]], 0, 1)
     iota(ik, [[1, 16]], 0, 0)
     iota(A("ix"), [[1, 144]], 0, 0)
+    iota(A("gx"), [[1, 8], [0, 16]], 0, 0)
     iota(A("ff"), [[1, 16], [1, 7]], 1, 0)
     iota(A("gg"), [[-1, 16], [1, 7]], 1, 0)
     iota(A("kk"), [[1, 16], [0, 7]], 0, 0)
-    iota(A("sc0"), [[0, 8], [1, 16]], 0, 0)
-    iota(A("jr0"), [[1, L]], 0, 0)
+    iota(A("sx"), [[0, 16], [1, 16]], 0, 0)
     iota(A("T4"), [[0, 2], [4, 512]], -1024, 0)
-    J, GC, MC, NJ, PJ, J0, JG, NJG, C7, C6, NC6, NJ0, R13, R16, OFF, HALF, JB, NJB, JP, UH, UL, NOFF = range(22)
+    (J, GC, MC, NJ, PJ, J0, JG, NJG, NJ0, R13, R16, HALF, JB, NJB, PP, UH, J12, CC, A32, PC, S0, S1, C1, NC1, QS, QB, TW, J16) = range(28)
     pci = A("pci", s_(0, 1))
+    cp(C(PP), pci)
     ts(A("ci", s_(0, 1)), pci, 15, None, Alu.bitwise_and); cp(C(J), A("ci", s_(0, 1)))
     ts(A("ci", s_(1, 2)), pci, 4, None, Alu.arith_shift_right); cp(C(GC), A("ci", s_(1, 2)))
-    ts(C(J0), C(J), 0.0, None, Alu.is_equal)
-    idn = Act.Identity
-    act(C(30), C(J), idn, -400 * 15.5, 400.0)
-    act(A("cb", s_(0, 7)), A("ik", s_(1, 8)), Act.Sigmoid, C(30), 400.0)
+    ts(A("dg"), ik, C(J), None, Alu.is_equal)
+    dg = A("dg"); dgc = lambda j: A("dg", s_(j, j + 1))
+    J0c = dgc(0)
+    act(C(TW), C(J), idn, -400 * 15.5, 400.0)
+    act(A("cb", s_(0, 7)), A("ik", s_(1, 8)), sig, C(TW), 400.0)
     aff(C(MC), C(GC), 15.0, 16.0, "V")
     aff(C(NJ), C(J), -7.5, -1.0, "V"); aff(C(PJ), C(J), -7.5, 1.0, "V")
-    for c, b, s in [(JG, 1.0, -1.0), (NJG, -1.0, 1.0), (C7, -1.0, 7.0), (C6, -1.0, 6.0), (NC6, 1.0, -6.0), (NJ0, 0.0, -1.0),
-                    (R13, 0.0, -13 * BIG), (R16, 0.0, 16 * BIG), (HALF, 0.5, -1.0), (JB, BIG, -BIG), (NJB, -BIG, BIG)]:
-        act(C(c), C(J0), idn, b, s)
-    ts(C(OFF), C(J), 14.5, SB, Alu.is_lt, Alu.mult)
-    act(C(NOFF), C(OFF), idn, 0.0, -1.0); act(C(29), C(OFF), idn, 200.0, -400.0)
-    ts(A("tf", s_(0, 1)), C(J), 1.0, None, Alu.add)
-    ts(C(JP), C(J), 14.5, A("tf", s_(0, 1)), Alu.is_lt, Alu.mult)
+    for c, b, s in [(JG, 1.0, -1.0), (NJG, -1.0, 1.0), (R13, 0.0, -9 * BIG), (R16, 0.0, 12 * BIG), (HALF, 0.5, -1.0), (JB, BIG, -BIG),
+                    (NJB, -BIG, BIG), (C1, 12288.0, -2048.0), (QS, 400.0, -400.0)]:
+        act(C(c), J0c, idn, b, s)
+    act(C(NC1), C(C1), idn, 0.0, -1.0)
+    act(C(S0), J0c, idn, 0.0, 1.0 / 32); act(C(S1), J0c, idn, 0.0, -1.0 / 32); act(C(J16), C(J), idn, 0.0, 16.0)
+    tt(C(J12), dgc(1), dgc(2), Alu.add)
+    act(C(A32), C(J12), idn, 0.0, 32.0)
+    act(A("tf", s_(0, 1)), J0c, idn, 0.0, -9.0 * 2 ** 22)
+    ts(C(PC), dgc(1), 10240.0, A("tf", s_(0, 1)), Alu.mult, Alu.add)
+    act(A("tf", s_(1, 2)), J0c, idn, 400 * 12288.0, 200.0)
+    ts(C(QB), dgc(2), -800 * 12288.0, A("tf", s_(1, 2)), Alu.mult, Alu.add)
     ts(A("gm"), A("ik", s_(0, 8)), C(GC), None, Alu.is_equal)
-    act(A("gmb", s_(0, 8)), A("gm"), idn, 0.0, 2.0); act(A("gmb", s_(8, 16)), A("gm"), idn, 0.0, -1.0)
     ts(A("km1"), ik, 1.0, None, Alu.min)
-    ts(A("dg"), ik, C(J), None, Alu.is_equal)
     ts(A("li", s_(0, 16)), ik, 16.0, C(J), Alu.mult, Alu.add)
-    act(A("li", s_(16, 32)), A("li", s_(0, 16)), idn, 1024.0, 1.0)
-    act(A("li", s_(32, 48)), A("li", s_(0, 16)), idn, 0.0, 16.0)
-    act(A("tf", s_(16, 32)), A("li", s_(0, 16)), idn, 255.0 / 128, -1.0 / 128)
-    act(A("base", s_(32, 48)), A("li", s_(0, 16)), idn)
-    mset(A("dlt", s_(32, 48)), 256.0)
-    ts(A("jr"), A("jr0"), 1.0 / 128, None, Alu.mult)
-    for m, v in enumerate([2048.0, -0.25, -2.0 ** 26, 10240.0]):
-        mset(A("cst", m), v)
-    mset(A("B", s_(NV, NV + L)), 0.0)
+    ts(A("li", s_(16, 32)), ik, 256.0, C(J16), Alu.mult, Alu.add)
+    mset(A("li", s_(32, 48)), 1.0)
+    act(A("lf"), A("li", s_(0, 16)), idn, 1024.0, 1.0)
+    mset(A("ka"), 0.0)
+    mset(A("cst", 0), 2048.0)
+    ts(A("cst", 1), A("cst", 0), 0.0, C(PC), Alu.mult, Alu.add)
+    for m, v in enumerate([2.0, -1.0, J0c, C(J12), 1.0]):
+        ts(A("ms", m), A("ix"), C(MC), v, Alu.is_equal, Alu.mult)
+    IB, NI, HI, TWO, I256, NL, DJ, NDJ, ONE, NONE, EC1, EC2, MA, MF, QD, QC, QA, H64, N64, MF32, NF32 = [M(m) for m in range(21)]
+    MI = A("MB", 0)
+    for m, v in [(IB, 1.0), (NI, -1.0), (DJ, C(JG)), (NDJ, C(NJG)), (HI, 511.0 / 1024), (TWO, 2.0), (I256, 256.0), (NL, -1.0 / 32), (H64, 1.0 / 64), (N64, -1.0 / 64), (MI, -2.0 ** 25)]:
+        ts(m, A("ix", s_(0, 128)), C(PP), v, Alu.is_equal, Alu.mult)
+    ts(ONE, A("gx"), C(GC), None, Alu.is_equal)
+    ts(NONE, A("gx"), C(GC), -1.0, Alu.is_equal, Alu.mult)
+    for m, v in [(EC1, C(NJG)), (EC2, C(JG)), (MA, C(A32)), (MF, J0c), (MF32, C(S0)), (NF32, C(S1))]:
+        act(m, ONE, idn, 0.0, v)
     cp(A("uf", s_(0, 1)), A("uwi", s_(0, 1)))
-    act(A("tf", s_(32, 48)), ik, idn, 1.0, 2.0)
-    ts(A("wi", s_(0, 16)), A("tf", s_(32, 48)), A("uf", s_(0, 1)), 2048.0, Alu.mult, Alu.add)
+    act(A("tf", s_(16, 32)), ik, idn, 1.0, 2.0)
+    ts(A("wi", s_(0, 16)), A("tf", s_(16, 32)), A("uf", s_(0, 1)), 2048.0, Alu.mult, Alu.add)
     ts(A("wi", s_(16, 32)), A("wi", s_(0, 16)), W - 1, None, Alu.bitwise_and)
-    ts(pf(15), A("wi", s_(16, 32)), -2048.0, None, Alu.add)
+    ts(pf(18), A("wi", s_(16, 32)), -2048.0, None, Alu.add)
     ts(C(UH), A("wi", s_(16, 17)), -2048.0, None, Alu.add)
     ts(A("mw"), A("ix"), C(MC), C(UH), Alu.is_equal, Alu.mult)
-    if not all(cfg["DT"][:len(CH)]):
-        for m, v in enumerate([2.0, -1.0]):
-            ts(A("ms", m), A("ix"), C(MC), v, Alu.is_equal, Alu.mult)
-    dg = A("dg")
-    for m, v in [(7, 1.0), (8, -1.0), (10, -2.0 ** 25), (11, 0.5)]:
-        act(pb(m), dg, idn, 0.0, v)
-    act(pb(9), dg, idn, -1.0, 0.0)
-    for nm, bias, neg, pos, dst in [("ff", NJ, NJG, JG, A("pf", s_(None, None), s_(0, 7))), ("gg", PJ, NJB, JB, A("pb", s_(None, None), s_(0, 7)))]:
+    for nm, bias, neg, dst in [("ff", NJ, NJG, A("pf", s_(None, None), s_(0, 7))), ("gg", PJ, NJB, A("pf", s_(None, None), s_(7, 14)))]:
         act(A(nm), A(nm), Act.Square, C(bias))
         ts(A(nm), A(nm), 56.25, C(neg), Alu.is_equal, Alu.mult)
         mset(A(nm, 0), 0.0)
@@ -256,226 +269,273 @@ def build(cfg=CFG):
             ts(A("r0"), A("km1"), C(R13), C(R16), Alu.mult, Alu.add)
             tt(A(nm, s_(None, None), 0), A(nm, s_(None, None), 0), A("r0"), Alu.add)
         tt(dst, A(nm), A("kk"), Alu.add)
-    for m, v in [(7, C(JG)), (8, C(NJG)), (14, 1.0)]:
-        ts(pf(m), dg, v, None, Alu.mult)
-    ts(pf(9), ik, 0.0, C(J0), Alu.mult, Alu.add)
-    ts(pf(12), ik, 0.0, C(C7), Alu.mult, Alu.add)
-    ts(pf(10), A("km1"), C(J0), C(C6), Alu.mult, Alu.add)
-    ts(pf(11), A("km1"), C(NJ0), C(NC6), Alu.mult, Alu.add)
-    ts(pf(13), dg, -2.0, 1.0, Alu.mult, Alu.add)
+    act(pf(14), dg, idn, 1.0, -2.0)
+    ts(pf(15), ik, 1.5, 2.0, Alu.is_lt, Alu.mult)
+    ts(pf(19), pf(15), -1.0, None, Alu.add)
+    act(pf(16), A("km1"), idn)
+    ts(pf(17), ik, 15.5 - cfg["NA"], -1.0, Alu.is_lt, Alu.mult)
     for gq in range(8):
-        ts(A("BDb", s_(16 * gq, 16 * gq + 16)), A("pb"), A("gm", s_(gq, gq + 1)), None, Alu.mult)
-    for gq in range(8):
-        ts(A("BDf", s_(16 * gq, 16 * gq + 16)), A("pf"), A("gm", s_(gq, gq + 1)), None, Alu.mult)
-    IB, NI, NONE, MI, HI = mb(7), mb(8), mb(9), mb(10), mb(11)
+        ts(A("BD", s_(16 * gq, 16 * gq + 16)), A("pf"), A("gm", s_(gq, gq + 1)), None, Alu.mult)
+    act(A("SW"), bd(14), idn)
+    ts(QD, bd(19), J0c, None, Alu.mult); ts(QC, bd(19), C(NJG), None, Alu.mult); ts(QA, bd(16), C(A32), None, Alu.mult)
+    NX, MW = bd(17), bd(18)
     ts(A("thr", s_(0, 7)), A("cb", s_(0, 7)), -1.0, C(HALF), Alu.mult, Alu.add)
     act(A("thr", s_(8, 15)), A("thr", s_(0, 7)), idn, 0.0, -400.0)
-    ts(A("sc1"), A("sc0"), C(J), -3 * SB, Alu.is_equal, Alu.mult)
-    ts(A("sc2"), A("sc0"), C(JP), SB, Alu.is_equal, Alu.mult)
-    tt(A("sc1"), A("sc1"), A("sc2"), Alu.add)
+    act(A("gmb", s_(0, 8)), A("gm"), idn, 0.0, 2.0); act(A("gmb", s_(8, 16)), A("gm"), idn, 0.0, -1.0)
+    ts(A("SP"), A("sx"), 0.0, None, Alu.is_equal)
+    ts(A("DC"), A("sx"), C(J), 64.0, Alu.is_le, Alu.mult)
+    mset(A("DC", s_(0, L, 16)), 0.0)
+    if cfg["LX"]:
+        ts(A("SQ"), A("sx"), 0.0, -1024.0, Alu.is_equal, Alu.mult)
+        ts(A("DG"), A("sx"), C(J), -256.0, Alu.not_equal, Alu.mult)
     cp(A("btb"), A("bti"))
-    mm(grp(A("p7", s_(0, 4)), [(NONE, A("btb"))]))
-    act(A("btc", s_(0, 4)), A("p7", s_(0, 4)), idn, 0.0, -1.0)
-    act(A("btc", s_(4, 8)), A("p7", s_(0, 4)), idn, -200.0, 400.0)
+    mm(grp(A("p5", s_(496, 500)), [(NONE, A("btb"))]))
+    ts(A("tf", s_(4, 8)), A("km1", s_(0, 4)), -32.0, -0.5, Alu.mult, Alu.add)
+    tt(A("btc", s_(0, 4)), A("p5", s_(496, 500)), A("tf", s_(4, 8)), Alu.add)
+    ts(A("btc", s_(4, 8)), A("btc", s_(0, 4)), C(C1), 400.0, Alu.add, Alu.mult)
+    ts(A("btc", s_(8, 12)), A("btc", s_(0, 4)), C(NC1), 400.0, Alu.add, Alu.mult)
+    ts(A("btc", s_(16, 20)), A("btc", s_(0, 4)), C(QS), C(QB), Alu.mult, Alu.add)
+
+    LP = lambda a, b, c=None: A("p5", s_(384 + a, 384 + b, c))
+    li, li16, one = A("li", s_(0, 16)), A("li", s_(16, 32)), A("li", s_(32, 48))
 
     def ulist(z, zo):
-        out = A("p4", s_(0, 16))
-        mm(grp(out, [(A("mw", s_(15 - r, 143 - r)), A(z, s_(zo + r, zo + L, 16))) for r in range(16)]))
-        cp(A("ti", s_(0, 16)), out)
+        mm(grp(LP(0, 16), [(A("mw", s_(15 - r, 143 - r)), A(z, s_(zo + r, zo + L, 16))) for r in range(16)]))
 
-    cp(A("offs", s_(0, 16)), A("v0i")); cp(A("res", s_(0, 16)), A("v0i"))
+    def toint(out, in0):
+        return act(out, in0, idn) if cfg["TI"] == "S" else cp(out, in0)
+
+    cp(A("offs0", s_(0, 16)), A("v0i"))
+    ts(A("vi", 1), A("v0i"), NV // 2 - 1, None, Alu.bitwise_and); act(A("nb", s_(0, 16)), A("vi", 1), idn, -512.0, 2.0)
     ulist("ZZ0", 0)
-    ts(A("ti", s_(16, 32)), A("ti", s_(0, 16)), 15, None, Alu.bitwise_and)
-    tt(A("res", s_(16, 32)), A("ti", s_(16, 32)), A("li", s_(32, 48)), Alu.add)
-    cp(A("offs", s_(16, 32)), A("res", s_(16, 32)))
+    toint(A("ti", s_(0, 16)), LP(0, 16))
+    ts(A("tj", s_(0, 16)), A("ti", s_(0, 16)), 15, None, Alu.bitwise_and)
+    act(A("nb", s_(16, 32)), A("tj", s_(0, 16)), idn)
+    mm(grp(LP(64, 80), [(IB, A("nb", s_(16, 32))), (IB, li16)]))
+    cp(A("offs0", s_(32, 48)), LP(64, 80))
 
+    begin = []
     for t in range(RO):
+        begin.append(len(ops))
         Z = "ZZ%d" % t; z = A(Z, s_(0, L)); last = t == RO - 1
-        voff = A("offs", s_(0, 16)); coff = A("offs", s_(16, 32))
+        of = "offs%d" % t; coff = A(of, s_(32, 48)); bits = "bits%d" % t
         cut = [0] + (cfg["PS"] if t else []) + [L]
         for a, b in zip(cut, cut[1:]):
-            vo = A("offs", s_(a // 16, b // 16))
-            if t == 0:
-                cp(A("Poff", s_(a, b)), ind(A("bagi"), vo))
-            else:
-                chain("vg", ts(A("Poff", s_(a, b)), ind(A("B", s_(0, NV)), vo), 2048.0, None, Alu.add))
+            vo = A(of, s_(a // 16, b // 16))
+            chain("vg", cp(A("Poff", s_(a, b)), ind(A("B", s_(0, NV)) if t else A("bagi"), vo)))
         Pn = "Pc%d" % t; HL = "hl%d" % t
         ts(A(Pn), A("Poff"), -2048.0, None, Alu.add)
-        send((z, A("zr%d" % t), HZ[t]), (A(Pn), A("pr%d" % t), HN[t]))
-        act(A("vm"), ind(A("T4"), voff), Act.Copy)
-        act(A("tf", s_(64, 80)), A("res", s_(0, 16)), idn, 0.0, 2.0)
-        act(A("base", s_(16, 32)), A("res", s_(16, 32)), idn)
-        bl = A("bl")
         if t == 0:
-            act(bl, A("li"), idn, A("btc", s_(0, 1)), 0.0)
+            i = send((z, A("zr%d" % t), HZ[t])); ops[i]["bias"] = 50.0
+            send((A(Pn), A("pr%d" % t), HN[t]))
         else:
-            act(bl, A("as%d" % (t - 1)), idn, A("btc", s_(t, t + 1)), 32.0)
-        if cfg["XS"]:
-            act(A("zm"), ind(A("X"), coff), idn, -256.0, 1.0)
-            xp = A("p1", s_(128, 128 + L))
-            mm(grp(xp, [(IB, A("zm")), (IB, z)]))
-            act(A("xs"), xp, idn)
-        else:
+            send((z, A("zr%d" % t), HZ[t]), (A(Pn), A("pr%d" % t), HN[t]))
+        act(A("vm"), ind(A("T4"), A(of, s_(0, 16))), Act.Copy)
+        if cfg["XV"]:
             act(A("zm"), z, idn, -256.0, 1.0)
             tt(A("xs"), ind(A("X"), coff), A("zm"), Alu.add)
-        ts(A("xm"), A("xs"), 0.0, 256.0, Alu.is_lt, Alu.mult)
+        else:
+            act(A("zm"), ind(A("X"), coff), idn, -256.0, 1.0)
+        for e, a, b in cfg["GA"]:
+            stage[0] = cfg["SW"] * (L - b) / 64 + cfg["UB"]
+            src = ind(A("X"), A("Poff", s_(a, b)))
+            if e == "V": chain("vg", cp(A("xg", s_(16 * a, 16 * b)), src))
+            else: chain("sg", act(A("xg", s_(16 * a, 16 * b)), src, Act.Copy))
+        stage[0] = 0.0
+        xk = lambda p, q, k: A("xg", s_(16 * p + k, 16 * q, 16))
+
+        def at(c, key, i=0, p=0, q=None):
+            bank, off = cfg["PL"][c][key]; n = CH[c][1] - CH[c][0]
+            return A(bank, s_(off + i * n + p, off + i * n + (n if q is None else q)))
         for c, (a, b) in enumerate(CH):
-            n = b - a; ln = s_(a, b); pd = "p%d" % (2 + c % 2)
-            xk = lambda p, q, k: A("xg", s_(16 * p + k, 16 * q, 16))
-            KL = ([1, 2, 3, 4, 5, 6, 7], [8, 9, 10, 11, 12], [13, 14, 15, 0])
-            for iu, (u0, u1, nv) in enumerate(UNS):
+            n = b - a; ln = s_(a, b); pd = cfg["PL"][c]["D"][0]
+            for iu, (u0, u1, ns) in enumerate(cfg["UN"]):
                 if u0 < a or u1 > b: continue
-                stage[0] = cfg["SW"] * (L - u1) / 64
-                UN = u1 - u0; lu = s_(u0, u1); x0 = A("p%d" % (iu % 2), s_(0, UN)); D = A(pd, s_(u0 - a, u1 - a)); um = u0 + nv
-                if um > u0:
-                    chain("vg", cp(A("xg", s_(16 * u0, 16 * um)), ind(A("X"), A("Poff", s_(u0, um)))))
-                if um < u1:
-                    chain("sg", act(A("xg", s_(16 * um, 16 * u1)), ind(A("X"), A("Poff", s_(um, u1))), Act.Copy))
-                dt_ = cfg["DT"][c]
+                stage[0] = cfg["SW"] * (L - u1) / 64 + cfg["UB"]
+                un = u1 - u0; lu = s_(u0, u1); x0 = A("p%d" % (iu % 2), s_(0, un)); D = at(c, "D", 0, u0 - a, u1 - a)
+                kv = list(range(1, 16 - ns)) + [0]; step = -(-len(kv) // cfg["KL"])
                 mm(grp(x0, [(IB, xk(u0, u1, 0))]))
-                if not dt_:
-                    mm(grp(D, [(NONE, xk(u0, u1, 0)), (sel(1, 0), A(Z, lu))] + [(sel(1, k), xk(u0, u1, k)) for k in range(1, 16)], stop=False))
-                for kl in KL:
+                if ns:
+                    pe = cfg["AB"]
+                    mm([m for i in range(ns) for m in grp(A(pe, s_(i * un, i * un + un)), [(IB, xk(u0, u1, 16 - ns + i)), (NI, xk(u0, u1, 0))])])
+                    act(A("ab", iu % 4, s_(0, ns * un)), A(pe, s_(0, ns * un)), Act.Abs)
+                dt = cfg["DT"][c]
+                if not dt:
+                    raw = grp(D, [(NX if ns else NONE, xk(u0, u1, 0)), (sel(1, 0), A(Z, lu))] + [(sel(1, k), xk(u0, u1, k)) for k in kv[:-1]], u0 == a, False)
+                    for i in range(0, len(raw), cfg["RW"]): mm(raw[i:i + cfg["RW"]], [at(c, "D")])
+                for i in range(0, len(kv), step):
+                    kl = kv[i:i + step]
                     chain("mx", tts([(A("mx", k, lu), xk(u0, u1, k) if k else A(Z, lu), x0, Alu.max) for k in kl]))
-                    if not dt_:
-                        mm(grp(D, [(sel(0, k), A("mx", k, lu)) for k in kl], start=False, stop=0 in kl))
-            Dc = A("Dc", ln); cl = A("cl", ln); tp = A(pd, s_(128, 128 + n))
-            if dt_:
+                    if dt: continue
+                    if ns and 0 in kl:
+                        mm(grp(D, [(sel(4, 16 - ns + i), A("ab", iu % 4, s_(i * un, i * un + un))) for i in range(ns)], start=False, stop=False))
+                    mm(grp(D, [(sel(0, k), A("mx", k, lu)) for k in kl], start=False, stop=0 in kl and u1 == b), [at(c, "D")])
+            stage[0] = cfg["RB"][c]
+            Dc = A("Dc", ln); cl = A("cl", ln); tp = at(c, "D", 1); cs = lambda x: A("cs", c, s_(x * n, x * n + n))
+            if dt:
                 pn = s_(0, n); DT = lambda k: A(pd, s_(k, 128, 16), part=pn)
-                two_, neg_ = A("gmb", s_(0, 8)), A("gmb", s_(8, 16))
-                mm([(A(pd, s_(0, 128), part=pn), xk(a, b, 0), NONE, True, False)]
-                   + [(DT(k), xk(a, b, k), neg_, False, False) for k in range(1, 16)] + [(DT(0), A(Z, ln), neg_, False, False)])
-                for kl in KL:
-                    mm([(DT(k), A("mx", k, ln), two_, False, k == 0) for k in kl])
+                raw = ([(A(pd, s_(0, 128), part=pn), xk(a, b, 0), NONE, True, False)]
+                       + [(DT(k), xk(a, b, k) if k else A(Z, ln), A("gmb", s_(8, 16)), False, False) for k in range(16)])
+                for i in range(0, len(raw), cfg["RW"]): mm(raw[i:i + cfg["RW"]])
+                for i in range(0, 16, step):
+                    mm([(DT(k), A("mx", k, ln), A("gmb", s_(0, 8)), False, k == 0) for k in kv[i:i + step]], [A(pd, s_(0, 128))])
                 DTs = A("DTs", s_(128 * (c % 2), 128 * (c % 2) + 128), part=pn)
-                ts(DTs, A(pd, s_(0, 128), part=pn), -2048.0, None, Alu.add)
-                mm(grp(A(pd, s_(384, 384 + n)), [(DTs, A("BDf", s_(0, n), 14, part=pn))]))
-                cp(Dc, A(pd, s_(384, 384 + n)))
+                aff(DTs, A(pd, s_(0, 128), part=pn), -2048.0, 1.0, dt)
+                mm(grp(A(pd, s_(384, 384 + n)), [(DTs, A("M", 0, s_(0, n), part=pn))]))
+                aff(Dc, A(pd, s_(384, 384 + n)), 0.0, 1.0, cfg["DC"][c])
             else:
-                ts(Dc, A(pd, s_(0, n)), -2048.0, None, Alu.add)
-            ns = cfg["NS"][c]; nb = ns if 3 <= ns <= 4 or n <= 64 else 4
-            dif = lambda s: A("p4", s_(s * n, s * n + n)) if s < nb else A("p5", s_((s - nb) * n, (s - nb + 1) * n))
-            for r_ in (range(nb), range(nb, 7)):
-                if len(r_): mm([(dif(s), mf(s), Dc, True, True) for s in r_])
-            for s in range(7):
-                if s < ns:
-                    act(A("cs", s, ln), dif(s), Act.Sigmoid, A("thr", s_(8 + s, 9 + s)), 400.0)
-                else:
-                    ts(A("cs", s, ln), dif(s), A("thr", s_(s, s + 1)), None, Alu.is_gt)
-            so = sorted(range(7), key=lambda s: s if s < ns else s - ns + 0.5)
-            mm(grp(tp, [(mf(7), Dc)] + [(mb(s), A("cs", s, ln)) for s in so[:4]], stop=False))
-            mm(grp(tp, [(mb(s), A("cs", s, ln)) for s in so[4:]], start=False))
+                aff(Dc, at(c, "D"), -2048.0, 1.0, cfg["DC"][c])
+            dif = lambda s: at(c, "A", s) if s < 4 else at(c, "B", s - 4)
+            for so in (range(4), range(4, 7)):
+                mm([(dif(s), bd(s), Dc, True, True) for s in so])
+            for so, e in zip((range(4), range(4, 7)), cfg["NS"][c]):
+                if e == "S": many([act(cs(s), dif(s), sig, A("thr", s_(8 + s, 9 + s)), 400.0) for s in so])
+                else: many([ts(cs(s), dif(s), A("thr", s_(s, s + 1)), None, Alu.is_gt) for s in so])
+            so = [range(4), range(4, 7)] if cfg["NS"][c] == "SS" else [range(4, 7), range(4)]
+            mm(grp(tp, [(DJ, Dc)] + [(bd(7 + s), cs(s)) for s in so[0]], stop=False))
+            mm(grp(tp, [(bd(7 + s), cs(s)) for s in so[1]], start=False))
             ts(cl, tp, -2048.0, 2048.0, Alu.max, Alu.min)
-            act(A("mask2", ln), tp, Act.Sigmoid, -9.5 * BIG, 1.0)
-            band = [(NI, A("A32", ln))] if t else []
-            E1, Q1 = A("p6", s_(2 * a, 2 * a + n)), A("p6", s_(2 * a + n, 2 * b))
-            E2, Q2 = A("p7", s_(2 * a, 2 * a + n)), A("p7", s_(2 * a + n, 2 * b))
-            mm(grp(E1, band + [(mf(7), Dc), (mf(10), cl)]))
-            mm(grp(E2, band + [(mf(8), Dc), (mf(11), cl)]))
-            if cfg["Q2"]: mm(grp(Q1, [(mf(9), Dc), (mf(12), cl)]))
-            else: Q1 = Q2
-            mm(grp(Q2, [(mf(9), Dc), (mf(12), cl)]))
-            act(A(HL, s_(2 * a, 2 * a + n)), E1, Act.Sigmoid, A("btc", s_(4 + t, 5 + t)), 400.0)
-            if cfg["LO"][c] == "V":
-                ts(A(HL, s_(2 * a + n, 2 * b)), E2, A("btc", s_(t, t + 1)), None, Alu.is_gt)
-            else:
-                act(A(HL, s_(2 * a + n, 2 * b)), E2, Act.Sigmoid, A("btc", s_(4 + t, 5 + t)), 400.0)
-            if cfg["M2P"]:
-                act(A(pd, s_(256, 256 + n)), tp, Act.Sigmoid, -9.5 * BIG, 1.0)
-            for (ma, mb_) in MS:
-                if mb_ == b: send((A(HL, s_(2 * ma, 2 * b)), A("hr%d" % t, s_(2 * ma, 2 * b)), HN[t]))
+            act(A("mask2", ln), tp, sig, -16 * (9.5 * BIG - 8), 16.0)
+            if cfg["HF"][c]: act(at(c, "D", 2), tp, sig, -16 * (9.5 * BIG - 8), 16.0)
+            prev = A("bits%d" % (t - 1), ln) if t else None
+            E1, E2, Q, Gp = [at(c, "E", e) for e in range(4)]
+            hi, lo = A(HL, s_(2 * a, 2 * a + n)), A(HL, s_(2 * a + n, 2 * b))
+            mm(grp(Gp, [(MW, A(Z, ln)), (IB, A(Pn, ln))]))
+            act(A("Gs", ln), Gp, idn, 2048.0 - 2.0 ** 23, 1.0)
+            if t: mm([(E1, MA, prev, True, False), (E2, MA, prev, False, False), (Q, QA, prev, False, False)])
+            mm([(E1, DJ, Dc, not t, False), (E2, NDJ, Dc, False, False), (Q, QD, Dc, False, False)])
+            mm([(E1, EC1, cl, False, False), (E2, EC2, cl, False, False), (Q, QC, cl, False, True)])
+            many([act(hi, E1, sig, A("btc", s_(4 + t, 5 + t)), 400.0), act(lo, E2, sig, A("btc", s_(8 + t, 9 + t)), 400.0)])
+            send((A(HL, s_(2 * a, 2 * b)), A("hr%d" % t, s_(2 * a, 2 * b)), HN[t]))
+            act(A(bits, ln), Q, sig, A("btc", s_(16 + t, 17 + t)), 400.0)
             stage[0] = 0.0
-            act(A("sg", ln), Q1, Act.Sign, 0.5, 1.0)
-            scan(A("scn", ln), A("sc1", s_(0, n)), Q2)
-            for (ta, tb) in cfg["TG"]:
-                if tb != b: continue
-                o = lambda x: s_(x + ta // 16, x + tb // 16)
-                act(A("cb", o(16)), A("scn", s_(ta + 15, tb, 16)), Act.Sigmoid, C(29), 400.0)
-                tt(A("ti", o(32)), A("tf", o(64)), A("cb", o(16)), Alu.add)
-                ts(A("ti", o(48)), A("ti", o(32)), NV - 1, None, Alu.bitwise_and)
-                ts(A("tf", o(128)), A("ti", o(48)), -2.0, 1025.0 - 255.5 / 128, Alu.mult, Alu.add)
-                tt(A("tf", o(144)), A("tf", o(128)), A("tf", o(16)), Alu.add)
-                kp = lambda x, y: A("p6", s_(2 * ta + x - ta, 2 * ta + y - ta))
-                mm(grp(kp(ta, tb), [(IB, A(x, s_(ta, tb))) for x in ("vm", "jr", "sg")]))
-                for (sa, sb) in SC:
-                    if sa < ta or sb > tb: continue
-                    for h in range(sa // 16, sb // 16, 2):
-                        acts([(A("junk", kb - 128 + s, s_(0, sb - 16 * s)), kp(16 * s, sb), Act.Sign, A("tf", s_(kb + s, kb + s + 1)), 1.0, A(acc, s_(s, s + 1)))
-                              for s in (h, h + 1) for kb, acc in ((128, "N2"), (144, "N1"))])
-        if t == 0:
-            ts(A("B", s_(0, NV)), A("bagi"), -2048.0, None, Alu.add)
-        tt(ind(A("X"), coff), A("xs"), A("xm"), Alu.add)
-        ql = A("scn", s_(15, L, 16))
-        for e in range(3):
-            act(A("aq", s_(16 * e, 16 * e + 16)), ql, Act.Abs, C(NOFF))
-        tt(A("as%d" % t), A("aq"), bl, Alu.is_le)
+            if c == cfg["ZC"]:
+                zp = A(cfg["ZP"][0], s_(cfg["ZP"][1], cfg["ZP"][1] + L))
+                mm(grp(zp, [(HI, z), (HI, A("zr%d" % t))]))
+                if cfg["ZS"]:
+                    act(A("zh"), zp, idn, 1024.0, 1.0)
+                    act(A(Z, s_(L, 2 * L)), A("zh"), idn, -1024.0, 1.0)
+                else:
+                    ts(A(Z, s_(L, 2 * L)), zp, 1.5 * 2 ** 23, 1.5 * 2 ** 23, Alu.add, Alu.subtract)
+                ulist(Z, L)
+        for c, (a, b) in enumerate(CH):
+            n = b - a; ln = s_(a, b); up, Pt = at(c, "U"), at(c, "D", 1)
+            hi, lo = A(HL, s_(2 * a, 2 * a + n)), A(HL, s_(2 * a + n, 2 * b))
+            mm(grp(up, [(IB, hi), (NI, lo), (MF, A(bits, ln))]))
+            act(A("sq", ln), up, Act.Square, -2048.0, 4096.0)
+            mm(grp(Pt, [(ONE, A("cst", 1, ln)), (IB, A("sq", ln)), (IB, A(Pn, ln))]))
+            tt(A("Lt", ln), A("Gs", ln), Pt, Alu.max)
+        kl, KR, KD = LP(16, 32), A("p0", s_(128, 128 + L)), A("p1", s_(0, L))
+        mm([(KR, H64, A("vm"), True, False)])
+        mm([(KD, IB, A("DC"), True, False), (KD, H64, A("vm"), False, False), (A("p1", s_(0, L, 16)), N64, A("vm", s_(0, L, 16)), False, False)])
+        if cfg["LX"]:
+            FA = lambda e: A("p4", s_(L * e, L * e + L))
+            mm([(FA(0), IB, A("DG"), True, False), (FA(1), IB, A("DG"), False, False)])
+            mm([(FA(0), MF, A(bits), False, False), (FA(1), MA, A(bits), False, True)])
+            scan(A("sd", 0), A("SQ"), FA(0), Alu.add, Alu.max)
+            tt(A("kc"), A("sd", 0, s_(15, L, 16)), A("nb", s_(0, 16)), Alu.add)
+            scan(A("sd", 1), A("SQ"), FA(1), Alu.add, Alu.max)
+            act(A("kb"), A("kc"), idn, -5.5413, -40.0)
+            many([act(A("as%d" % t, s_(16 * e, 16 * e + 16)), A("sd", 1, s_(15, L, 16)), sig, 200.0, -12.5) for e in range(2)])
+            toint(A("ti", s_(0, 16)), LP(0, 16))
+            aff(A("ti", s_(16, 32)), A("kc"), 513.0, 1.0, cfg["TI"])
+        else:
+            mm(grp(kl, [(IB, A("nb", s_(0, 16)))] + [(sel(2, r), A(bits, s_(r, L, 16))) for r in range(16)]))
+            act(A("kb"), kl, idn, -5.5413, -40.0)
+            act(A("kc"), kl, idn)
+            toint(A("ti", s_(0, 16)), LP(0, 16))
+            aff(A("ti", s_(16, 32)), kl, 513.0, 1.0, cfg["TI"])
+            mm(grp(LP(96, 112), [(sel(3, r), A(bits, s_(r, L, 16))) for r in range(16)]))
+            many([act(A("as%d" % t, s_(16 * e, 16 * e + 16)), LP(96, 112), sig, 200.0, -400.0) for e in range(2)])
+        mm([(KR, MF32, A(bits), False, True)])
+        mm([(KD, MF32, A(bits), False, False), (A("p1", s_(0, L, 16)), NF32, A(bits, s_(0, L, 16)), False, False)])
+        mm([(A("p1", s_(r, L, 16)), NL, A("kc"), False, r == 15) for r in range(1, 16)])
+        for a, b in CH:
+            many([act(A("junk", h, s_(0, b - 16 * h - 16)), A("p0", s_(144 + 16 * h, 128 + b)), sig, A("kb", s_(h, h + 1)), 1280.0, A("ka", s_(h, h + 1)))
+                  for h in range(a // 16, b // 16 - 1)])
+        scan(A("sc"), KD, A("SP"), Alu.mult, Alu.add)
+        for e in (16, 0):
+            ts(A("tj", s_(16 + e, 32 + e)), A("ti", s_(e, 16 + e)), NV - 1, None, Alu.bitwise_and)
+        act(A("nb", s_(32, 48)), A("tj", s_(32, 48)), idn)
+        ts(A("fl", 0), A("sc", s_(15, L, 16)), 0.0, 2048.0, Alu.is_equal, Alu.mult)
+        tt(A("fl", 1), A("fl", 0), A("tj", s_(32, 48)), Alu.add)
+        aff(A("ki", 0), A("ka"), 2.0 ** 9, 2.0 ** 19, cfg["TI"])
+        ts(A("ki", 1), A("ki", 0), 255 << 11, None, Alu.bitwise_and)
+        tt(A("fl", 2), A("fl", 1), A("ki", 1), Alu.add)
+        if cfg["TU"]:
+            tt(A("woff"), A("fl", 2), A("lf"), Alu.min)
+        else:
+            tt(A("fl", 3), A("fl", 2), A("lf"), Alu.min)
+            cp(A("woff"), A("fl", 3))
         send((A("as%d" % t), A("ar%d" % t), HZ[t]))
+        if t == 0:
+            act(A("B", s_(0, NV)), A("bagi"), idn)
+        if not cfg["XV"]:
+            xp = A("p4", s_(0, L))
+            mm(grp(xp, [(IB, A("zm")), (IB, z)]))
+            act(A("xs"), xp, idn)
+        ts(A("xm"), A("xs"), 0.0, 256.0, Alu.is_lt, Alu.mult)
+        stage[0] = cfg["XB"]
+        for a in range(0, L, cfg["XP"]):
+            tt(ind(A("X"), A(of, s_(32 + a // 16, 32 + (a + cfg["XP"]) // 16))), A("xs", s_(a, a + cfg["XP"])), A("xm", s_(a, a + cfg["XP"])), Alu.add)
+        stage[0] = 0.0
         if last:
-            i = store("Y", A("X"), "yx", None, 5.0)
+            i = store("Y", A("X"), "yx", None, 3.5)
             ops[i]["after"] += [j for j, o_ in enumerate(ops) if o_["kind"] == "send"]
-        ts(A("ti", s_(64, 80)), A("ti", s_(32, 48)), 1.0, None, Alu.add)
-        wl = A("ti", s_(80, 96))
-        ts(wl, A("ti", s_(64, 80)), NV - 1, None, Alu.bitwise_and)
-        cp(A("base", s_(0, 16)), wl)
-        up, Pt, Gp = A("p0", s_(0, L)), A("p0", s_(L, 2 * L)), A("p1", s_(0, L))
-        for (a, b) in CH:
-            mm(grp(A("p0", s_(a, b)), [(IB, A(HL, s_(2 * a, a + b))), (NI, A(HL, s_(a + b, 2 * b))), (IB, A("sg", s_(a, b)))]))
-        act(A("sq"), up, Act.Square, 0.0, 4096.0)
-        mm(grp(Gp, [(mf(15), z), (mf(14), A(Pn))]))
-        act(A("Gs"), Gp, idn, 2048.0 - 2.0 ** 23, 1.0)
-        mm(grp(Pt, [(IB, A("cst", 2)), (IB, A("sq")), (IB, A("cst", 3)), (mf(14), A(Pn))]))
-        tt(A("Lt"), A("Gs"), Pt, Alu.max)
-        for (a, b) in cfg["NG"]:
-            sl = s_(a // 16, b // 16); o = lambda x: s_(x + a // 16, x + b // 16)
-            tt(A("N1", sl), A("N1", sl), A("N2", sl), Alu.is_gt)
-            tt(A("N1", sl), A("N1", sl), A("li", o(16)), Alu.mult)
-            tt(A("N1", sl), A("N1", sl), A("base", o(0)), Alu.max)
-            cp(A("woff", sl), A("N1", sl))
+        ts(A("tj", s_(0, 16)), A("ti", s_(0, 16)), 15, None, Alu.bitwise_and)
+        tt(A("dlt"), A("tj", s_(0, 32)), A("nb", s_(16, 48)), Alu.subtract)
+        for c, (a, b) in enumerate(CH):
+            n = b - a; hr = "hr%d" % t
+            Y = at(c, "D")
+            mm(grp(Y, [(IB, A("cst", 0, s_(a, b))), (IB, A("pr%d" % t, s_(a, b)))], stop=False))
+            mm(grp(Y, [(MI, A(hr, s_(2 * a, a + b))), (MI, A(hr, s_(a + b, 2 * b)))], start=False))
+            for pa in range(a, b, cfg["PO"]):
+                pb = min(b, pa + cfg["PO"]); ln = s_(pa, pb); H = at(c, "H", 0, pa - a, pb - a)
+                chain("po", tt(A("yi", ln), A("Lt", ln), at(c, "D", 0, pa - a, pb - a), Alu.max))
+                ts(A("Fi", ln), A("yi", ln), W - 1, None, Alu.bitwise_and)
+                if cfg["HF"][c]:
+                    tt(A("tF", ln), A("Fi", ln), at(c, "D", 2, pa - a, pb - a), Alu.mult)
+                    act(A("Fc", ln), A("Fi", ln), idn)
+                    mm(grp(H, [(A("SW"), A("tF", ln))]))
+                else:
+                    act(A("Fc", ln), A("Fi", ln), idn)
+                    act(at(c, "D", 1, pa - a, pb - a), A("Fi", ln), idn, -2048.0, 1.0)
+                    tt(A("tH", ln), A("mask2", ln), at(c, "D", 1, pa - a, pb - a), Alu.mult)
+                    mm(grp(H, [(bd(14), A("tH", ln))]))
+                tt(A("t2", ln), A("mask2", ln), H, Alu.mult)
+                tt(ind(A("B"), A("woff", s_(pa // 16, pb // 16))), A("Fc", ln), A("t2", ln), Alu.add)
+        ar = "ar%d" % t; nx = "offs%d" % (t + 1)
+        tt(A("prd"), A(ar), A("dlt"), Alu.mult)
+        items = grp(LP(32, 48), [(IB, A("prd", s_(16, 32))), (IB, A("nb", s_(32, 48)))])
         if not last:
-            ts(A("aoff"), A("as%d" % t, s_(0, 16)), 8.0, 256.0, Alu.mult, Alu.add)
-            act(A("A32"), ind(A("T4"), A("aoff")), Act.Copy)
-        zp = A("p1", s_(L, 2 * L))
-        mm(grp(zp, [(IB, A("cst", 1)), (HI, z), (HI, A("zr%d" % t))]))
-        ts(A(Z, s_(L, 2 * L)), zp, 1.5 * 2 ** 23, 1.5 * 2 ** 23, Alu.add, Alu.subtract)
-        ulist(Z, L)
-        ts(A("ti", s_(16, 32)), A("ti", s_(0, 16)), NV - 1, None, Alu.bitwise_and)
-        tt(A("dlt", s_(0, 16)), A("ti", s_(16, 32)), A("base", s_(0, 16)), Alu.subtract)
-        if not last:
-            ts(A("wi", s_(0, 16)), A("ti", s_(0, 16)), 15, None, Alu.bitwise_and)
-            tt(A("wi", s_(16, 32)), A("wi", s_(0, 16)), A("li", s_(32, 48)), Alu.add)
-            tt(A("dlt", s_(16, 32)), A("wi", s_(16, 32)), A("base", s_(16, 32)), Alu.subtract)
-        for c, (a, b) in enumerate(MS):
-            ln = s_(a, b); pb_ = "p%d" % (3 - c % 2); Y, H = A(pb_, s_(0, b - a)), A("p5", s_(L + a, L + b))
-            for (ca, cb) in CH:
-                if ca < a or cb > b: continue
-                Yc = A(pb_, s_(ca - a, cb - a)); hr = "hr%d" % t
-                mm(grp(Yc, [(IB, A("cst", 0, s_(ca, cb))), (mf(14), A("pr%d" % t, s_(ca, cb)))], stop=False))
-                mm(grp(Yc, [(MI, A(hr, s_(2 * ca, ca + cb))), (MI, A(hr, s_(ca + cb, 2 * cb)))], start=False))
-            chain("po", tt(A("yi", ln), A("Lt", ln), Y, Alu.max))
-            ts(A("Fi", ln), A("yi", ln), W - 1, None, Alu.bitwise_and)
-            ts(A("Fc", ln), A("Fi", ln), -2048.0, None, Alu.add)
-            if cfg["M2P"]:
-                tt(A("tF", ln), A("Fc", ln), A("p%d" % (2 + c % 2), s_(256, 256 + b - a)), Alu.mult)
-            else:
-                tt(A("tF", ln), A("Fc", ln), A("mask2", ln), Alu.mult)
-            mm(grp(H, [(mf(13), A("tF", ln))]))
-            tt(A("t2", ln), A("mask2", ln), H, Alu.mult)
-            for (sa, sb) in SC:
-                if a <= sa and sb <= b:
-                    chain("po", tt(ind(A("B"), A("woff", s_(sa // 16, sb // 16))), A("Fc", s_(sa, sb)), A("t2", s_(sa, sb)), Alu.add))
-        tt(A("prd"), A("ar%d" % t), A("dlt"), Alu.mult)
-        tt(A("res"), A("prd"), A("base"), Alu.add)
-        cp(A("offs"), A("res"))
-        act(A("ZZ%d" % (t + 1), s_(0, L)), ind(A(Z), A("offs", s_(32, 48))), Act.Copy)
-    store("Y", A("res", s_(0, 16)), "yv", None, 0.0)
+            items += grp(LP(48, 64), [(IB, A("prd", s_(0, 16))), (IB, A("nb", s_(16, 32)))])
+            items += grp(LP(64, 80), [(IB, A("prd", s_(0, 16))), (IB, A("nb", s_(16, 32))), (IB, li16)])
+        items += grp(LP(80, 96), [(I256, A(ar, s_(0, 16))), (IB, li)])
+        mm(items)
+        if last:
+            cp(A(nx, s_(48, 64)), LP(80, 96)); act(A("res"), LP(32, 48), idn)
+        else:
+            cp(A(nx), LP(32, 96)); act(A("nb", s_(16, 32)), LP(48, 64), idn)
+            toint(A("vi", 0), LP(32, 48))
+            ts(A("vi", 1), A("vi", 0), NV // 2 - 1, None, Alu.bitwise_and); act(A("nb", s_(0, 16)), A("vi", 1), idn, -512.0, 2.0)
+        act(A("ZZ%d" % (t + 1), s_(0, L)), ind(A(Z), A(nx, s_(48, 64))), Act.Copy)
+    store("Y", A("res"), "yv", None, 0.0)
     store("Y", A("ZZ3"), "yz", None, 0.3)
     h = NV // 4
     for e in range(2):
-        pp = A("p%d" % (6 + e), s_(0, h))
-        act(pp, A("B", s_(2 * h + e * h, 3 * h + e * h)), idn, 2048.0 * 4097, 4096.0)
+        pp = A("p%d" % (5 + e), s_(0, h))
+        act(pp, A("B", s_(2 * h + e * h, 3 * h + e * h)), idn, 0.0, 4096.0)
         tt(A("pk", s_(e * h, e * h + h)), A("B", s_(e * h, e * h + h)), pp, Alu.add)
         store("YS"[e], A("pk", s_(e * h, e * h + h)), "yb", (e * h, e * h + h), 0.5)
+    name = [o["eng"] + ":" + (o["wr"] or o["rd"])[0][0].rstrip("0123456789") + ":" + str((o["wr"] or o["rd"])[0][1][-1][0]) for o in ops]
+    for a, b in zip(begin, begin[1:] + [len(ops)]):
+        for x, y in cfg["DUE"]:
+            for i in range(a, b):
+                if name[i] == x: ops[i]["due"] += [j for j in range(a, b) if name[j] == y][:1]
     return ops
+
+
+COMP = ("many", "ts", "tt", "tts", "cp", "mset", "scan", "act", "mm", "iota")
 
 
 def overlap(a, b):
@@ -483,36 +543,38 @@ def overlap(a, b):
 
 
 def deps(ops):
-    n = len(ops); pred = [set(o["after"]) for o in ops]
+    n = len(ops); pred = [set(o["after"]) for o in ops]; free = set()
     hist = {}
     for i, o in enumerate(ops):
+        hard = set(o["after"])
         for b, r in o["rd"]:
             for j, rj, w in hist.get(b, ()):
-                if w and overlap(r, rj): pred[i].add(j)
+                if w and overlap(r, rj): pred[i].add(j); hard.add(j)
         for b, r in o["wr"]:
             for j, rj, w in hist.get(b, ()):
-                if overlap(r, rj): pred[i].add(j)
+                if overlap(r, rj):
+                    pred[i].add(j)
+                    if w: hard.add(j)
         for b, r in o["wr"]:
             hist[b] = [h for h in hist.get(b, []) if not all(x[0] <= y[0] and y[1] <= x[1] for x, y in zip(r, h[1]))] + [(i, r, True)]
         for b, r in o["rd"]:
             hist.setdefault(b, []).append((i, r, False))
         pred[i].discard(i)
+        for j in pred[i]:
+            if o["eng"] == ops[j]["eng"] and o["kind"] in COMP and ops[j]["kind"] in COMP and (o["eng"] == "P" or j not in hard): free.add((j, i))
     succ = [[] for _ in ops]
     for i in range(n):
         for j in pred[i] | set(ops[i]["soft"]): succ[j].append(i)
-    return pred, succ
-
-
-def tag(o):
-    b, r = (o["wr"] or o["rd"])[0]
-    return o["eng"] + (b if b[0] == "p" or b[0] == "N" else b.rstrip("0123")) + "_" + "_".join(str(x[0]) for x in r)
+    return pred, succ, free
 
 
 def costs(ops, fig):
-    return [o["cost"][0] + o["cost"][1] * fig[o["cost"][2]] for o in ops]
+    return [o["cost"][0] + o["cost"][1] * fig[o["cost"][2]]
+            + (fig["ov"] * (len(o["args"]) if o["kind"] in ("tts", "many") else 1) if o["eng"] in "VS" else 0.0) for o in ops]
 
 
-def place(ops, pred, succ, prio, fig, back=False):
+def place(ops, dp, prio, fig, back=False):
+    pred, succ, free = dp
     n = len(ops); c = costs(ops, fig); sy = fig["sync"]
     if back:
         pred, succ = succ, [p | set(o["soft"]) for p, o in zip(pred, ops)]
@@ -520,7 +582,7 @@ def place(ops, pred, succ, prio, fig, back=False):
     beg = [0.0] * n; fin = [0.0] * n; busy = {}; seq = []
     while ready:
         i = max(ready, key=lambda k: prio[k]); ready.remove(i); o = ops[i]; e = o["eng"]
-        t = max([fin[j] + (0.0 if e == "P" == ops[j]["eng"] else sy) for j in pred[i]] + [beg[j] + c[j] for j in o["soft"] if not back], default=0.0)
+        t = max([fin[j] + (0.0 if (j, i) in free or (i, j) in free else fig["own"] if ops[j]["eng"] == e else sy) for j in pred[i]] + [beg[j] + c[j] for j in o["soft"] if not back], default=0.0)
         if back: t += o["lat"]
         if e != "R":
             iv = [(a, b) for a, b, _ in busy.get(e, ()) if b > t]
@@ -547,32 +609,107 @@ def place(ops, pred, succ, prio, fig, back=False):
     return order, full, beg, fin
 
 
-def replay(ops, order, full, fig):
-    c = costs(ops, fig); sy = fig["sync"]; free = {}; fin = {}; beg = {}
+def replay(ops, order, full, free, fig):
+    c = costs(ops, fig); sy = fig["sync"]; busy = {}; fin = {}; beg = {}
     for i in order:
         e = ops[i]["eng"]
-        t = max([fin[j] + (0.0 if e == "P" == ops[j]["eng"] else sy) for j in full[i]], default=0.0)
+        t = max([fin[j] + (0.0 if (j, i) in free else fig["own"] if ops[j]["eng"] == e else sy) for j in full[i]], default=0.0)
         if e != "R":
-            t = max(t, free.get(e, 0.0)); free[e] = t + c[i]
+            t = max(t, busy.get(e, 0.0)); busy[e] = t + c[i]
         beg[i] = t; fin[i] = t + c[i] + ops[i]["lat"]
     return max(fin.values()), beg, fin
 
 
-def plan(ops, seed=None, dp=None, fig=FIG):
-    seed = CFG["SEED"] if seed is None else seed
-    pred, succ = dp or deps(ops)
-    n = len(ops); c = costs(ops, fig); prio = [0.0] * n
-    jit = np.random.RandomState(seed).uniform(1 - CFG["JIT"], 1 + CFG["JIT"], n)
-    for i in range(n - 1, -1, -1):
-        prio[i] = (c[i] + ops[i]["lat"] + fig["sync"]) * float(jit[i]) + max([prio[k] for k in succ[i]], default=0.0)
-    prio = [p + o["bias"] + BIAS.get(tag(o), 0.0) for p, o in zip(prio, ops)]
-    best = None
-    for _ in range(CFG["IT"]):
-        order, full, beg, fin = place(ops, pred, succ, prio, fig)
-        if best is None or max(fin) < max(best[3]): best = (order, full, beg, fin)
-        if CFG["IT"] > 1:
-            prio = place(ops, pred, succ, fin, fig, True)
-    return best
+def figs(fig):
+    def slow(f, gam, sca, hop):
+        return dict(fig, cy=f * fig["cy"], pcy=f * fig["pcy"], gam=f * gam * fig["gam"], sca=f * sca * fig["sca"], ov=f * fig["ov"],
+                    sync=(0.5 + 0.5 * f) * fig["sync"], own=(0.5 + 0.5 * f) * fig["own"], hop=hop * fig["hop"])
+    return [fig, slow(1.45, 1.25, 1.4, 1.2), slow(1.25, 0.72, 0.6, 1.4), slow(1.15, 1.25, 0.8, 0.8)]
+
+
+MID = dict(FIG, cy=1e-3, pcy=0.5e-3, gam=1.6e-3, sca=3.8e-3, sync=0.165, own=0.21, ov=0.021, hop=2.9)
+
+
+def plan(ops, cfg=CFG, fig=MID):
+    dp = deps(ops); succ = dp[1]
+    n = len(ops); c = costs(ops, fig); best = None
+    for seed in range(cfg["SEEDS"]):
+        prio = [0.0] * n
+        jit = np.random.RandomState(seed).uniform(1 - cfg["JIT"], 1 + cfg["JIT"], n)
+        for i in list(range(n - 1, -1, -1)) * 3:
+            prio[i] = (c[i] + ops[i]["lat"] + fig["sync"]) * (float(jit[i]) if seed else 1.0) + max([prio[k] for k in succ[i] + ops[i]["due"]], default=0.0)
+        prio = [p + o["bias"] for p, o in zip(prio, ops)]
+        for _ in range(cfg["IT"]):
+            order, full, beg, fin = place(ops, dp, prio, fig)
+            score = sum(replay(ops, order, full, dp[2], f)[0] / f["cy"] for f in figs(FIG))
+            if best is None or score < best[0]: best = (score, order, full, dp[2])
+            prio = place(ops, dp, fin, fig, True)
+            prio = [p + (o["bias"] if o["bias"] >= 50 else 0.0) for p, o in zip(prio, ops)]
+    return polish(ops, best[1], dp, cfg["MOVES"])
+
+
+def polish(ops, order, dp, moves, seed=0, heat=300.0):
+    pred, succ, free = dp
+    fs = figs(FIG); cs = [costs(ops, f) for f in fs]
+    eng = [o["eng"] for o in ops]; lat = [o["lat"] for o in ops]; banks = [tuple(o["banks"]) for o in ops]
+    must = [p | set(o["soft"]) for p, o in zip(pred, ops)]
+    lag = [[[(j, 0.0 if (j, i) in free else f["own"] if eng[j] == eng[i] else f["sync"]) for j in p] for i, p in enumerate(pred)] for f in fs]
+
+    def run(seq, k):
+        c = cs[k]; sy = fs[k]["sync"]; fin = [0.0] * len(ops); why = [None] * len(ops); busy = {}; last = {}
+        for i in seq:
+            e = eng[i]; t = 0.0; w = None
+            for j, d in lag[k][i]:
+                if fin[j] + d > t: t = fin[j] + d; w = (j, 0)
+            for b in banks[i]:
+                d = last.setdefault(b, {})
+                for f, j in d.items():
+                    if f != e and fin[j] + sy > t: t = fin[j] + sy; w = (j, 1)
+                d[e] = i
+            if e != "R":
+                if e in busy and busy[e][0] > t: t, w = busy[e][0], (busy[e][1], 1)
+                busy[e] = (t + c[i], i)
+            fin[i] = t + c[i] + lat[i]; why[i] = w
+        return fin, why
+
+    def score(seq):
+        r = [run(seq, k) for k in range(len(fs))]
+        return sum(max(x[0]) / f["cy"] for x, f in zip(r, fs)), r
+    rs = np.random.RandomState(seed); now, res = score(order); best = (now, order)
+    for it in range(moves):
+        fin, why = res[rs.randint(len(fs))]
+        i = fin.index(max(fin)); held = []
+        while why[i] is not None:
+            if why[i][1] and why[i][0] not in must[i]: held.append((why[i][0], i))
+            i = why[i][0]
+        if not held: break
+        j, i = held[rs.randint(len(held))]
+        a, b = order.index(j), order.index(i); kind = rs.randint(4); far = int(rs.exponential(40))
+        if kind == 2: a, b, i = max(0, a - 1 - far), a, j
+        if kind == 3: b = min(len(order) - 1, b + far)
+        mid = order[a:b + 1]
+        if kind % 2 == 0:
+            take = {i}
+            for x in mid[::-1]:
+                if any(y in take for y in succ[x]): take.add(x)
+            seq = order[:a] + [x for x in mid if x in take] + [x for x in mid if x not in take] + order[b + 1:]
+        else:
+            take = {j}
+            for x in mid:
+                if must[x] & take: take.add(x)
+            seq = order[:a] + [x for x in mid if x not in take] + [x for x in mid if x in take] + order[b + 1:]
+        if seq == order: continue
+        new, r = score(seq)
+        if new < now + heat * (1 - it / moves) * rs.exponential():
+            order, now, res = seq, new, r
+            if now < best[0]: best = (now, order)
+    order = best[1]; full = [set(p) for p in pred]; last = {}
+    for i in order:
+        for b in banks[i]:
+            d = last.setdefault(b, {})
+            full[i].update(j for f, j in d.items() if f != eng[i])
+            d[eng[i]] = i
+    return order, full, free
 
 
 PLAN = []
@@ -584,12 +721,11 @@ def rank_program(g, core, T, topo):
         return
     if not PLAN:
         o_ = build(); PLAN.append(o_); PLAN.append(plan(o_))
-    ops, (order, pred, _b, _f) = PLAN
+    ops, (order, pred, free) = PLAN
     Q = {"V": g.vector, "S": g.scalar, "P": g.tensor, "G": g, "Y": g.sync}
     cores = T.cores
     eng = [e for e in topo.engines(cores[0], cores[1]) if all(e in topo.engines(a, b) for a in cores for b in cores if a != b)]
     mask = sum(1 << e for e in eng)
-    comp = ("ts", "tt", "tts", "cp", "mset", "scan", "act", "acts", "mm", "iota")
     pos = {}; cnt = {}
     for i in order:
         e = ops[i]["eng"]; cnt[e] = cnt.get(e, 0) + 1; pos[i] = cnt[e]
@@ -600,8 +736,8 @@ def rank_program(g, core, T, topo):
         best = {}
         for j in pred[i]:
             oj = ops[j]
-            if oj["kind"] in comp:
-                if e == "P" and oj["eng"] == "P": continue
+            if oj["kind"] in COMP:
+                if (j, i) in free: continue
                 if pos[j] > seen.get((e, oj["eng"]), 0) and pos[j] > pos.get(best.get(oj["eng"]), 0): best[oj["eng"]] = j
             elif oj["kind"] != "send" and (e, j) not in seen:
                 seen[(e, j)] = 1; w.append(j)
@@ -611,7 +747,7 @@ def rank_program(g, core, T, topo):
     semof = {}; num = {}; nd = 0; nr = 0
     for i in order:
         o = ops[i]
-        if o["kind"] in comp:
+        if o["kind"] in COMP:
             if i in need:
                 num[o["eng"]] = num.get(o["eng"], 0) + 1; semof[i] = (T.sem["e" + o["eng"]], num[o["eng"]])
         elif o["kind"] in ("load", "store"):
@@ -627,6 +763,19 @@ def rank_program(g, core, T, topo):
     def hbm(name, idx):
         return T[name][:] if idx is None else T[name][:, idx[0]:idx[1]]
 
+    def call(q, k, a):
+        if k == "ts":
+            return q.tensor_scalar(R(a[0]), R(a[1]), R(a[2]), R(a[3]), *[x for x in a[4:6] if x is not None])
+        if k == "tt": return q.tensor_tensor(R(a[0]), R(a[1]), R(a[2]), a[3])
+        if k == "tts": return [q.tensor_tensor(R(m[0]), R(m[1]), R(m[2]), m[3]) for m in a][-1]
+        if k == "cp": return q.tensor_copy(R(a[0]), R(a[1]))
+        if k == "mset": return q.memset(R(a[0]), a[1])
+        if k == "scan": return q.tensor_tensor_scan(R(a[0]), R(a[1]), R(a[2]), 0.0, a[3], a[4])
+        if k == "act": return q.activation(R(a[0]), R(a[1]), a[2], bias=R(a[3]), scale=R(a[4]), accum_out=R(a[5]))
+        if k == "mm": return [q.matmul(R(m[0]), R(m[1]), R(m[2]), m[3], m[4]) for m in a][-1]
+        if SCRATCH[a[0][0]][2] == I32: return q.iota(R(a[0]), a[1], a[2], a[3])
+        return q.iota(R(a[0]), a[1], a[2], a[3], allow_small_or_imprecise_dtypes=True)
+
     sent = 0
     for i in order:
         o = ops[i]; k = o["kind"]; a = o["args"]
@@ -634,23 +783,9 @@ def rank_program(g, core, T, topo):
         q = Q[o["eng"]]
         for j in waits[i]:
             q.wait_ge(*semof[j])
-        if k == "ts":
-            ins = q.tensor_scalar(R(a[0]), R(a[1]), R(a[2]), R(a[3]), a[4]) if a[5] is None else q.tensor_scalar(R(a[0]), R(a[1]), R(a[2]), R(a[3]), a[4], a[5])
-        elif k == "tt": ins = q.tensor_tensor(R(a[0]), R(a[1]), R(a[2]), a[3])
-        elif k == "tts":
-            for m in a: ins = q.tensor_tensor(R(m[0]), R(m[1]), R(m[2]), m[3])
-        elif k == "cp": ins = q.tensor_copy(R(a[0]), R(a[1]))
-        elif k == "mset": ins = q.memset(R(a[0]), a[1])
-        elif k == "scan": ins = q.tensor_tensor_scan(R(a[0]), R(a[1]), R(a[2]), 0.0, Alu.add, Alu.max)
-        elif k == "act":
-            ins = q.activation(R(a[0]), R(a[1]), a[2], bias=R(a[3]), scale=R(a[4]), accum_out=R(a[5]))
-        elif k == "acts":
-            for m in a: ins = q.activation(R(m[0]), R(m[1]), m[2], bias=R(m[3]), scale=m[4], accum_out=R(m[5]))
-        elif k == "mm":
-            for m in a: ins = q.matmul(R(m[0]), R(m[1]), R(m[2]), m[3], m[4])
-        elif k == "iota":
-            if SCRATCH[a[0][0]][2] == I32: ins = q.iota(R(a[0]), a[1], a[2], a[3])
-            else: ins = q.iota(R(a[0]), a[1], a[2], a[3], allow_small_or_imprecise_dtypes=True)
+        if k == "many":
+            for m in a: ins = call(q, m["kind"], m["args"])
+        elif k in COMP: ins = call(q, k, a)
         elif k == "load":
             q.dma_start(R(a[0]), hbm(a[1], a[2])).then_inc(semof[i][0], 16); continue
         elif k == "store":

@@ -28,36 +28,48 @@ for _n, _s, _d in [
     ("pf", [16, NF], F16), ("BD", [128, NF], F16), ("M", [22, 128], F16), ("MB", [2, 128], BF), ("T4", [NV], BF), ("vm", [L], BF), ("junk", [16, 128], BF), ("SW", [128], F32),
     ("gm", [8], F32), ("mw", [144], F16), ("km1", [16], F32), ("dg", [16], F32), ("dgs", [16], F32), ("r0", [16], F32), ("wi", [32], I32),
     ("thr", [16], F32), ("gmb", [16], BF), ("DTs", [L], F16), ("tH", [L], F16), ("sx", [L], BF), ("DC", [L], BF), ("SP", [L], BF), ("sc", [L], F32),
-    ("SQ", [L], BF), ("DG", [L], BF), ("sd", [2, L], BF), ("zh", [L], F16),
+    ("SQ", [L], BF), ("sd", [2, L], F32), ("zh", [L], F16),
     ("cst", [2, L], BF), ("btb", [4], BF), ("btc", [20], F32), ("uf", [4], F32), ("tf", [32], F32),
-    ("ti", [32], I32), ("tj", [48], I32), ("nb", [48], F16), ("dlt", [32], F16), ("prd", [32], F16),
-    ("kb", [16], F32), ("kc", [16], F16), ("ka", [16], F32), ("ki", [2, 16], I32), ("vi", [2, 16], I32), ("fl", [4, 16], F32), ("lf", [16], F32), ("woff", [16], U16), ("res", [16], F32),
+    ("ti", [2, 16], I32), ("bs", [6, 16], I32), ("dlt", [3, 16], F32), ("prd", [3, 16], F32), ("Gc", [L], F16),
+    ("kb", [16], F32), ("kc", [16], F16), ("ka", [16], F32), ("ki", [2, 16], I32), ("vi", [16], I32), ("fl", [4, 16], F32), ("lf", [16], F32), ("woff", [16], U16), ("res", [16], F32),
 ]:
     _sb(_n, _s, _d)
 for _t in range(RO):
     _sb("Pc%d" % _t, [L], F16); _sb("pr%d" % _t, [L], F16); _sb("zr%d" % _t, [L], BF)
-    _sb("hl%d" % _t, [2 * L], BF); _sb("hr%d" % _t, [2 * L], BF); _sb("bits%d" % _t, [L], BF)
-    _sb("as%d" % _t, [32], BF); _sb("ar%d" % _t, [32], BF)
+    _sb("hl%d" % _t, [2 * L], BF); _sb("hr%d" % _t, [L], BF); _sb("bits%d" % _t, [L], BF)
+    _sb("as%d" % _t, [3, 16], BF); _sb("ar%d" % _t, [3, 16], BF)
 for _t in range(RO + 1):
-    _sb("offs%d" % _t, [64], U16)
+    _sb("offs%d" % _t, [3, 16], U16)
 for _b in range(8):
     SCRATCH["p%d" % _b] = ("psum", [128, 512], F32)
 
 SEMAPHORES = ["eV", "eS", "eP", "eG", "sent"] + ["d%d" % i for i in range(24)] + ["r%d" % i for i in range(24)]
 
-FIG = {"cy": 0.83e-3, "gam": 1.3e-3, "sca": 3.15e-3, "pcy": 0.42e-3, "iss": 0.5, "hop": 2.7, "sync": 0.15, "own": 0.19, "ov": 0.018}
+FIG = {"cy": 0.83e-3, "gam": 1.3e-3, "sca": 3.15e-3, "pcy": 0.42e-3, "iss": 0.5, "hop": 3.2, "sync": 0.14, "own": 0.18, "ov": 0.016}
 CFG = {"CH": [(0, 128), (128, 256)],
-       "PS": [64],
+       "PS": [("V", 0, 64), ("S", 64, 128), ("V", 128, 256)],
        "GA": [("V", 0, 64), ("S", 64, 128), ("S", 128, 192), ("S", 192, 256)],
        "UN": [(0, 128, 0), (128, 192, 0), (192, 256, 0)],
-       "PL": [{"D": ("p2", 0), "A": ("p4", 0), "B": ("p5", 0), "E": ("p6", 0), "U": ("p2", 384), "H": ("p0", 384)},
-              {"D": ("p3", 0), "A": ("p0", 0), "B": ("p1", 0), "E": ("p7", 0), "U": ("p3", 384), "H": ("p1", 384)}],
-       "DUE": [("V:xs:0", "V:mx:0"), ("V:X:0", "V:cs:512"), ("V:ZZ:256", "V:cl:128"), ("S:vm:0", "S:Dc:128"), ("V:tj:16", "V:sc:0"),
-               ("V:Lt:128", "V:sc:0"), ("V:Lt:0", "V:sd:0"), ("V:woff:0", "V:yi:128"), ("V:t:0", "V:yi:128"), ("S:B:0", "S:ka:0"),
-               ("V:dlt:0", "V:yi:128")],
-       "AB": "p7", "ZC": 0, "ZP": ("p4", 0),
-       "DT": ["S", 0], "RW": 9, "NS": ["SS", "SV"], "HF": [0, 1], "RB": [0.0, 0.0], "UB": 0.0, "XV": 1, "LX": 1, "ZS": 0,
-       "NA": 8, "KL": 2, "XP": 128, "XB": 0.0, "PO": 128, "DC": "SS", "TI": "S", "TU": 1, "SW": 0.5, "IT": 2, "MOVES": 8000, "SEEDS": 3, "JIT": 0.1}
+       "PL": [{"D": ("p2", 0), "A": ("p4", 0), "B": ("p5", 0), "E": ("p6", 0), "U": ("p2", 384), "H": ("p0", 384), "X": ("p4", 256)},
+              {"D": ("p3", 0), "A": ("p0", 0), "B": ("p1", 0), "E": ("p7", 0), "U": ("p3", 384), "H": ("p1", 384), "X": ("p1", 256)}],
+       "DUE": [("V:xs:0", "V:mx:0"), ("V:X:0", "V:cs:0"), ("V:ZZ:256", "V:cl:128"), ("S:vm:0", "S:Dc:128"), ("V:tj:0", "V:sc:0"),
+               ("V:Lt:0", "V:sd:0"), ("V:woff:0", "V:tF:128"), ("V:t:0", "V:tF:128"), ("S:B:0", "S:ka:0"), ("V:dlt:0", "V:tF:128"),
+               ("S:Gc:128", "V:cl:128")],
+       "DL": [1, 1], "BE": "S", "ROUNDS": 5, "AM": 1,
+       "ORDER": {
+           "V": "Poff:0 Poff:128 xg:0 Pc:0 mx:10 mx:90 mx:1128 mx:9128 mx:1192 mx:9192 xs:0 Fi:0 xm:0 Fi:128 X:0' cl:0 cs:10 X:0 cl:128 sq:0 p2:0 bs:50 "
+                "sd:10 sd:00 p2:128' p2:384 Lt:0 ZZ:256 tH:0 sq:128 sc:0 p3:128' p3:0 fl:00 Lt:128 tF:0 p2:128 p3:384 bs:40 bs:00 tH:128 ki:10 fl:10 "
+                "Fc:0 dlt:00 fl:20 t:0 woff:0 tF:128 p3:128 B:0' Fc:128 prd:00 t:128 offs:00 B:0 res:0",
+           "S": "Poff:64 xg:1024 xg:2048 xg:3072 DTs:0 zm:0 bs:20 Dc:0 yi:128 yi:0 cs:00 cs:0512 Dc:128 Gc:0 cs:1384 p2:256 hl:0 bits:0 vm:0 Gc:128 mask:128 "
+                "bits:128 hl:256 mask:0 as:00 kb:0 kc:0 p3:256 ka:0 ka:8 ti:00 ti:10 ki:00 ZZ:0",
+           "P": "p0:0<xg0 p2:0<gmb8 p2:8<gmb8 p6:384<Pc0 p6:0<bits0 p7:384<Pc128 p7:0<bits128 p2:1<gmb0 p1:0<xg2048 p3:0<xg2055 p3:0<xg2063 p2:9<gmb0 "
+                "p0:0<xg3072 p3:64<xg3079 p4:0<M00 p3:0<mx8128 p3:0<mx0128 p4:0<Dc0 p5:0<Dc0 p3:64<mx8192 p3:64<xg3087 p3:64<mx0192 p2:128<cs0384 "
+                "p2:128<cs0768 p0:0<Dc128 p1:0<Dc128 p6:0<Dc0 p6:0<cl0 p4:256<Pc0 p3:128<cs1256 p3:128<cs1768 p2:384<bits0 p7:0<Dc128 p7:0<cl128 p0:128<vm0 "
+                "p5:0<zr0 p4:0<bits0 p0:128<bits0 p3:384<bits128 p1:256<Pc128 p1:0<vm0 p1:0<bits0 p1:1<kc0 p5:384<ZZ271 p0:384<tH0 p1:384<tH128",
+           "G": "ZZ:0 Pc:0 hl:0 hl:256 as:00"},
+       "AB": "p7", "ZC": 0, "ZP": ("p5", 0), "ZL": 1,
+       "DT": ["S", 0], "RW": 9, "NS": [[("p4", 4, "S"), ("p5", 3, "S")], [("p1", 3, "V"), ("p0", 4, "S")]], "RT": [0, 0], "HF": [1, 1], "RB": [0.0, 0.0], "UB": 0.0, "XV": 1, "LX": 1, "ZS": 0,
+       "NA": 8, "KL": 2, "XP": 128, "XB": 0.0, "PO": 128, "DC": "SS", "TI": "S", "TU": 1, "SW": 0.5, "IT": 2, "MOVES": 5000, "SEEDS": 3, "JIT": 0.1}
 
 
 class Ap(tuple):
@@ -103,7 +115,7 @@ def build(cfg=CFG):
             else:
                 wr.append(a)
         banks = set(b for b, _ in rd + wr if b in SCRATCH and SCRATCH[b][0] == "psum")
-        ops.append({"eng": eng, "kind": kind, "args": args, "rd": rd, "wr": wr, "cost": cost, "lat": lat, "banks": banks, "after": [], "soft": [], "due": [], "bias": stage[0]})
+        ops.append({"eng": eng, "kind": kind, "args": args, "rd": rd, "wr": wr, "cost": cost, "lat": lat, "banks": banks, "after": [], "soft": [], "due": [], "role": None, "bias": stage[0]})
         return len(ops) - 1
 
     def chain(key, i):
@@ -179,7 +191,7 @@ def build(cfg=CFG):
         return add(q, "store", (buf, name, idx), [buf], [], (0.06, 0, "cy"), 1.6 + us)
 
     def send(*trs):
-        i = add("G", "send", trs, [x[0] for x in trs], [], (0.0, 1, "iss"))
+        i = add("G", "send", trs, [y for x in trs for y in ([x[0]] if isinstance(x[0], Ap) else x[0])], [], (0.0, 1, "iss"))
         j = add("R", "recv", trs, [], [x[1] for x in trs], (0.0, 1, "hop"))
         ops[j]["after"].append(i)
         return i
@@ -194,9 +206,9 @@ def build(cfg=CFG):
 
     chain("ly", load("Y", A("bagi"), "bag", None, 1.5))
     chain("ls", load("S", A("v0i"), "v0", None, 0.0))
-    chain("ls", load("S", A("ZZ0", s_(0, L)), "z0", None, 0.5))
     chain("ls", load("S", A("uwi", s_(0, 1)), "uw", None, 0.5))
-    chain("ly", load("Y", A("X"), "xt", None, 3.5))
+    chain("ly", load("Y", A("X"), "xt", None, 3.4))
+    chain("ly", load("Y", A("ZZ0", s_(0, L)), "z0", None, 3.6))
     mset(A("bti"), 0)
     chain("ly", load("Y", A("bti", s_(0, 3), part=s_(0, 128, 16)), "bt", None, 3.5))
 
@@ -228,29 +240,31 @@ def build(cfg=CFG):
     act(C(S0), J0c, idn, 0.0, 1.0 / 32); act(C(S1), J0c, idn, 0.0, -1.0 / 32); act(C(J16), C(J), idn, 0.0, 16.0)
     tt(C(J12), dgc(1), dgc(2), Alu.add)
     act(C(A32), C(J12), idn, 0.0, 32.0)
-    act(A("tf", s_(0, 1)), J0c, idn, 0.0, -9.0 * 2 ** 22)
-    ts(C(PC), dgc(1), 10240.0, A("tf", s_(0, 1)), Alu.mult, Alu.add)
     act(A("tf", s_(1, 2)), J0c, idn, 400 * 12288.0, 200.0)
     ts(C(QB), dgc(2), -800 * 12288.0, A("tf", s_(1, 2)), Alu.mult, Alu.add)
     ts(A("gm"), A("ik", s_(0, 8)), C(GC), None, Alu.is_equal)
     ts(A("km1"), ik, 1.0, None, Alu.min)
     ts(A("li", s_(0, 16)), ik, 16.0, C(J), Alu.mult, Alu.add)
     ts(A("li", s_(16, 32)), ik, 256.0, C(J16), Alu.mult, Alu.add)
-    mset(A("li", s_(32, 48)), 1.0)
     act(A("lf"), A("li", s_(0, 16)), idn, 1024.0, 1.0)
     mset(A("ka"), 0.0)
     mset(A("cst", 0), 2048.0)
-    ts(A("cst", 1), A("cst", 0), 0.0, C(PC), Alu.mult, Alu.add)
+    mset(A("cst", 1), 10240.0)
+    apart = any(u[2] for u in cfg["UN"])
     for m, v in enumerate([2.0, -1.0, J0c, C(J12), 1.0]):
-        ts(A("ms", m), A("ix"), C(MC), v, Alu.is_equal, Alu.mult)
+        if m < 2 or (m == 4 and apart): ts(A("ms", m), A("ix"), C(MC), v, Alu.is_equal, Alu.mult)
     IB, NI, HI, TWO, I256, NL, DJ, NDJ, ONE, NONE, EC1, EC2, MA, MF, QD, QC, QA, H64, N64, MF32, NF32 = [M(m) for m in range(21)]
     MI = A("MB", 0)
-    for m, v in [(IB, 1.0), (NI, -1.0), (DJ, C(JG)), (NDJ, C(NJG)), (HI, 511.0 / 1024), (TWO, 2.0), (I256, 256.0), (NL, -1.0 / 32), (H64, 1.0 / 64), (N64, -1.0 / 64), (MI, -2.0 ** 25)]:
+    for m, v in [(IB, 1.0), (DJ, C(JG)), (NDJ, C(NJG)), (HI, 511.0 / 1024), (H64, 1.0 / 64)]:
         ts(m, A("ix", s_(0, 128)), C(PP), v, Alu.is_equal, Alu.mult)
+    for m, v in [(NI, -1.0), (N64, -1.0 / 64), (MI, -2.0 ** 25)]:
+        act(m, IB, idn, 0.0, v)
     ts(ONE, A("gx"), C(GC), None, Alu.is_equal)
     ts(NONE, A("gx"), C(GC), -1.0, Alu.is_equal, Alu.mult)
-    for m, v in [(EC1, C(NJG)), (EC2, C(JG)), (MA, C(A32)), (MF, J0c), (MF32, C(S0)), (NF32, C(S1))]:
+    for m, v in [(EC1, C(NJG)), (EC2, C(JG)), (MA, C(A32)), (MF32, C(S0)), (NF32, C(S1))]:
         act(m, ONE, idn, 0.0, v)
+    MF2 = TWO
+    act(MF2, MF32, idn, 0.0, -64.0)
     cp(A("uf", s_(0, 1)), A("uwi", s_(0, 1)))
     act(A("tf", s_(16, 32)), ik, idn, 1.0, 2.0)
     ts(A("wi", s_(0, 16)), A("tf", s_(16, 32)), A("uf", s_(0, 1)), 2048.0, Alu.mult, Alu.add)
@@ -284,10 +298,11 @@ def build(cfg=CFG):
     act(A("gmb", s_(0, 8)), A("gm"), idn, 0.0, 2.0); act(A("gmb", s_(8, 16)), A("gm"), idn, 0.0, -1.0)
     ts(A("SP"), A("sx"), 0.0, None, Alu.is_equal)
     ts(A("DC"), A("sx"), C(J), 64.0, Alu.is_le, Alu.mult)
+    ts(A("SQ"), A("DC"), -16.5, 32.0, Alu.mult, Alu.add)
     mset(A("DC", s_(0, L, 16)), 0.0)
-    if cfg["LX"]:
-        ts(A("SQ"), A("sx"), 0.0, -1024.0, Alu.is_equal, Alu.mult)
-        ts(A("DG"), A("sx"), C(J), -256.0, Alu.not_equal, Alu.mult)
+    OK, OC, OW, OA = 28, 29, 30, 31
+    for c, b, s in [(OK, 1280 * 480 - 5.5413, -1280 * 32.0), (OC, -480.0, 32.0), (OW, 513 - 32 * 480.0, 1024.0), (OA, 200 + 12.5 * 480, -400.0)]:
+        act(C(c), C(J), idn, b, s)
     cp(A("btb"), A("bti"))
     mm(grp(A("p5", s_(496, 500)), [(NONE, A("btb"))]))
     ts(A("tf", s_(4, 8)), A("km1", s_(0, 4)), -32.0, -0.5, Alu.mult, Alu.add)
@@ -305,32 +320,33 @@ def build(cfg=CFG):
     def toint(out, in0):
         return act(out, in0, idn) if cfg["TI"] == "S" else cp(out, in0)
 
-    cp(A("offs0", s_(0, 16)), A("v0i"))
-    ts(A("vi", 1), A("v0i"), NV // 2 - 1, None, Alu.bitwise_and); act(A("nb", s_(0, 16)), A("vi", 1), idn, -512.0, 2.0)
+    cp(A("offs0", 0), A("v0i"))
     ulist("ZZ0", 0)
-    toint(A("ti", s_(0, 16)), LP(0, 16))
-    ts(A("tj", s_(0, 16)), A("ti", s_(0, 16)), 15, None, Alu.bitwise_and)
-    act(A("nb", s_(16, 32)), A("tj", s_(0, 16)), idn)
-    mm(grp(LP(64, 80), [(IB, A("nb", s_(16, 32))), (IB, li16)]))
-    cp(A("offs0", s_(32, 48)), LP(64, 80))
+    toint(A("ti", 0), LP(0, 16))
+    ts(A("bs", 4), A("ti", 0), 15, None, Alu.bitwise_and)
+    tt(A("offs0", 1), A("bs", 4), li16, Alu.add)
+    act(A("bs", 3), li, idn)
+    mset(A("dlt", 2), 256.0)
 
     begin = []
     for t in range(RO):
         begin.append(len(ops))
         Z = "ZZ%d" % t; z = A(Z, s_(0, L)); last = t == RO - 1
-        of = "offs%d" % t; coff = A(of, s_(32, 48)); bits = "bits%d" % t
-        cut = [0] + (cfg["PS"] if t else []) + [L]
-        for a, b in zip(cut, cut[1:]):
-            vo = A(of, s_(a // 16, b // 16))
-            chain("vg", cp(A("Poff", s_(a, b)), ind(A("B", s_(0, NV)) if t else A("bagi"), vo)))
+        of = "offs%d" % t; coff = A(of, 1); bits = "bits%d" % t
+        for e, a, b in (cfg["PS"] if t else [("V", 0, L)]):
+            src = ind(A("B", s_(0, NV)) if t else A("bagi"), A(of, 0, s_(a // 16, b // 16)))
+            if e == "V": chain("vg", ts(A("Poff", s_(a, b)), src, 2048.0 if t else 0.0, None, Alu.add))
+            else: chain("sg", act(A("Poff", s_(a, b)), src, idn, 2048.0, 1.0))
+        aff(A("bs", 2), A(of, 1), 0.0, 1.0, cfg["BE"])
+        ts(A("bs", 5), A("bs", 2), 15, None, Alu.bitwise_and)
         Pn = "Pc%d" % t; HL = "hl%d" % t
         ts(A(Pn), A("Poff"), -2048.0, None, Alu.add)
-        if t == 0:
-            i = send((z, A("zr%d" % t), HZ[t])); ops[i]["bias"] = 50.0
+        if t == 0 or cfg["ZC"] < 0:
+            i = send((z, A("zr%d" % t), HZ[t]))
             send((A(Pn), A("pr%d" % t), HN[t]))
         else:
             send((z, A("zr%d" % t), HZ[t]), (A(Pn), A("pr%d" % t), HN[t]))
-        act(A("vm"), ind(A("T4"), A(of, s_(0, 16))), Act.Copy)
+        act(A("vm"), ind(A("T4"), A(of, 0)), Act.Copy)
         if cfg["XV"]:
             act(A("zm"), z, idn, -256.0, 1.0)
             tt(A("xs"), ind(A("X"), coff), A("zm"), Alu.add)
@@ -347,6 +363,17 @@ def build(cfg=CFG):
         def at(c, key, i=0, p=0, q=None):
             bank, off = cfg["PL"][c][key]; n = CH[c][1] - CH[c][0]
             return A(bank, s_(off + i * n + p, off + i * n + (n if q is None else q)))
+
+        def average():
+            zp = A(cfg["ZP"][0], s_(cfg["ZP"][1], cfg["ZP"][1] + L))
+            mm(grp(zp, [(HI, z), (HI, A("zr%d" % t))]))
+            if cfg["ZS"]:
+                act(A("zh"), zp, idn, 1024.0, 1.0)
+                act(A(Z, s_(L, 2 * L)), A("zh"), idn, -1024.0, 1.0)
+            else:
+                ts(A(Z, s_(L, 2 * L)), zp, 1.5 * 2 ** 23, 1.5 * 2 ** 23, Alu.add, Alu.subtract)
+            ulist(Z, L)
+        if cfg["ZC"] < 0: average()
         for c, (a, b) in enumerate(CH):
             n = b - a; ln = s_(a, b); pd = cfg["PL"][c]["D"][0]
             for iu, (u0, u1, ns) in enumerate(cfg["UN"]):
@@ -359,8 +386,15 @@ def build(cfg=CFG):
                     pe = cfg["AB"]
                     mm([m for i in range(ns) for m in grp(A(pe, s_(i * un, i * un + un)), [(IB, xk(u0, u1, 16 - ns + i)), (NI, xk(u0, u1, 0))])])
                     act(A("ab", iu % 4, s_(0, ns * un)), A(pe, s_(0, ns * un)), Act.Abs)
-                dt = cfg["DT"][c]
-                if not dt:
+                dt = cfg["DT"][c]; rt = cfg["RT"][c]
+                if rt:
+                    if u0 == a:
+                        own = [(A(rt, s_(k, 128, 16)), xk(a, b, k) if k else A(Z, ln), A("gmb", s_(8, 16)), k == 0, k == 15) for k in range(16)]
+                        for i in (0, 8): mm(own[i:i + 8], [A(rt, s_(0, 128))])
+                        aff(A("DTs", ln), A(rt, s_(0, 128)), 2048.0, 1.0, "S")
+                    mm(grp(D, [(NONE, xk(u0, u1, 0))], u0 == a, False), [at(c, "D")])
+                    if u0 == a: mm([(at(c, "D"), A("DTs", ln), IB, False, False)])
+                elif not dt:
                     raw = grp(D, [(NX if ns else NONE, xk(u0, u1, 0)), (sel(1, 0), A(Z, lu))] + [(sel(1, k), xk(u0, u1, k)) for k in kv[:-1]], u0 == a, False)
                     for i in range(0, len(raw), cfg["RW"]): mm(raw[i:i + cfg["RW"]], [at(c, "D")])
                 for i in range(0, len(kv), step):
@@ -381,84 +415,79 @@ def build(cfg=CFG):
                     mm([(DT(k), A("mx", k, ln), A("gmb", s_(0, 8)), False, k == 0) for k in kv[i:i + step]], [A(pd, s_(0, 128))])
                 DTs = A("DTs", s_(128 * (c % 2), 128 * (c % 2) + 128), part=pn)
                 aff(DTs, A(pd, s_(0, 128), part=pn), -2048.0, 1.0, dt)
-                mm(grp(A(pd, s_(384, 384 + n)), [(DTs, A("M", 0, s_(0, n), part=pn))]))
-                aff(Dc, A(pd, s_(384, 384 + n)), 0.0, 1.0, cfg["DC"][c])
+                mm(grp(at(c, "A"), [(DTs, A("M", 0, s_(0, n), part=pn))]))
+                aff(Dc, at(c, "A"), 0.0, 1.0, cfg["DC"][c])
             else:
-                aff(Dc, at(c, "D"), -2048.0, 1.0, cfg["DC"][c])
-            dif = lambda s: at(c, "A", s) if s < 4 else at(c, "B", s - 4)
-            for so in (range(4), range(4, 7)):
+                aff(Dc, at(c, "D"), -4096.0 if rt else -2048.0, 1.0, cfg["DC"][c])
+            parts = []; s0 = 0
+            for bank, cnt, e in cfg["NS"][c]:
+                so = range(s0, s0 + cnt); s0 += cnt; parts.append(so)
+                dif = lambda s: A(bank, s_((s - so[0]) * n, (s - so[0] + 1) * n))
                 mm([(dif(s), bd(s), Dc, True, True) for s in so])
-            for so, e in zip((range(4), range(4, 7)), cfg["NS"][c]):
                 if e == "S": many([act(cs(s), dif(s), sig, A("thr", s_(8 + s, 9 + s)), 400.0) for s in so])
                 else: many([ts(cs(s), dif(s), A("thr", s_(s, s + 1)), None, Alu.is_gt) for s in so])
-            so = [range(4), range(4, 7)] if cfg["NS"][c] == "SS" else [range(4, 7), range(4)]
-            mm(grp(tp, [(DJ, Dc)] + [(bd(7 + s), cs(s)) for s in so[0]], stop=False))
-            mm(grp(tp, [(bd(7 + s), cs(s)) for s in so[1]], start=False))
+            for i, so in enumerate(parts):
+                mm(grp(tp, [(DJ, Dc)] * (i == 0) + [(bd(7 + s), cs(s)) for s in so], i == 0, i == len(parts) - 1))
             ts(cl, tp, -2048.0, 2048.0, Alu.max, Alu.min)
             act(A("mask2", ln), tp, sig, -16 * (9.5 * BIG - 8), 16.0)
-            if cfg["HF"][c]: act(at(c, "D", 2), tp, sig, -16 * (9.5 * BIG - 8), 16.0)
+            act(at(c, "D", 2), tp, sig, -16 * (9.5 * BIG - 8), 16.0)
             prev = A("bits%d" % (t - 1), ln) if t else None
             E1, E2, Q, Gp = [at(c, "E", e) for e in range(4)]
             hi, lo = A(HL, s_(2 * a, 2 * a + n)), A(HL, s_(2 * a + n, 2 * b))
             mm(grp(Gp, [(MW, A(Z, ln)), (IB, A(Pn, ln))]))
-            act(A("Gs", ln), Gp, idn, 2048.0 - 2.0 ** 23, 1.0)
+            if cfg["DL"][c]:
+                act(A("yi", ln), Gp, idn, 2048.0, 1.0)
+                ts(A("Fi", ln), A("yi", ln), W - 1, None, Alu.bitwise_and)
+                act(A("Gc", ln), A("Fi", ln), idn, -2048.0, 1.0)
+            else:
+                act(A("Gs", ln), Gp, idn, 2048.0 - 2.0 ** 23, 1.0)
             if t: mm([(E1, MA, prev, True, False), (E2, MA, prev, False, False), (Q, QA, prev, False, False)])
             mm([(E1, DJ, Dc, not t, False), (E2, NDJ, Dc, False, False), (Q, QD, Dc, False, False)])
             mm([(E1, EC1, cl, False, False), (E2, EC2, cl, False, False), (Q, QC, cl, False, True)])
             many([act(hi, E1, sig, A("btc", s_(4 + t, 5 + t)), 400.0), act(lo, E2, sig, A("btc", s_(8 + t, 9 + t)), 400.0)])
-            send((A(HL, s_(2 * a, 2 * b)), A("hr%d" % t, s_(2 * a, 2 * b)), HN[t]))
+            send(((hi, lo), A("hr%d" % t, ln), HN[t]))
             act(A(bits, ln), Q, sig, A("btc", s_(16 + t, 17 + t)), 400.0)
             stage[0] = 0.0
-            if c == cfg["ZC"]:
-                zp = A(cfg["ZP"][0], s_(cfg["ZP"][1], cfg["ZP"][1] + L))
-                mm(grp(zp, [(HI, z), (HI, A("zr%d" % t))]))
-                if cfg["ZS"]:
-                    act(A("zh"), zp, idn, 1024.0, 1.0)
-                    act(A(Z, s_(L, 2 * L)), A("zh"), idn, -1024.0, 1.0)
-                else:
-                    ts(A(Z, s_(L, 2 * L)), zp, 1.5 * 2 ** 23, 1.5 * 2 ** 23, Alu.add, Alu.subtract)
-                ulist(Z, L)
+            if c == cfg["ZC"]: average()
         for c, (a, b) in enumerate(CH):
             n = b - a; ln = s_(a, b); up, Pt = at(c, "U"), at(c, "D", 1)
             hi, lo = A(HL, s_(2 * a, 2 * a + n)), A(HL, s_(2 * a + n, 2 * b))
-            mm(grp(up, [(IB, hi), (NI, lo), (MF, A(bits, ln))]))
-            act(A("sq", ln), up, Act.Square, -2048.0, 4096.0)
-            mm(grp(Pt, [(ONE, A("cst", 1, ln)), (IB, A("sq", ln)), (IB, A(Pn, ln))]))
-            tt(A("Lt", ln), A("Gs", ln), Pt, Alu.max)
+            mm(grp(up, [(IB, hi), (NI, lo), (MF2, A(bits, ln))]))
+            if cfg["DL"][c]:
+                pr = A("pr%d" % t, ln)
+                mm(grp(at(c, "X", 0), [(IB, A("Gc", ln)), (NI, pr)]) + grp(at(c, "X", 1), [(IB, pr), (NI, A(Pn, ln))]))
+                ts(A("sq", ln), up, -1.0, None, Alu.not_equal)
+                tt(at(c, "D"), A("sq", ln), at(c, "X", 0), Alu.mult)
+                tt(at(c, "D", 1), A("sq", ln), at(c, "X", 1), Alu.mult)
+                tt(at(c, "D", 3), A("mask2", ln), at(c, "D"), Alu.mult)
+                tt(A("Lt", ln), A(Pn, ln), at(c, "D", 1), Alu.add)
+                tt(A("tH", ln), A("Lt", ln), at(c, "D", 2), Alu.mult)
+            else:
+                act(A("sq", ln), up, Act.Square, 8192.0, 8192.0)
+                mm(grp(Pt, [(IB, A("cst", 1, ln)), (IB, A(Pn, ln)), (NI, A("sq", ln))]))
+                tt(A("Lt", ln), A("Gs", ln), Pt, Alu.max)
         kl, KR, KD = LP(16, 32), A("p0", s_(128, 128 + L)), A("p1", s_(0, L))
         mm([(KR, H64, A("vm"), True, False)])
         mm([(KD, IB, A("DC"), True, False), (KD, H64, A("vm"), False, False), (A("p1", s_(0, L, 16)), N64, A("vm", s_(0, L, 16)), False, False)])
-        if cfg["LX"]:
-            FA = lambda e: A("p4", s_(L * e, L * e + L))
-            mm([(FA(0), IB, A("DG"), True, False), (FA(1), IB, A("DG"), False, False)])
-            mm([(FA(0), MF, A(bits), False, False), (FA(1), MA, A(bits), False, True)])
-            scan(A("sd", 0), A("SQ"), FA(0), Alu.add, Alu.max)
-            tt(A("kc"), A("sd", 0, s_(15, L, 16)), A("nb", s_(0, 16)), Alu.add)
-            scan(A("sd", 1), A("SQ"), FA(1), Alu.add, Alu.max)
-            act(A("kb"), A("kc"), idn, -5.5413, -40.0)
-            many([act(A("as%d" % t, s_(16 * e, 16 * e + 16)), A("sd", 1, s_(15, L, 16)), sig, 200.0, -12.5) for e in range(2)])
-            toint(A("ti", s_(0, 16)), LP(0, 16))
-            aff(A("ti", s_(16, 32)), A("kc"), 513.0, 1.0, cfg["TI"])
-        else:
-            mm(grp(kl, [(IB, A("nb", s_(0, 16)))] + [(sel(2, r), A(bits, s_(r, L, 16))) for r in range(16)]))
-            act(A("kb"), kl, idn, -5.5413, -40.0)
-            act(A("kc"), kl, idn)
-            toint(A("ti", s_(0, 16)), LP(0, 16))
-            aff(A("ti", s_(16, 32)), kl, 513.0, 1.0, cfg["TI"])
-            mm(grp(LP(96, 112), [(sel(3, r), A(bits, s_(r, L, 16))) for r in range(16)]))
-            many([act(A("as%d" % t, s_(16 * e, 16 * e + 16)), LP(96, 112), sig, 200.0, -400.0) for e in range(2)])
+        FA = A("p4", s_(0, L)); own = lambda e: A("sd", e, s_(15, L, 16))
         mm([(KR, MF32, A(bits), False, True)])
+        mm(grp(FA, [(MA, A(bits))]))
+        scan(A("sd", 0), A("SQ"), KR, Alu.add, Alu.max)
+        scan(A("sd", 1), A("SQ"), FA, Alu.add, Alu.max)
+        act(A("kb"), own(0), idn, C(OK), -1280.0)
+        act(A("kc"), own(0), idn, C(OC), 1.0)
+        act(A("ti", 1), own(0), idn, C(OW), 32.0)
+        many([act(A("as%d" % t, e), own(1), sig, C(OA), -12.5) for e in range(3)])
+        toint(A("ti", 0), LP(0, 16))
         mm([(KD, MF32, A(bits), False, False), (A("p1", s_(0, L, 16)), NF32, A(bits, s_(0, L, 16)), False, False)])
-        mm([(A("p1", s_(r, L, 16)), NL, A("kc"), False, r == 15) for r in range(1, 16)])
+        mm([(A("p1", s_(r, L, 16)), NI, A("kc"), False, r == 15) for r in range(1, 16)])
         for a, b in CH:
             many([act(A("junk", h, s_(0, b - 16 * h - 16)), A("p0", s_(144 + 16 * h, 128 + b)), sig, A("kb", s_(h, h + 1)), 1280.0, A("ka", s_(h, h + 1)))
                   for h in range(a // 16, b // 16 - 1)])
         scan(A("sc"), KD, A("SP"), Alu.mult, Alu.add)
-        for e in (16, 0):
-            ts(A("tj", s_(16 + e, 32 + e)), A("ti", s_(e, 16 + e)), NV - 1, None, Alu.bitwise_and)
-        act(A("nb", s_(32, 48)), A("tj", s_(32, 48)), idn)
+        for e in ([s_(0, 2)] if cfg["AM"] else [1, 0]): ts(A("bs", e), A("ti", e), NV - 1, None, Alu.bitwise_and)
         ts(A("fl", 0), A("sc", s_(15, L, 16)), 0.0, 2048.0, Alu.is_equal, Alu.mult)
-        tt(A("fl", 1), A("fl", 0), A("tj", s_(32, 48)), Alu.add)
+        tt(A("fl", 1), A("fl", 0), A("bs", 1), Alu.add)
         aff(A("ki", 0), A("ka"), 2.0 ** 9, 2.0 ** 19, cfg["TI"])
         ts(A("ki", 1), A("ki", 0), 255 << 11, None, Alu.bitwise_and)
         tt(A("fl", 2), A("fl", 1), A("ki", 1), Alu.add)
@@ -469,7 +498,7 @@ def build(cfg=CFG):
             cp(A("woff"), A("fl", 3))
         send((A("as%d" % t), A("ar%d" % t), HZ[t]))
         if t == 0:
-            act(A("B", s_(0, NV)), A("bagi"), idn)
+            act(A("B", s_(0, NV)), A("bagi"), idn, -2048.0, 1.0)
         if not cfg["XV"]:
             xp = A("p4", s_(0, L))
             mm(grp(xp, [(IB, A("zm")), (IB, z)]))
@@ -477,58 +506,56 @@ def build(cfg=CFG):
         ts(A("xm"), A("xs"), 0.0, 256.0, Alu.is_lt, Alu.mult)
         stage[0] = cfg["XB"]
         for a in range(0, L, cfg["XP"]):
-            tt(ind(A("X"), A(of, s_(32 + a // 16, 32 + (a + cfg["XP"]) // 16))), A("xs", s_(a, a + cfg["XP"])), A("xm", s_(a, a + cfg["XP"])), Alu.add)
+            tt(ind(A("X"), A(of, 1, s_(a // 16, (a + cfg["XP"]) // 16))), A("xs", s_(a, a + cfg["XP"])), A("xm", s_(a, a + cfg["XP"])), Alu.add)
         stage[0] = 0.0
         if last:
             i = store("Y", A("X"), "yx", None, 3.5)
             ops[i]["after"] += [j for j, o_ in enumerate(ops) if o_["kind"] == "send"]
-        ts(A("tj", s_(0, 16)), A("ti", s_(0, 16)), 15, None, Alu.bitwise_and)
-        tt(A("dlt"), A("tj", s_(0, 32)), A("nb", s_(16, 48)), Alu.subtract)
+        ts(A("bs", 4), A("ti", 0), 15, None, Alu.bitwise_and)
+        tt(A("dlt", s_(0, 2)), A("bs", s_(0, 5, 4)), A("bs", s_(1, 6, 4)), Alu.subtract)
         for c, (a, b) in enumerate(CH):
-            n = b - a; hr = "hr%d" % t
-            Y = at(c, "D")
-            mm(grp(Y, [(IB, A("cst", 0, s_(a, b))), (IB, A("pr%d" % t, s_(a, b)))], stop=False))
-            mm(grp(Y, [(MI, A(hr, s_(2 * a, a + b))), (MI, A(hr, s_(a + b, 2 * b)))], start=False))
-            for pa in range(a, b, cfg["PO"]):
-                pb = min(b, pa + cfg["PO"]); ln = s_(pa, pb); H = at(c, "H", 0, pa - a, pb - a)
-                chain("po", tt(A("yi", ln), A("Lt", ln), at(c, "D", 0, pa - a, pb - a), Alu.max))
+            ln = s_(a, b); hr = A("hr%d" % t, ln); H = at(c, "H")
+            if cfg["DL"][c]:
+                mm(grp(H, [(bd(14), A("tH", ln))], stop=False))
+                tt(A("tF", ln), hr, at(c, "D", 3), Alu.mult)
+                tt(at(c, "D", 1), hr, at(c, "D"), Alu.mult)
+                mm(grp(H, [(A("SW"), A("tF", ln))], start=False))
+                tt(A("Fc", ln), A("Lt", ln), at(c, "D", 1), Alu.add)
+            else:
+                Y = at(c, "D")
+                mm(grp(Y, [(IB, A("cst", 0, ln)), (IB, A("pr%d" % t, ln))], stop=False))
+                mm(grp(Y, [(MI, hr)], start=False))
+                tt(A("yi", ln), A("Lt", ln), Y, Alu.max)
                 ts(A("Fi", ln), A("yi", ln), W - 1, None, Alu.bitwise_and)
+                act(A("Fc", ln), A("Fi", ln), idn, -2048.0, 1.0)
                 if cfg["HF"][c]:
-                    tt(A("tF", ln), A("Fi", ln), at(c, "D", 2, pa - a, pb - a), Alu.mult)
-                    act(A("Fc", ln), A("Fi", ln), idn)
+                    tt(A("tF", ln), A("Fi", ln), at(c, "D", 2), Alu.mult)
                     mm(grp(H, [(A("SW"), A("tF", ln))]))
                 else:
-                    act(A("Fc", ln), A("Fi", ln), idn)
-                    act(at(c, "D", 1, pa - a, pb - a), A("Fi", ln), idn, -2048.0, 1.0)
-                    tt(A("tH", ln), A("mask2", ln), at(c, "D", 1, pa - a, pb - a), Alu.mult)
+                    tt(A("tH", ln), A("Fc", ln), at(c, "D", 2), Alu.mult)
                     mm(grp(H, [(bd(14), A("tH", ln))]))
-                tt(A("t2", ln), A("mask2", ln), H, Alu.mult)
-                tt(ind(A("B"), A("woff", s_(pa // 16, pb // 16))), A("Fc", ln), A("t2", ln), Alu.add)
-        ar = "ar%d" % t; nx = "offs%d" % (t + 1)
-        tt(A("prd"), A(ar), A("dlt"), Alu.mult)
-        items = grp(LP(32, 48), [(IB, A("prd", s_(16, 32))), (IB, A("nb", s_(32, 48)))])
-        if not last:
-            items += grp(LP(48, 64), [(IB, A("prd", s_(0, 16))), (IB, A("nb", s_(16, 32)))])
-            items += grp(LP(64, 80), [(IB, A("prd", s_(0, 16))), (IB, A("nb", s_(16, 32))), (IB, li16)])
-        items += grp(LP(80, 96), [(I256, A(ar, s_(0, 16))), (IB, li)])
-        mm(items)
-        if last:
-            cp(A(nx, s_(48, 64)), LP(80, 96)); act(A("res"), LP(32, 48), idn)
-        else:
-            cp(A(nx), LP(32, 96)); act(A("nb", s_(16, 32)), LP(48, 64), idn)
-            toint(A("vi", 0), LP(32, 48))
-            ts(A("vi", 1), A("vi", 0), NV // 2 - 1, None, Alu.bitwise_and); act(A("nb", s_(0, 16)), A("vi", 1), idn, -512.0, 2.0)
-        act(A("ZZ%d" % (t + 1), s_(0, L)), ind(A(Z), A(nx, s_(48, 64))), Act.Copy)
+            tt(A("t2", ln), A("mask2", ln), H, Alu.mult)
+            tt(ind(A("B"), A("woff", s_(a // 16, b // 16))), A("Fc", ln), A("t2", ln), Alu.add)
+        nx = "offs%d" % (t + 1)
+        tt(A("prd"), A("ar%d" % t), A("dlt"), Alu.mult)
+        tt(A(nx), A("prd"), A("bs", s_(1, 4)), Alu.add)
+        if last: tt(A("res"), A("prd", 0), A("bs", 1), Alu.add)
+        act(A("ZZ%d" % (t + 1), s_(0, L)), ind(A(Z), A(nx, 2)), Act.Copy)
+    end = len(ops)
     store("Y", A("res"), "yv", None, 0.0)
     store("Y", A("ZZ3"), "yz", None, 0.3)
     h = NV // 4
     for e in range(2):
         pp = A("p%d" % (5 + e), s_(0, h))
-        act(pp, A("B", s_(2 * h + e * h, 3 * h + e * h)), idn, 0.0, 4096.0)
+        act(pp, A("B", s_(2 * h + e * h, 3 * h + e * h)), idn, 2048.0 * 4097, 4096.0)
         tt(A("pk", s_(e * h, e * h + h)), A("B", s_(e * h, e * h + h)), pp, Alu.add)
         store("YS"[e], A("pk", s_(e * h, e * h + h)), "yb", (e * h, e * h + h), 0.5)
-    name = [o["eng"] + ":" + (o["wr"] or o["rd"])[0][0].rstrip("0123456789") + ":" + str((o["wr"] or o["rd"])[0][1][-1][0]) for o in ops]
-    for a, b in zip(begin, begin[1:] + [len(ops)]):
+    name = [(o["wr"] or o["rd"])[0] for o in ops]
+    name = [o["eng"] + ":" + (b if b in o["banks"] else b.rstrip("0123456789")) + ":" + "".join(str(x[0]) for x in r) for o, (b, r) in zip(ops, name)]
+    name = [x + "<" + o["args"][-1][2][0].rstrip("0123") + "".join(str(y[0]) for y in o["args"][-1][2][2]) if o["kind"] == "mm" else x for x, o in zip(name, ops)]
+    for t, (a, b) in enumerate(zip(begin, begin[1:] + [end])):
+        for i in range(a, b):
+            ops[i]["role"] = (t, name[i] + "'" * name[i + 1:b].count(name[i]))
         for x, y in cfg["DUE"]:
             for i in range(a, b):
                 if name[i] == x: ops[i]["due"] += [j for j in range(a, b) if name[j] == y][:1]
@@ -561,7 +588,7 @@ def deps(ops):
             hist.setdefault(b, []).append((i, r, False))
         pred[i].discard(i)
         for j in pred[i]:
-            if o["eng"] == ops[j]["eng"] and o["kind"] in COMP and ops[j]["kind"] in COMP and (o["eng"] == "P" or j not in hard): free.add((j, i))
+            if o["eng"] == "P" == ops[j]["eng"]: free.add((j, i))
     succ = [[] for _ in ops]
     for i in range(n):
         for j in pred[i] | set(ops[i]["soft"]): succ[j].append(i)
@@ -624,13 +651,21 @@ def figs(fig):
     def slow(f, gam, sca, hop):
         return dict(fig, cy=f * fig["cy"], pcy=f * fig["pcy"], gam=f * gam * fig["gam"], sca=f * sca * fig["sca"], ov=f * fig["ov"],
                     sync=(0.5 + 0.5 * f) * fig["sync"], own=(0.5 + 0.5 * f) * fig["own"], hop=hop * fig["hop"])
-    return [fig, slow(1.45, 1.25, 1.4, 1.2), slow(1.25, 0.72, 0.6, 1.4), slow(1.15, 1.25, 0.8, 0.8)]
+    return [fig, slow(1.45, 1.25, 1.4, 1.15), slow(1.25, 0.72, 0.6, 1.25), slow(1.15, 1.25, 0.8, 0.9)]
 
 
-MID = dict(FIG, cy=1e-3, pcy=0.5e-3, gam=1.6e-3, sca=3.8e-3, sync=0.165, own=0.21, ov=0.021, hop=2.9)
+MID = dict(FIG, cy=1e-3, pcy=0.5e-3, gam=1.6e-3, sca=3.8e-3, sync=0.155, own=0.2, ov=0.019, hop=3.4)
 
 
-def plan(ops, cfg=CFG, fig=MID):
+def plan(ops, cfg=CFG):
+    dp = deps(ops); order = listed(ops, dp, cfg["ORDER"])
+    for r in range(cfg["ROUNDS"]):
+        if r: order = alike(ops, order, dp)
+        order, full, free = polish(ops, order, dp, cfg["MOVES"], r, 150.0)
+    return order, full, free
+
+
+def plan0(ops, cfg=CFG, fig=MID):
     dp = deps(ops); succ = dp[1]
     n = len(ops); c = costs(ops, fig); best = None
     for seed in range(cfg["SEEDS"]):
@@ -648,6 +683,50 @@ def plan(ops, cfg=CFG, fig=MID):
     return polish(ops, best[1], dp, cfg["MOVES"])
 
 
+def listed(ops, dp, lists, fig=MID):
+    pred, succ, free = dp; n = len(ops); c = costs(ops, fig)
+    must = [p | set(o["soft"]) for p, o in zip(pred, ops)]
+    byrole = {o["role"]: i for i, o in enumerate(ops) if o["role"]}
+    line = {e: [byrole[(t, e + ":" + x)] for t in range(RO) for x in names.split() if (t, e + ":" + x) in byrole] for e, names in lists.items()}
+    fixed = set(i for x in line.values() for i in x)
+    prio = [0.0] * n
+    for i in range(n - 1, -1, -1):
+        prio[i] = c[i] + ops[i]["lat"] + fig["sync"] + max([prio[k] for k in succ[i]], default=0.0) + ops[i]["bias"]
+    left = [len(p) for p in must]; ready = set(i for i in range(n) if not left[i]); fin = {}; busy = {}; seq = []
+    while ready:
+        can = [i for i in ready if i not in fixed or line[ops[i]["eng"]][0] == i] or list(ready)
+        start = {i: max([fin[j] + fig["sync"] for j in must[i]] + [busy.get(ops[i]["eng"], 0.0)]) for i in can}
+        i = min(can, key=lambda k: (round(start[k] * 5), k not in fixed, -prio[k]))
+        if i in fixed: line[ops[i]["eng"]].remove(i)
+        ready.remove(i); seq.append(i); fin[i] = start[i] + c[i] + ops[i]["lat"]
+        if ops[i]["eng"] != "R": busy[ops[i]["eng"]] = start[i] + c[i]
+        for k in succ[i]:
+            left[k] -= 1
+            if not left[k]: ready.add(k)
+    return seq
+
+
+def alike(ops, order, dp):
+    must = [p | set(o["soft"]) for p, o in zip(dp[0], ops)]
+    _, full, free = polish(ops, order, dp, 0)
+    beg = replay(ops, order, full, free, MID)[1]
+    zero = [min(beg[i] for i, o in enumerate(ops) if o["role"] and o["role"][0] == t) for t in range(RO)]
+    best = None
+    for s in range(-1, RO):
+        pat = {o["role"][1]: beg[i] - zero[s] for i, o in enumerate(ops) if o["role"] and o["role"][0] == s}
+        when = [zero[o["role"][0]] + pat[o["role"][1]] if o["role"] and o["role"][1] in pat else beg[i] for i, o in enumerate(ops)]
+        left = [len(p) for p in must]; ready = [i for i, x in enumerate(left) if not x]; seq = []
+        while ready:
+            i = min(ready, key=lambda k: when[k]); ready.remove(i); seq.append(i)
+            for k in dp[1][i]:
+                left[k] -= 1
+                if not left[k]: ready.append(k)
+        _, full, free = polish(ops, seq, dp, 0)
+        score = sum(replay(ops, seq, full, free, f)[0] / f["cy"] for f in figs(FIG))
+        if best is None or score < best[0]: best = (score, seq)
+    return best[1]
+
+
 def polish(ops, order, dp, moves, seed=0, heat=300.0):
     pred, succ, free = dp
     fs = figs(FIG); cs = [costs(ops, f) for f in fs]
@@ -655,26 +734,30 @@ def polish(ops, order, dp, moves, seed=0, heat=300.0):
     must = [p | set(o["soft"]) for p, o in zip(pred, ops)]
     lag = [[[(j, 0.0 if (j, i) in free else f["own"] if eng[j] == eng[i] else f["sync"]) for j in p] for i, p in enumerate(pred)] for f in fs]
 
-    def run(seq, k):
-        c = cs[k]; sy = fs[k]["sync"]; fin = [0.0] * len(ops); why = [None] * len(ops); busy = {}; last = {}
-        for i in seq:
-            e = eng[i]; t = 0.0; w = None
-            for j, d in lag[k][i]:
-                if fin[j] + d > t: t = fin[j] + d; w = (j, 0)
+    def score(seq, a=0, old=None):
+        prev = {}; last = {}; held = []
+        for n, i in enumerate(seq):
+            e = eng[i]; h = []
             for b in banks[i]:
                 d = last.setdefault(b, {})
-                for f, j in d.items():
-                    if f != e and fin[j] + sy > t: t = fin[j] + sy; w = (j, 1)
+                if n >= a: h += [j for f, j in d.items() if f != e]
                 d[e] = i
-            if e != "R":
-                if e in busy and busy[e][0] > t: t, w = busy[e][0], (busy[e][1], 1)
-                busy[e] = (t + c[i], i)
-            fin[i] = t + c[i] + lat[i]; why[i] = w
-        return fin, why
-
-    def score(seq):
-        r = [run(seq, k) for k in range(len(fs))]
-        return sum(max(x[0]) / f["cy"] for x, f in zip(r, fs)), r
+            if n >= a: held.append((i, h, prev.get(e)))
+            if e != "R": prev[e] = i
+        res = []
+        for k, f in enumerate(fs):
+            c = cs[k]; sy = f["sync"]; lg = lag[k]
+            fin, why = (list(old[k][0]), list(old[k][1])) if old else ([0.0] * len(ops), [None] * len(ops))
+            for i, h, p in held:
+                t = 0.0; w = None
+                for j, d in lg[i]:
+                    if fin[j] + d > t: t = fin[j] + d; w = (j, 0)
+                for j in h:
+                    if fin[j] + sy > t: t = fin[j] + sy; w = (j, 1)
+                if p is not None and fin[p] - lat[p] > t: t = fin[p] - lat[p]; w = (p, 1)
+                fin[i] = t + c[i] + lat[i]; why[i] = w
+            res.append((fin, why))
+        return sum(max(x[0]) / f["cy"] for x, f in zip(res, fs)), res
     rs = np.random.RandomState(seed); now, res = score(order); best = (now, order)
     for it in range(moves):
         fin, why = res[rs.randint(len(fs))]
@@ -699,7 +782,7 @@ def polish(ops, order, dp, moves, seed=0, heat=300.0):
                 if must[x] & take: take.add(x)
             seq = order[:a] + [x for x in mid if x not in take] + [x for x in mid if x in take] + order[b + 1:]
         if seq == order: continue
-        new, r = score(seq)
+        new, r = score(seq, a, res)
         if new < now + heat * (1 - it / moves) * rs.exponential():
             order, now, res = seq, new, r
             if now < best[0]: best = (now, order)
@@ -793,7 +876,10 @@ def rank_program(g, core, T, topo):
             q.dma_start(hbm(a[1], a[2]), R(a[0])).then_inc(semof[i][0], 16); continue
         else:
             sent += len(eng); to = [topo.addr(cores[(rank + x[2]) % N]) for x in a]
-            if len(a) == 1:
+            if not isinstance(a[0][0], Ap):
+                g.remote_dma_fused([RemoteDMATransfer(dst_ids=[DstId(rid=to[0][0], pnc=to[0][1])], dma_engine_mask=mask, remote_sem=semof[i][0],
+                                                      srcs=[R(x) for x in a[0][0]], dsts=[R(a[0][1])], alu_op=1)], local_sem=T.sem.sent)
+            elif len(a) == 1:
                 g.remote_dma(R(a[0][1]), R(a[0][0]), semof[i][0], T.sem.sent, to[0][1], to[0][0], mask)
             else:
                 m = len(eng) // len(a)

import numpy as np
from concourse.bass import DstId, RemoteDMATransfer
from concourse.mybir import AluOpType as Alu, ActivationFunctionType as Act

N, L, NV, W, RO = 8, 256, 1024, 4096, 3
HN, HZ = [1, 3, 6], [7, 2, 5]
BIG = 4096.0
NF = 20
F32, BF, F16, I32, U16 = "float32", "bfloat16", "float16", "int32", "uint16"

SCRATCH = {}


def _sb(name, shape, dt):
    SCRATCH[name] = ("sbuf", [128] + shape, dt)


for _n, _s, _d in [
    ("X", [W], BF), ("bagi", [NV], I32), ("B", [NV + L], F32), ("v0i", [16], I32), ("uwi", [4], I32), ("bti", [4], I32),
    ("xg", [16 * L], BF), ("mx", [16, L], BF), ("ab", [4, 512], BF), ("Poff", [L], U16),
    ("Dc", [L], F16), ("cs", [4, 7 * 128], BF), ("cl", [L], F16), ("mask2", [L], BF),
    ("sq", [L], BF), ("Gs", [L], F32), ("Lt", [L], F32),
    ("yi", [L], I32), ("Fi", [L], I32), ("Fc", [L], F32), ("tF", [L], F32), ("t2", [L], F32),
    ("zm", [L], BF), ("xs", [L], BF), ("xm", [L], BF), ("pk", [NV // 2], F32),
    ("ZZ0", [2 * L], BF), ("ZZ1", [2 * L], BF), ("ZZ2", [2 * L], BF), ("ZZ3", [L], BF),
    ("ik", [16], F32), ("pci", [2], I32), ("ci", [8], I32), ("col", [40], F32), ("cb", [8], BF), ("li", [48], BF),
    ("ff", [16, 7], F32), ("gg", [16, 7], F32), ("kk", [16, 7], F32), ("ix", [144], BF), ("gx", [128], BF), ("ms", [5, 144], BF),
    ("pf", [16, NF], F16), ("BD", [128, NF], F16), ("M", [22, 128], F16), ("MB", [2, 128], BF), ("T4", [NV], BF), ("vm", [L], BF), ("junk", [16, 128], BF), ("SW", [128], F32),
    ("gm", [8], F32), ("mw", [144], F16), ("km1", [16], F32), ("dg", [16], F32), ("dgs", [16], F32), ("r0", [16], F32), ("wi", [32], I32),
    ("thr", [16], F32), ("gmb", [16], BF), ("DTs", [L], F16), ("tH", [L], F16), ("sx", [L], BF), ("DC", [L], BF), ("SP", [L], BF), ("sc", [L], F32),
    ("SQ", [L], BF), ("sd", [2, L], F32), ("zh", [L], F16),
    ("cst", [2, L], BF), ("btb", [4], BF), ("btc", [20], F32), ("uf", [4], F32), ("tf", [32], F32),
    ("ti", [2, 16], I32), ("bs", [6, 16], I32), ("dlt", [3, 16], F32), ("prd", [3, 16], F32), ("Gc", [L], F16),
    ("kb", [16], F32), ("kc", [16], F16), ("ka", [16], F32), ("ki", [2, 16], I32), ("vi", [16], I32), ("fl", [4, 16], F32), ("lf", [16], F32), ("woff", [16], U16), ("res", [16], F32),
]:
    _sb(_n, _s, _d)
for _t in range(RO):
    _sb("Pc%d" % _t, [L], F16); _sb("pr%d" % _t, [L], F16); _sb("zr%d" % _t, [L], BF)
    _sb("hl%d" % _t, [2 * L], BF); _sb("hr%d" % _t, [L], BF); _sb("bits%d" % _t, [L], BF)
    _sb("as%d" % _t, [3, 16], BF); _sb("ar%d" % _t, [3, 16], BF)
for _t in range(RO + 1):
    _sb("offs%d" % _t, [3, 16], U16)
for _b in range(8):
    SCRATCH["p%d" % _b] = ("psum", [128, 512], F32)

SEMAPHORES = ["eV", "eS", "eP", "eG", "sent"] + ["d%d" % i for i in range(24)] + ["r%d" % i for i in range(24)]

FIG = {"cy": 0.83e-3, "gam": 1.3e-3, "sca": 3.15e-3, "pcy": 0.42e-3, "iss": 0.5, "hop": 3.2, "sync": 0.14, "own": 0.18, "ov": 0.016}
CFG = {"CH": [(0, 128), (128, 256)],
       "PS": [("V", 0, 64), ("S", 64, 128), ("V", 128, 256)],
       "GA": [("V", 0, 64), ("S", 64, 128), ("S", 128, 192), ("S", 192, 256)],
       "UN": [(0, 128, 0), (128, 192, 0), (192, 256, 0)],
       "PL": [{"D": ("p2", 0), "A": ("p4", 0), "B": ("p5", 0), "E": ("p6", 0), "U": ("p2", 384), "H": ("p0", 384), "X": ("p4", 256)},
              {"D": ("p3", 0), "A": ("p0", 0), "B": ("p1", 0), "E": ("p7", 0), "U": ("p3", 384), "H": ("p1", 384), "X": ("p1", 256)}],
       "DUE": [("V:xs:0", "V:mx:0"), ("V:X:0", "V:cs:0"), ("V:ZZ:256", "V:cl:128"), ("S:vm:0", "S:Dc:128"), ("V:tj:0", "V:sc:0"),
               ("V:Lt:0", "V:sd:0"), ("V:woff:0", "V:tF:128"), ("V:t:0", "V:tF:128"), ("S:B:0", "S:ka:0"), ("V:dlt:0", "V:tF:128"),
               ("S:Gc:128", "V:cl:128")],
       "DL": [1, 1], "BE": "S", "ROUNDS": 5, "AM": 1,
       "ORDER": {
           "V": "Poff:0 Poff:128 xg:0 Pc:0 mx:10 mx:90 mx:1128 mx:9128 mx:1192 mx:9192 xs:0 Fi:0 xm:0 Fi:128 X:0' cl:0 cs:10 X:0 cl:128 sq:0 p2:0 bs:50 "
                "sd:10 sd:00 p2:128' p2:384 Lt:0 ZZ:256 tH:0 sq:128 sc:0 p3:128' p3:0 fl:00 Lt:128 tF:0 p2:128 p3:384 bs:40 bs:00 tH:128 ki:10 fl:10 "
                "Fc:0 dlt:00 fl:20 t:0 woff:0 tF:128 p3:128 B:0' Fc:128 prd:00 t:128 offs:00 B:0 res:0",
           "S": "Poff:64 xg:1024 xg:2048 xg:3072 DTs:0 zm:0 bs:20 Dc:0 yi:128 yi:0 cs:00 cs:0512 Dc:128 Gc:0 cs:1384 p2:256 hl:0 bits:0 vm:0 Gc:128 mask:128 "
                "bits:128 hl:256 mask:0 as:00 kb:0 kc:0 p3:256 ka:0 ka:8 ti:00 ti:10 ki:00 ZZ:0",
           "P": "p0:0<xg0 p2:0<gmb8 p2:8<gmb8 p6:384<Pc0 p6:0<bits0 p7:384<Pc128 p7:0<bits128 p2:1<gmb0 p1:0<xg2048 p3:0<xg2055 p3:0<xg2063 p2:9<gmb0 "
                "p0:0<xg3072 p3:64<xg3079 p4:0<M00 p3:0<mx8128 p3:0<mx0128 p4:0<Dc0 p5:0<Dc0 p3:64<mx8192 p3:64<xg3087 p3:64<mx0192 p2:128<cs0384 "
                "p2:128<cs0768 p0:0<Dc128 p1:0<Dc128 p6:0<Dc0 p6:0<cl0 p4:256<Pc0 p3:128<cs1256 p3:128<cs1768 p2:384<bits0 p7:0<Dc128 p7:0<cl128 p0:128<vm0 "
                "p5:0<zr0 p4:0<bits0 p0:128<bits0 p3:384<bits128 p1:256<Pc128 p1:0<vm0 p1:0<bits0 p1:1<kc0 p5:384<ZZ271 p0:384<tH0 p1:384<tH128",
           "G": "ZZ:0 Pc:0 hl:0 hl:256 as:00"},
       "AB": "p7", "ZC": 0, "ZP": ("p5", 0), "ZL": 1,
       "DT": ["S", 0], "RW": 9, "NS": [[("p4", 4, "S"), ("p5", 3, "S")], [("p1", 3, "V"), ("p0", 4, "S")]], "RT": [0, 0], "HF": [1, 1], "RB": [0.0, 0.0], "UB": 0.0, "XV": 1, "LX": 1, "ZS": 0,
       "NA": 8, "KL": 2, "XP": 128, "XB": 0.0, "PO": 128, "DC": "SS", "TI": "S", "TU": 1, "SW": 0.5, "IT": 2, "MOVES": 5000, "SEEDS": 3, "JIT": 0.1}


class Ap(tuple):
    pass


def ap(buf, *idx, part=None):
    shape = SCRATCH[buf][1][1:]
    idx = list(idx) + [slice(None)] * (len(shape) - len(idx))
    reg, cnt = [], 1
    for i, n in zip(idx, shape):
        if isinstance(i, slice):
            r = range(*i.indices(n)); reg.append((r[0], r[-1] + 1)); cnt *= len(r)
        else:
            reg.append((i, i + 1))
    return Ap((buf, tuple(idx), tuple(reg), cnt, part, None))


def ind(win, off):
    return Ap((win[0], win[1], win[2], off[3] * 16, None, off))


def s_(a, b, c=None):
    return slice(a, b, c)


def build(cfg=CFG):
    ops = []; tab = []; stage = [0.0]; tail = {}
    CH = cfg["CH"]

    def add(eng, kind, args, reads, writes, cost, lat=0.0):
        rd, wr = [], []
        for a in reads:
            if isinstance(a, Ap):
                rd.append((a[0], a[2]))
                if a[5] is not None: rd.append((a[5][0], a[5][2]))
            elif isinstance(a, tuple):
                rd.append(a)
        for a in writes:
            if isinstance(a, Ap):
                wr.append((a[0], a[2]))
                if a[5] is not None: rd.append((a[5][0], a[5][2]))
            else:
                wr.append(a)
        banks = set(b for b, _ in rd + wr if b in SCRATCH and SCRATCH[b][0] == "psum")
        ops.append({"eng": eng, "kind": kind, "args": args, "rd": rd, "wr": wr, "cost": cost, "lat": lat, "banks": banks, "after": [], "soft": [], "due": [], "role": None, "bias": stage[0]})
        return len(ops) - 1

    def chain(key, i):
        if key in tail: ops[i]["soft"].append(tail[key])
        if ops[i]["kind"] == "load": ops[i]["bias"] = 100.0 - i
        tail[key] = i

    def two(*a):
        return all(SCRATCH[x[0]][2] in (BF, F16, U16) for x in a)

    def vcost(out, in0, per):
        if in0[5] is not None: return (0.05, in0[3], "gam")
        if out[5] is not None: return (0.05, out[3], "sca")
        return (0.0, max(64, out[3] * per), "cy")

    def ts(out, in0, s1, s2, op0, op1=None):
        return add("V", "ts", (out, in0, s1, s2, op0, op1), [in0, s1, s2], [out], vcost(out, in0, 0.5 if two(out, in0) else 1))

    def tt(out, in0, in1, op):
        ps = SCRATCH[in0[0]][0] == "psum" or SCRATCH[in1[0]][0] == "psum"
        return add("V", "tt", (out, in0, in1, op), [in0, in1], [out], vcost(out, in0, 1 if ps else 2))

    def tts(items):
        return add("V", "tts", items, [x for a in items for x in a[1:3]], [a[0] for a in items], (0.0, sum(max(64, a[0][3]) for a in items), "cy"))

    def cp(out, in0):
        return add("V", "cp", (out, in0), [in0], [out], vcost(out, in0, 0.5 if two(out, in0) else 1))

    def mset(out, v):
        return add("V", "mset", (out, v), [], [out], vcost(out, out, 0.5 if two(out) else 1))

    def scan(out, d0, d1, op0, op1):
        return add("V", "scan", (out, d0, d1, op0, op1), [d0, d1], [out], vcost(out, out, 1))

    def act(out, in0, fn, bias=0.0, scale=1.0, acc=None):
        c = (0.065, in0[3], "gam") if in0[5] is not None else (0.02 if acc else 0.0, max(64, in0[3]), "cy")
        if fn == Act.Sigmoid and not tab:
            tab.append(1); c = (1.3, c[1], c[2])
        return add("S", "act", (out, in0, fn, bias, scale, acc), [in0, bias, scale], [acc, out] if acc else [out], c)

    def many(ids):
        part = [ops.pop() for _ in ids][::-1]; o = dict(part[0])
        o.update(kind="many", args=part, rd=sum([p["rd"] for p in part], []), wr=sum([p["wr"] for p in part], []),
                 cost=(sum(p["cost"][0] for p in part), sum(p["cost"][1] for p in part), "cy"), banks=set().union(*[p["banks"] for p in part]))
        ops.append(o)
        return len(ops) - 1

    def aff(out, in0, bias, scale, eng):
        if eng == "S": return act(out, in0, Act.Identity, bias, scale)
        return ts(out, in0, scale, bias, Alu.mult, Alu.add)

    def mm(items, area=()):
        outs = [i[0] for i in items]
        keys = [("open" + b, ((0, 1),)) for b in set(o[0] for o in outs)]
        first, final = items[0][3], items[-1][4]
        c = sum(max(64, i[2][3]) * (4 if SCRATCH[i[2][0]][2] == F32 else 1) for i in items)
        rd = [i[1] for i in items] + [i[2] for i in items]
        if first and final: rd, wr = rd + keys, outs
        elif first or final: wr = outs + keys + list(area)
        else: rd, wr = outs + rd + keys, []
        return add("P", "mm", items, rd, wr, (0.03, c, "pcy"))

    def grp(out, pairs, start=True, stop=True):
        return [(out, a, b, start and i == 0, stop and i == len(pairs) - 1) for i, (a, b) in enumerate(pairs)]

    def iota(out, pat, base, cm):
        return add("G", "iota", (out, pat, base, cm), [], [out], (0.13, 2 * out[3], "cy"))

    def load(q, buf, name, idx, us):
        return add(q, "load", (buf, name, idx), [], [buf], (0.06, 0, "cy"), 1.6 + us)

    def store(q, buf, name, idx, us):
        return add(q, "store", (buf, name, idx), [buf], [], (0.06, 0, "cy"), 1.6 + us)

    def send(*trs):
        i = add("G", "send", trs, [y for x in trs for y in ([x[0]] if isinstance(x[0], Ap) else x[0])], [], (0.0, 1, "iss"))
        j = add("R", "recv", trs, [], [x[1] for x in trs], (0.0, 1, "hop"))
        ops[j]["after"].append(i)
        return i

    A = ap
    C = lambda j: A("col", s_(j, j + 1))
    bd = lambda m: A("BD", s_(None, None), m)
    pf = lambda m: A("pf", s_(None, None), m)
    M = lambda m: A("M", m)
    sel = lambda m, r: A("ms", m, s_(15 - r, 143 - r))
    ik = A("ik"); idn = Act.Identity; sig = Act.Sigmoid

    chain("ly", load("Y", A("bagi"), "bag", None, 1.5))
    chain("ls", load("S", A("v0i"), "v0", None, 0.0))
    chain("ls", load("S", A("uwi", s_(0, 1)), "uw", None, 0.5))
    chain("ly", load("Y", A("X"), "xt", None, 3.4))
    chain("ly", load("Y", A("ZZ0", s_(0, L)), "z0", None, 3.6))
    mset(A("bti"), 0)
    chain("ly", load("Y", A("bti", s_(0, 3), part=s_(0, 128, 16)), "bt", None, 3.5))

    iota(A("pci", s_(0, 1)), [[1, 1]], 0, 1)
    iota(ik, [[1, 16]], 0, 0)
    iota(A("ix"), [[1, 144]], 0, 0)
    iota(A("gx"), [[1, 8], [0, 16]], 0, 0)
    iota(A("ff"), [[1, 16], [1, 7]], 1, 0)
    iota(A("gg"), [[-1, 16], [1, 7]], 1, 0)
    iota(A("kk"), [[1, 16], [0, 7]], 0, 0)
    iota(A("sx"), [[0, 16], [1, 16]], 0, 0)
    iota(A("T4"), [[0, 2], [4, 512]], -1024, 0)
    (J, GC, MC, NJ, PJ, J0, JG, NJG, NJ0, R13, R16, HALF, JB, NJB, PP, UH, J12, CC, A32, PC, S0, S1, C1, NC1, QS, QB, TW, J16) = range(28)
    pci = A("pci", s_(0, 1))
    cp(C(PP), pci)
    ts(A("ci", s_(0, 1)), pci, 15, None, Alu.bitwise_and); cp(C(J), A("ci", s_(0, 1)))
    ts(A("ci", s_(1, 2)), pci, 4, None, Alu.arith_shift_right); cp(C(GC), A("ci", s_(1, 2)))
    ts(A("dg"), ik, C(J), None, Alu.is_equal)
    dg = A("dg"); dgc = lambda j: A("dg", s_(j, j + 1))
    J0c = dgc(0)
    act(C(TW), C(J), idn, -400 * 15.5, 400.0)
    act(A("cb", s_(0, 7)), A("ik", s_(1, 8)), sig, C(TW), 400.0)
    aff(C(MC), C(GC), 15.0, 16.0, "V")
    aff(C(NJ), C(J), -7.5, -1.0, "V"); aff(C(PJ), C(J), -7.5, 1.0, "V")
    for c, b, s in [(JG, 1.0, -1.0), (NJG, -1.0, 1.0), (R13, 0.0, -9 * BIG), (R16, 0.0, 12 * BIG), (HALF, 0.5, -1.0), (JB, BIG, -BIG),
                    (NJB, -BIG, BIG), (C1, 12288.0, -2048.0), (QS, 400.0, -400.0)]:
        act(C(c), J0c, idn, b, s)
    act(C(NC1), C(C1), idn, 0.0, -1.0)
    act(C(S0), J0c, idn, 0.0, 1.0 / 32); act(C(S1), J0c, idn, 0.0, -1.0 / 32); act(C(J16), C(J), idn, 0.0, 16.0)
    tt(C(J12), dgc(1), dgc(2), Alu.add)
    act(C(A32), C(J12), idn, 0.0, 32.0)
    act(A("tf", s_(1, 2)), J0c, idn, 400 * 12288.0, 200.0)
    ts(C(QB), dgc(2), -800 * 12288.0, A("tf", s_(1, 2)), Alu.mult, Alu.add)
    ts(A("gm"), A("ik", s_(0, 8)), C(GC), None, Alu.is_equal)
    ts(A("km1"), ik, 1.0, None, Alu.min)
    ts(A("li", s_(0, 16)), ik, 16.0, C(J), Alu.mult, Alu.add)
    ts(A("li", s_(16, 32)), ik, 256.0, C(J16), Alu.mult, Alu.add)
    act(A("lf"), A("li", s_(0, 16)), idn, 1024.0, 1.0)
    mset(A("ka"), 0.0)
    mset(A("cst", 0), 2048.0)
    mset(A("cst", 1), 10240.0)
    apart = any(u[2] for u in cfg["UN"])
    for m, v in enumerate([2.0, -1.0, J0c, C(J12), 1.0]):
        if m < 2 or (m == 4 and apart): ts(A("ms", m), A("ix"), C(MC), v, Alu.is_equal, Alu.mult)
    IB, NI, HI, TWO, I256, NL, DJ, NDJ, ONE, NONE, EC1, EC2, MA, MF, QD, QC, QA, H64, N64, MF32, NF32 = [M(m) for m in range(21)]
    MI = A("MB", 0)
    for m, v in [(IB, 1.0), (DJ, C(JG)), (NDJ, C(NJG)), (HI, 511.0 / 1024), (H64, 1.0 / 64)]:
        ts(m, A("ix", s_(0, 128)), C(PP), v, Alu.is_equal, Alu.mult)
    for m, v in [(NI, -1.0), (N64, -1.0 / 64), (MI, -2.0 ** 25)]:
        act(m, IB, idn, 0.0, v)
    ts(ONE, A("gx"), C(GC), None, Alu.is_equal)
    ts(NONE, A("gx"), C(GC), -1.0, Alu.is_equal, Alu.mult)
    for m, v in [(EC1, C(NJG)), (EC2, C(JG)), (MA, C(A32)), (MF32, C(S0)), (NF32, C(S1))]:
        act(m, ONE, idn, 0.0, v)
    MF2 = TWO
    act(MF2, MF32, idn, 0.0, -64.0)
    cp(A("uf", s_(0, 1)), A("uwi", s_(0, 1)))
    act(A("tf", s_(16, 32)), ik, idn, 1.0, 2.0)
    ts(A("wi", s_(0, 16)), A("tf", s_(16, 32)), A("uf", s_(0, 1)), 2048.0, Alu.mult, Alu.add)
    ts(A("wi", s_(16, 32)), A("wi", s_(0, 16)), W - 1, None, Alu.bitwise_and)
    ts(pf(18), A("wi", s_(16, 32)), -2048.0, None, Alu.add)
    ts(C(UH), A("wi", s_(16, 17)), -2048.0, None, Alu.add)
    ts(A("mw"), A("ix"), C(MC), C(UH), Alu.is_equal, Alu.mult)
    for nm, bias, neg, dst in [("ff", NJ, NJG, A("pf", s_(None, None), s_(0, 7))), ("gg", PJ, NJB, A("pf", s_(None, None), s_(7, 14)))]:
        act(A(nm), A(nm), Act.Square, C(bias))
        ts(A(nm), A(nm), 56.25, C(neg), Alu.is_equal, Alu.mult)
        mset(A(nm, 0), 0.0)
        if nm == "ff":
            ts(A("kk"), A("kk"), C(J), C(JG), Alu.is_equal, Alu.mult)
        else:
            ts(A("kk"), A("kk"), BIG, None, Alu.mult)
            ts(A("r0"), A("km1"), C(R13), C(R16), Alu.mult, Alu.add)
            tt(A(nm, s_(None, None), 0), A(nm, s_(None, None), 0), A("r0"), Alu.add)
        tt(dst, A(nm), A("kk"), Alu.add)
    act(pf(14), dg, idn, 1.0, -2.0)
    ts(pf(15), ik, 1.5, 2.0, Alu.is_lt, Alu.mult)
    ts(pf(19), pf(15), -1.0, None, Alu.add)
    act(pf(16), A("km1"), idn)
    ts(pf(17), ik, 15.5 - cfg["NA"], -1.0, Alu.is_lt, Alu.mult)
    for gq in range(8):
        ts(A("BD", s_(16 * gq, 16 * gq + 16)), A("pf"), A("gm", s_(gq, gq + 1)), None, Alu.mult)
    act(A("SW"), bd(14), idn)
    ts(QD, bd(19), J0c, None, Alu.mult); ts(QC, bd(19), C(NJG), None, Alu.mult); ts(QA, bd(16), C(A32), None, Alu.mult)
    NX, MW = bd(17), bd(18)
    ts(A("thr", s_(0, 7)), A("cb", s_(0, 7)), -1.0, C(HALF), Alu.mult, Alu.add)
    act(A("thr", s_(8, 15)), A("thr", s_(0, 7)), idn, 0.0, -400.0)
    act(A("gmb", s_(0, 8)), A("gm"), idn, 0.0, 2.0); act(A("gmb", s_(8, 16)), A("gm"), idn, 0.0, -1.0)
    ts(A("SP"), A("sx"), 0.0, None, Alu.is_equal)
    ts(A("DC"), A("sx"), C(J), 64.0, Alu.is_le, Alu.mult)
    ts(A("SQ"), A("DC"), -16.5, 32.0, Alu.mult, Alu.add)
    mset(A("DC", s_(0, L, 16)), 0.0)
    OK, OC, OW, OA = 28, 29, 30, 31
    for c, b, s in [(OK, 1280 * 480 - 5.5413, -1280 * 32.0), (OC, -480.0, 32.0), (OW, 513 - 32 * 480.0, 1024.0), (OA, 200 + 12.5 * 480, -400.0)]:
        act(C(c), C(J), idn, b, s)
    cp(A("btb"), A("bti"))
    mm(grp(A("p5", s_(496, 500)), [(NONE, A("btb"))]))
    ts(A("tf", s_(4, 8)), A("km1", s_(0, 4)), -32.0, -0.5, Alu.mult, Alu.add)
    tt(A("btc", s_(0, 4)), A("p5", s_(496, 500)), A("tf", s_(4, 8)), Alu.add)
    ts(A("btc", s_(4, 8)), A("btc", s_(0, 4)), C(C1), 400.0, Alu.add, Alu.mult)
    ts(A("btc", s_(8, 12)), A("btc", s_(0, 4)), C(NC1), 400.0, Alu.add, Alu.mult)
    ts(A("btc", s_(16, 20)), A("btc", s_(0, 4)), C(QS), C(QB), Alu.mult, Alu.add)

    LP = lambda a, b, c=None: A("p5", s_(384 + a, 384 + b, c))
    li, li16, one = A("li", s_(0, 16)), A("li", s_(16, 32)), A("li", s_(32, 48))

    def ulist(z, zo):
        mm(grp(LP(0, 16), [(A("mw", s_(15 - r, 143 - r)), A(z, s_(zo + r, zo + L, 16))) for r in range(16)]))

    def toint(out, in0):
        return act(out, in0, idn) if cfg["TI"] == "S" else cp(out, in0)

    cp(A("offs0", 0), A("v0i"))
    ulist("ZZ0", 0)
    toint(A("ti", 0), LP(0, 16))
    ts(A("bs", 4), A("ti", 0), 15, None, Alu.bitwise_and)
    tt(A("offs0", 1), A("bs", 4), li16, Alu.add)
    act(A("bs", 3), li, idn)
    mset(A("dlt", 2), 256.0)

    begin = []
    for t in range(RO):
        begin.append(len(ops))
        Z = "ZZ%d" % t; z = A(Z, s_(0, L)); last = t == RO - 1
        of = "offs%d" % t; coff = A(of, 1); bits = "bits%d" % t
        for e, a, b in (cfg["PS"] if t else [("V", 0, L)]):
            src = ind(A("B", s_(0, NV)) if t else A("bagi"), A(of, 0, s_(a // 16, b // 16)))
            if e == "V": chain("vg", ts(A("Poff", s_(a, b)), src, 2048.0 if t else 0.0, None, Alu.add))
            else: chain("sg", act(A("Poff", s_(a, b)), src, idn, 2048.0, 1.0))
        aff(A("bs", 2), A(of, 1), 0.0, 1.0, cfg["BE"])
        ts(A("bs", 5), A("bs", 2), 15, None, Alu.bitwise_and)
        Pn = "Pc%d" % t; HL = "hl%d" % t
        ts(A(Pn), A("Poff"), -2048.0, None, Alu.add)
        if t == 0 or cfg["ZC"] < 0:
            i = send((z, A("zr%d" % t), HZ[t]))
            send((A(Pn), A("pr%d" % t), HN[t]))
        else:
            send((z, A("zr%d" % t), HZ[t]), (A(Pn), A("pr%d" % t), HN[t]))
        act(A("vm"), ind(A("T4"), A(of, 0)), Act.Copy)
        if cfg["XV"]:
            act(A("zm"), z, idn, -256.0, 1.0)
            tt(A("xs"), ind(A("X"), coff), A("zm"), Alu.add)
        else:
            act(A("zm"), ind(A("X"), coff), idn, -256.0, 1.0)
        for e, a, b in cfg["GA"]:
            stage[0] = cfg["SW"] * (L - b) / 64 + cfg["UB"]
            src = ind(A("X"), A("Poff", s_(a, b)))
            if e == "V": chain("vg", cp(A("xg", s_(16 * a, 16 * b)), src))
            else: chain("sg", act(A("xg", s_(16 * a, 16 * b)), src, Act.Copy))
        stage[0] = 0.0
        xk = lambda p, q, k: A("xg", s_(16 * p + k, 16 * q, 16))

        def at(c, key, i=0, p=0, q=None):
            bank, off = cfg["PL"][c][key]; n = CH[c][1] - CH[c][0]
            return A(bank, s_(off + i * n + p, off + i * n + (n if q is None else q)))

        def average():
            zp = A(cfg["ZP"][0], s_(cfg["ZP"][1], cfg["ZP"][1] + L))
            mm(grp(zp, [(HI, z), (HI, A("zr%d" % t))]))
            if cfg["ZS"]:
                act(A("zh"), zp, idn, 1024.0, 1.0)
                act(A(Z, s_(L, 2 * L)), A("zh"), idn, -1024.0, 1.0)
            else:
                ts(A(Z, s_(L, 2 * L)), zp, 1.5 * 2 ** 23, 1.5 * 2 ** 23, Alu.add, Alu.subtract)
            ulist(Z, L)
        if cfg["ZC"] < 0: average()
        for c, (a, b) in enumerate(CH):
            n = b - a; ln = s_(a, b); pd = cfg["PL"][c]["D"][0]
            for iu, (u0, u1, ns) in enumerate(cfg["UN"]):
                if u0 < a or u1 > b: continue
                stage[0] = cfg["SW"] * (L - u1) / 64 + cfg["UB"]
                un = u1 - u0; lu = s_(u0, u1); x0 = A("p%d" % (iu % 2), s_(0, un)); D = at(c, "D", 0, u0 - a, u1 - a)
                kv = list(range(1, 16 - ns)) + [0]; step = -(-len(kv) // cfg["KL"])
                mm(grp(x0, [(IB, xk(u0, u1, 0))]))
                if ns:
                    pe = cfg["AB"]
                    mm([m for i in range(ns) for m in grp(A(pe, s_(i * un, i * un + un)), [(IB, xk(u0, u1, 16 - ns + i)), (NI, xk(u0, u1, 0))])])
                    act(A("ab", iu % 4, s_(0, ns * un)), A(pe, s_(0, ns * un)), Act.Abs)
                dt = cfg["DT"][c]; rt = cfg["RT"][c]
                if rt:
                    if u0 == a:
                        own = [(A(rt, s_(k, 128, 16)), xk(a, b, k) if k else A(Z, ln), A("gmb", s_(8, 16)), k == 0, k == 15) for k in range(16)]
                        for i in (0, 8): mm(own[i:i + 8], [A(rt, s_(0, 128))])
                        aff(A("DTs", ln), A(rt, s_(0, 128)), 2048.0, 1.0, "S")
                    mm(grp(D, [(NONE, xk(u0, u1, 0))], u0 == a, False), [at(c, "D")])
                    if u0 == a: mm([(at(c, "D"), A("DTs", ln), IB, False, False)])
                elif not dt:
                    raw = grp(D, [(NX if ns else NONE, xk(u0, u1, 0)), (sel(1, 0), A(Z, lu))] + [(sel(1, k), xk(u0, u1, k)) for k in kv[:-1]], u0 == a, False)
                    for i in range(0, len(raw), cfg["RW"]): mm(raw[i:i + cfg["RW"]], [at(c, "D")])
                for i in range(0, len(kv), step):
                    kl = kv[i:i + step]
                    chain("mx", tts([(A("mx", k, lu), xk(u0, u1, k) if k else A(Z, lu), x0, Alu.max) for k in kl]))
                    if dt: continue
                    if ns and 0 in kl:
                        mm(grp(D, [(sel(4, 16 - ns + i), A("ab", iu % 4, s_(i * un, i * un + un))) for i in range(ns)], start=False, stop=False))
                    mm(grp(D, [(sel(0, k), A("mx", k, lu)) for k in kl], start=False, stop=0 in kl and u1 == b), [at(c, "D")])
            stage[0] = cfg["RB"][c]
            Dc = A("Dc", ln); cl = A("cl", ln); tp = at(c, "D", 1); cs = lambda x: A("cs", c, s_(x * n, x * n + n))
            if dt:
                pn = s_(0, n); DT = lambda k: A(pd, s_(k, 128, 16), part=pn)
                raw = ([(A(pd, s_(0, 128), part=pn), xk(a, b, 0), NONE, True, False)]
                       + [(DT(k), xk(a, b, k) if k else A(Z, ln), A("gmb", s_(8, 16)), False, False) for k in range(16)])
                for i in range(0, len(raw), cfg["RW"]): mm(raw[i:i + cfg["RW"]])
                for i in range(0, 16, step):
                    mm([(DT(k), A("mx", k, ln), A("gmb", s_(0, 8)), False, k == 0) for k in kv[i:i + step]], [A(pd, s_(0, 128))])
                DTs = A("DTs", s_(128 * (c % 2), 128 * (c % 2) + 128), part=pn)
                aff(DTs, A(pd, s_(0, 128), part=pn), -2048.0, 1.0, dt)
                mm(grp(at(c, "A"), [(DTs, A("M", 0, s_(0, n), part=pn))]))
                aff(Dc, at(c, "A"), 0.0, 1.0, cfg["DC"][c])
            else:
                aff(Dc, at(c, "D"), -4096.0 if rt else -2048.0, 1.0, cfg["DC"][c])
            parts = []; s0 = 0
            for bank, cnt, e in cfg["NS"][c]:
                so = range(s0, s0 + cnt); s0 += cnt; parts.append(so)
                dif = lambda s: A(bank, s_((s - so[0]) * n, (s - so[0] + 1) * n))
                mm([(dif(s), bd(s), Dc, True, True) for s in so])
                if e == "S": many([act(cs(s), dif(s), sig, A("thr", s_(8 + s, 9 + s)), 400.0) for s in so])
                else: many([ts(cs(s), dif(s), A("thr", s_(s, s + 1)), None, Alu.is_gt) for s in so])
            for i, so in enumerate(parts):
                mm(grp(tp, [(DJ, Dc)] * (i == 0) + [(bd(7 + s), cs(s)) for s in so], i == 0, i == len(parts) - 1))
            ts(cl, tp, -2048.0, 2048.0, Alu.max, Alu.min)
            act(A("mask2", ln), tp, sig, -16 * (9.5 * BIG - 8), 16.0)
            act(at(c, "D", 2), tp, sig, -16 * (9.5 * BIG - 8), 16.0)
            prev = A("bits%d" % (t - 1), ln) if t else None
            E1, E2, Q, Gp = [at(c, "E", e) for e in range(4)]
            hi, lo = A(HL, s_(2 * a, 2 * a + n)), A(HL, s_(2 * a + n, 2 * b))
            mm(grp(Gp, [(MW, A(Z, ln)), (IB, A(Pn, ln))]))
            if cfg["DL"][c]:
                act(A("yi", ln), Gp, idn, 2048.0, 1.0)
                ts(A("Fi", ln), A("yi", ln), W - 1, None, Alu.bitwise_and)
                act(A("Gc", ln), A("Fi", ln), idn, -2048.0, 1.0)
            else:
                act(A("Gs", ln), Gp, idn, 2048.0 - 2.0 ** 23, 1.0)
            if t: mm([(E1, MA, prev, True, False), (E2, MA, prev, False, False), (Q, QA, prev, False, False)])
            mm([(E1, DJ, Dc, not t, False), (E2, NDJ, Dc, False, False), (Q, QD, Dc, False, False)])
            mm([(E1, EC1, cl, False, False), (E2, EC2, cl, False, False), (Q, QC, cl, False, True)])
            many([act(hi, E1, sig, A("btc", s_(4 + t, 5 + t)), 400.0), act(lo, E2, sig, A("btc", s_(8 + t, 9 + t)), 400.0)])
            send(((hi, lo), A("hr%d" % t, ln), HN[t]))
            act(A(bits, ln), Q, sig, A("btc", s_(16 + t, 17 + t)), 400.0)
            stage[0] = 0.0
            if c == cfg["ZC"]: average()
        for c, (a, b) in enumerate(CH):
            n = b - a; ln = s_(a, b); up, Pt = at(c, "U"), at(c, "D", 1)
            hi, lo = A(HL, s_(2 * a, 2 * a + n)), A(HL, s_(2 * a + n, 2 * b))
            mm(grp(up, [(IB, hi), (NI, lo), (MF2, A(bits, ln))]))
            if cfg["DL"][c]:
                pr = A("pr%d" % t, ln)
                mm(grp(at(c, "X", 0), [(IB, A("Gc", ln)), (NI, pr)]) + grp(at(c, "X", 1), [(IB, pr), (NI, A(Pn, ln))]))
                ts(A("sq", ln), up, -1.0, None, Alu.not_equal)
                tt(at(c, "D"), A("sq", ln), at(c, "X", 0), Alu.mult)
                tt(at(c, "D", 1), A("sq", ln), at(c, "X", 1), Alu.mult)
                tt(at(c, "D", 3), A("mask2", ln), at(c, "D"), Alu.mult)
                tt(A("Lt", ln), A(Pn, ln), at(c, "D", 1), Alu.add)
                tt(A("tH", ln), A("Lt", ln), at(c, "D", 2), Alu.mult)
            else:
                act(A("sq", ln), up, Act.Square, 8192.0, 8192.0)
                mm(grp(Pt, [(IB, A("cst", 1, ln)), (IB, A(Pn, ln)), (NI, A("sq", ln))]))
                tt(A("Lt", ln), A("Gs", ln), Pt, Alu.max)
        kl, KR, KD = LP(16, 32), A("p0", s_(128, 128 + L)), A("p1", s_(0, L))
        mm([(KR, H64, A("vm"), True, False)])
        mm([(KD, IB, A("DC"), True, False), (KD, H64, A("vm"), False, False), (A("p1", s_(0, L, 16)), N64, A("vm", s_(0, L, 16)), False, False)])
        FA = A("p4", s_(0, L)); own = lambda e: A("sd", e, s_(15, L, 16))
        mm([(KR, MF32, A(bits), False, True)])
        mm(grp(FA, [(MA, A(bits))]))
        scan(A("sd", 0), A("SQ"), KR, Alu.add, Alu.max)
        scan(A("sd", 1), A("SQ"), FA, Alu.add, Alu.max)
        act(A("kb"), own(0), idn, C(OK), -1280.0)
        act(A("kc"), own(0), idn, C(OC), 1.0)
        act(A("ti", 1), own(0), idn, C(OW), 32.0)
        many([act(A("as%d" % t, e), own(1), sig, C(OA), -12.5) for e in range(3)])
        toint(A("ti", 0), LP(0, 16))
        mm([(KD, MF32, A(bits), False, False), (A("p1", s_(0, L, 16)), NF32, A(bits, s_(0, L, 16)), False, False)])
        mm([(A("p1", s_(r, L, 16)), NI, A("kc"), False, r == 15) for r in range(1, 16)])
        for a, b in CH:
            many([act(A("junk", h, s_(0, b - 16 * h - 16)), A("p0", s_(144 + 16 * h, 128 + b)), sig, A("kb", s_(h, h + 1)), 1280.0, A("ka", s_(h, h + 1)))
                  for h in range(a // 16, b // 16 - 1)])
        scan(A("sc"), KD, A("SP"), Alu.mult, Alu.add)
        for e in ([s_(0, 2)] if cfg["AM"] else [1, 0]): ts(A("bs", e), A("ti", e), NV - 1, None, Alu.bitwise_and)
        ts(A("fl", 0), A("sc", s_(15, L, 16)), 0.0, 2048.0, Alu.is_equal, Alu.mult)
        tt(A("fl", 1), A("fl", 0), A("bs", 1), Alu.add)
        aff(A("ki", 0), A("ka"), 2.0 ** 9, 2.0 ** 19, cfg["TI"])
        ts(A("ki", 1), A("ki", 0), 255 << 11, None, Alu.bitwise_and)
        tt(A("fl", 2), A("fl", 1), A("ki", 1), Alu.add)
        if cfg["TU"]:
            tt(A("woff"), A("fl", 2), A("lf"), Alu.min)
        else:
            tt(A("fl", 3), A("fl", 2), A("lf"), Alu.min)
            cp(A("woff"), A("fl", 3))
        send((A("as%d" % t), A("ar%d" % t), HZ[t]))
        if t == 0:
            act(A("B", s_(0, NV)), A("bagi"), idn, -2048.0, 1.0)
        if not cfg["XV"]:
            xp = A("p4", s_(0, L))
            mm(grp(xp, [(IB, A("zm")), (IB, z)]))
            act(A("xs"), xp, idn)
        ts(A("xm"), A("xs"), 0.0, 256.0, Alu.is_lt, Alu.mult)
        stage[0] = cfg["XB"]
        for a in range(0, L, cfg["XP"]):
            tt(ind(A("X"), A(of, 1, s_(a // 16, (a + cfg["XP"]) // 16))), A("xs", s_(a, a + cfg["XP"])), A("xm", s_(a, a + cfg["XP"])), Alu.add)
        stage[0] = 0.0
        if last:
            i = store("Y", A("X"), "yx", None, 3.5)
            ops[i]["after"] += [j for j, o_ in enumerate(ops) if o_["kind"] == "send"]
        ts(A("bs", 4), A("ti", 0), 15, None, Alu.bitwise_and)
        tt(A("dlt", s_(0, 2)), A("bs", s_(0, 5, 4)), A("bs", s_(1, 6, 4)), Alu.subtract)
        for c, (a, b) in enumerate(CH):
            ln = s_(a, b); hr = A("hr%d" % t, ln); H = at(c, "H")
            if cfg["DL"][c]:
                mm(grp(H, [(bd(14), A("tH", ln))], stop=False))
                tt(A("tF", ln), hr, at(c, "D", 3), Alu.mult)
                tt(at(c, "D", 1), hr, at(c, "D"), Alu.mult)
                mm(grp(H, [(A("SW"), A("tF", ln))], start=False))
                tt(A("Fc", ln), A("Lt", ln), at(c, "D", 1), Alu.add)
            else:
                Y = at(c, "D")
                mm(grp(Y, [(IB, A("cst", 0, ln)), (IB, A("pr%d" % t, ln))], stop=False))
                mm(grp(Y, [(MI, hr)], start=False))
                tt(A("yi", ln), A("Lt", ln), Y, Alu.max)
                ts(A("Fi", ln), A("yi", ln), W - 1, None, Alu.bitwise_and)
                act(A("Fc", ln), A("Fi", ln), idn, -2048.0, 1.0)
                if cfg["HF"][c]:
                    tt(A("tF", ln), A("Fi", ln), at(c, "D", 2), Alu.mult)
                    mm(grp(H, [(A("SW"), A("tF", ln))]))
                else:
                    tt(A("tH", ln), A("Fc", ln), at(c, "D", 2), Alu.mult)
                    mm(grp(H, [(bd(14), A("tH", ln))]))
            tt(A("t2", ln), A("mask2", ln), H, Alu.mult)
            tt(ind(A("B"), A("woff", s_(a // 16, b // 16))), A("Fc", ln), A("t2", ln), Alu.add)
        nx = "offs%d" % (t + 1)
        tt(A("prd"), A("ar%d" % t), A("dlt"), Alu.mult)
        tt(A(nx), A("prd"), A("bs", s_(1, 4)), Alu.add)
        if last: tt(A("res"), A("prd", 0), A("bs", 1), Alu.add)
        act(A("ZZ%d" % (t + 1), s_(0, L)), ind(A(Z), A(nx, 2)), Act.Copy)
    end = len(ops)
    store("Y", A("res"), "yv", None, 0.0)
    store("Y", A("ZZ3"), "yz", None, 0.3)
    h = NV // 4
    for e in range(2):
        pp = A("p%d" % (5 + e), s_(0, h))
        act(pp, A("B", s_(2 * h + e * h, 3 * h + e * h)), idn, 2048.0 * 4097, 4096.0)
        tt(A("pk", s_(e * h, e * h + h)), A("B", s_(e * h, e * h + h)), pp, Alu.add)
        store("YS"[e], A("pk", s_(e * h, e * h + h)), "yb", (e * h, e * h + h), 0.5)
    name = [(o["wr"] or o["rd"])[0] for o in ops]
    name = [o["eng"] + ":" + (b if b in o["banks"] else b.rstrip("0123456789")) + ":" + "".join(str(x[0]) for x in r) for o, (b, r) in zip(ops, name)]
    name = [x + "<" + o["args"][-1][2][0].rstrip("0123") + "".join(str(y[0]) for y in o["args"][-1][2][2]) if o["kind"] == "mm" else x for x, o in zip(name, ops)]
    for t, (a, b) in enumerate(zip(begin, begin[1:] + [end])):
        for i in range(a, b):
            ops[i]["role"] = (t, name[i] + "'" * name[i + 1:b].count(name[i]))
        for x, y in cfg["DUE"]:
            for i in range(a, b):
                if name[i] == x: ops[i]["due"] += [j for j in range(a, b) if name[j] == y][:1]
    return ops


COMP = ("many", "ts", "tt", "tts", "cp", "mset", "scan", "act", "mm", "iota")


def overlap(a, b):
    return all(x[0] < y[1] and y[0] < x[1] for x, y in zip(a, b))


def deps(ops):
    n = len(ops); pred = [set(o["after"]) for o in ops]; free = set()
    hist = {}
    for i, o in enumerate(ops):
        hard = set(o["after"])
        for b, r in o["rd"]:
            for j, rj, w in hist.get(b, ()):
                if w and overlap(r, rj): pred[i].add(j); hard.add(j)
        for b, r in o["wr"]:
            for j, rj, w in hist.get(b, ()):
                if overlap(r, rj):
                    pred[i].add(j)
                    if w: hard.add(j)
        for b, r in o["wr"]:
            hist[b] = [h for h in hist.get(b, []) if not all(x[0] <= y[0] and y[1] <= x[1] for x, y in zip(r, h[1]))] + [(i, r, True)]
        for b, r in o["rd"]:
            hist.setdefault(b, []).append((i, r, False))
        pred[i].discard(i)
        for j in pred[i]:
            if o["eng"] == "P" == ops[j]["eng"]: free.add((j, i))
    succ = [[] for _ in ops]
    for i in range(n):
        for j in pred[i] | set(ops[i]["soft"]): succ[j].append(i)
    return pred, succ, free


def costs(ops, fig):
    return [o["cost"][0] + o["cost"][1] * fig[o["cost"][2]]
            + (fig["ov"] * (len(o["args"]) if o["kind"] in ("tts", "many") else 1) if o["eng"] in "VS" else 0.0) for o in ops]


def place(ops, dp, prio, fig, back=False):
    pred, succ, free = dp
    n = len(ops); c = costs(ops, fig); sy = fig["sync"]
    if back:
        pred, succ = succ, [p | set(o["soft"]) for p, o in zip(pred, ops)]
    left = [len(p) if back else len(p | set(o["soft"])) for p, o in zip(pred, ops)]; ready = [i for i in range(n) if not left[i]]
    beg = [0.0] * n; fin = [0.0] * n; busy = {}; seq = []
    while ready:
        i = max(ready, key=lambda k: prio[k]); ready.remove(i); o = ops[i]; e = o["eng"]
        t = max([fin[j] + (0.0 if (j, i) in free or (i, j) in free else fig["own"] if ops[j]["eng"] == e else sy) for j in pred[i]] + [beg[j] + c[j] for j in o["soft"] if not back], default=0.0)
        if back: t += o["lat"]
        if e != "R":
            iv = [(a, b) for a, b, _ in busy.get(e, ()) if b > t]
            for k in o["banks"]:
                iv += [(a - sy, b + sy) for a, b, f in busy.get(k, ()) if f != e and b + sy > t]
            for a, b in sorted(iv):
                if t + c[i] <= a + 1e-9: break
                t = max(t, b)
            for k in [e] + list(o["banks"]):
                busy.setdefault(k, []).append((t, t + c[i], e))
        beg[i] = t; fin[i] = t + c[i] + (0.0 if back else o["lat"]); seq.append(i)
        for k in succ[i]:
            left[k] -= 1
            if not left[k]: ready.append(k)
    if back: return fin
    order = sorted(seq, key=lambda k: beg[k])
    full = [set(p) for p in pred]; last = {}
    for i in order:
        e = ops[i]["eng"]
        for k in ops[i]["banks"]:
            d = last.setdefault(k, {})
            full[i].update(j for f, j in d.items() if f != e)
            d[e] = i
    return order, full, beg, fin


def replay(ops, order, full, free, fig):
    c = costs(ops, fig); sy = fig["sync"]; busy = {}; fin = {}; beg = {}
    for i in order:
        e = ops[i]["eng"]
        t = max([fin[j] + (0.0 if (j, i) in free else fig["own"] if ops[j]["eng"] == e else sy) for j in full[i]], default=0.0)
        if e != "R":
            t = max(t, busy.get(e, 0.0)); busy[e] = t + c[i]
        beg[i] = t; fin[i] = t + c[i] + ops[i]["lat"]
    return max(fin.values()), beg, fin


def figs(fig):
    def slow(f, gam, sca, hop):
        return dict(fig, cy=f * fig["cy"], pcy=f * fig["pcy"], gam=f * gam * fig["gam"], sca=f * sca * fig["sca"], ov=f * fig["ov"],
                    sync=(0.5 + 0.5 * f) * fig["sync"], own=(0.5 + 0.5 * f) * fig["own"], hop=hop * fig["hop"])
    return [fig, slow(1.45, 1.25, 1.4, 1.15), slow(1.25, 0.72, 0.6, 1.25), slow(1.15, 1.25, 0.8, 0.9)]


MID = dict(FIG, cy=1e-3, pcy=0.5e-3, gam=1.6e-3, sca=3.8e-3, sync=0.155, own=0.2, ov=0.019, hop=3.4)


def plan(ops, cfg=CFG):
    dp = deps(ops); order = listed(ops, dp, cfg["ORDER"])
    for r in range(cfg["ROUNDS"]):
        if r: order = alike(ops, order, dp)
        order, full, free = polish(ops, order, dp, cfg["MOVES"], r, 150.0)
    return order, full, free


def plan0(ops, cfg=CFG, fig=MID):
    dp = deps(ops); succ = dp[1]
    n = len(ops); c = costs(ops, fig); best = None
    for seed in range(cfg["SEEDS"]):
        prio = [0.0] * n
        jit = np.random.RandomState(seed).uniform(1 - cfg["JIT"], 1 + cfg["JIT"], n)
        for i in list(range(n - 1, -1, -1)) * 3:
            prio[i] = (c[i] + ops[i]["lat"] + fig["sync"]) * (float(jit[i]) if seed else 1.0) + max([prio[k] for k in succ[i] + ops[i]["due"]], default=0.0)
        prio = [p + o["bias"] for p, o in zip(prio, ops)]
        for _ in range(cfg["IT"]):
            order, full, beg, fin = place(ops, dp, prio, fig)
            score = sum(replay(ops, order, full, dp[2], f)[0] / f["cy"] for f in figs(FIG))
            if best is None or score < best[0]: best = (score, order, full, dp[2])
            prio = place(ops, dp, fin, fig, True)
            prio = [p + (o["bias"] if o["bias"] >= 50 else 0.0) for p, o in zip(prio, ops)]
    return polish(ops, best[1], dp, cfg["MOVES"])


def listed(ops, dp, lists, fig=MID):
    pred, succ, free = dp; n = len(ops); c = costs(ops, fig)
    must = [p | set(o["soft"]) for p, o in zip(pred, ops)]
    byrole = {o["role"]: i for i, o in enumerate(ops) if o["role"]}
    line = {e: [byrole[(t, e + ":" + x)] for t in range(RO) for x in names.split() if (t, e + ":" + x) in byrole] for e, names in lists.items()}
    fixed = set(i for x in line.values() for i in x)
    prio = [0.0] * n
    for i in range(n - 1, -1, -1):
        prio[i] = c[i] + ops[i]["lat"] + fig["sync"] + max([prio[k] for k in succ[i]], default=0.0) + ops[i]["bias"]
    left = [len(p) for p in must]; ready = set(i for i in range(n) if not left[i]); fin = {}; busy = {}; seq = []
    while ready:
        can = [i for i in ready if i not in fixed or line[ops[i]["eng"]][0] == i] or list(ready)
        start = {i: max([fin[j] + fig["sync"] for j in must[i]] + [busy.get(ops[i]["eng"], 0.0)]) for i in can}
        i = min(can, key=lambda k: (round(start[k] * 5), k not in fixed, -prio[k]))
        if i in fixed: line[ops[i]["eng"]].remove(i)
        ready.remove(i); seq.append(i); fin[i] = start[i] + c[i] + ops[i]["lat"]
        if ops[i]["eng"] != "R": busy[ops[i]["eng"]] = start[i] + c[i]
        for k in succ[i]:
            left[k] -= 1
            if not left[k]: ready.add(k)
    return seq


def alike(ops, order, dp):
    must = [p | set(o["soft"]) for p, o in zip(dp[0], ops)]
    _, full, free = polish(ops, order, dp, 0)
    beg = replay(ops, order, full, free, MID)[1]
    zero = [min(beg[i] for i, o in enumerate(ops) if o["role"] and o["role"][0] == t) for t in range(RO)]
    best = None
    for s in range(-1, RO):
        pat = {o["role"][1]: beg[i] - zero[s] for i, o in enumerate(ops) if o["role"] and o["role"][0] == s}
        when = [zero[o["role"][0]] + pat[o["role"][1]] if o["role"] and o["role"][1] in pat else beg[i] for i, o in enumerate(ops)]
        left = [len(p) for p in must]; ready = [i for i, x in enumerate(left) if not x]; seq = []
        while ready:
            i = min(ready, key=lambda k: when[k]); ready.remove(i); seq.append(i)
            for k in dp[1][i]:
                left[k] -= 1
                if not left[k]: ready.append(k)
        _, full, free = polish(ops, seq, dp, 0)
        score = sum(replay(ops, seq, full, free, f)[0] / f["cy"] for f in figs(FIG))
        if best is None or score < best[0]: best = (score, seq)
    return best[1]


def polish(ops, order, dp, moves, seed=0, heat=300.0):
    pred, succ, free = dp
    fs = figs(FIG); cs = [costs(ops, f) for f in fs]
    eng = [o["eng"] for o in ops]; lat = [o["lat"] for o in ops]; banks = [tuple(o["banks"]) for o in ops]
    must = [p | set(o["soft"]) for p, o in zip(pred, ops)]
    lag = [[[(j, 0.0 if (j, i) in free else f["own"] if eng[j] == eng[i] else f["sync"]) for j in p] for i, p in enumerate(pred)] for f in fs]

    def score(seq, a=0, old=None):
        prev = {}; last = {}; held = []
        for n, i in enumerate(seq):
            e = eng[i]; h = []
            for b in banks[i]:
                d = last.setdefault(b, {})
                if n >= a: h += [j for f, j in d.items() if f != e]
                d[e] = i
            if n >= a: held.append((i, h, prev.get(e)))
            if e != "R": prev[e] = i
        res = []
        for k, f in enumerate(fs):
            c = cs[k]; sy = f["sync"]; lg = lag[k]
            fin, why = (list(old[k][0]), list(old[k][1])) if old else ([0.0] * len(ops), [None] * len(ops))
            for i, h, p in held:
                t = 0.0; w = None
                for j, d in lg[i]:
                    if fin[j] + d > t: t = fin[j] + d; w = (j, 0)
                for j in h:
                    if fin[j] + sy > t: t = fin[j] + sy; w = (j, 1)
                if p is not None and fin[p] - lat[p] > t: t = fin[p] - lat[p]; w = (p, 1)
                fin[i] = t + c[i] + lat[i]; why[i] = w
            res.append((fin, why))
        return sum(max(x[0]) / f["cy"] for x, f in zip(res, fs)), res
    rs = np.random.RandomState(seed); now, res = score(order); best = (now, order)
    for it in range(moves):
        fin, why = res[rs.randint(len(fs))]
        i = fin.index(max(fin)); held = []
        while why[i] is not None:
            if why[i][1] and why[i][0] not in must[i]: held.append((why[i][0], i))
            i = why[i][0]
        if not held: break
        j, i = held[rs.randint(len(held))]
        a, b = order.index(j), order.index(i); kind = rs.randint(4); far = int(rs.exponential(40))
        if kind == 2: a, b, i = max(0, a - 1 - far), a, j
        if kind == 3: b = min(len(order) - 1, b + far)
        mid = order[a:b + 1]
        if kind % 2 == 0:
            take = {i}
            for x in mid[::-1]:
                if any(y in take for y in succ[x]): take.add(x)
            seq = order[:a] + [x for x in mid if x in take] + [x for x in mid if x not in take] + order[b + 1:]
        else:
            take = {j}
            for x in mid:
                if must[x] & take: take.add(x)
            seq = order[:a] + [x for x in mid if x not in take] + [x for x in mid if x in take] + order[b + 1:]
        if seq == order: continue
        new, r = score(seq, a, res)
        if new < now + heat * (1 - it / moves) * rs.exponential():
            order, now, res = seq, new, r
            if now < best[0]: best = (now, order)
    order = best[1]; full = [set(p) for p in pred]; last = {}
    for i in order:
        for b in banks[i]:
            d = last.setdefault(b, {})
            full[i].update(j for f, j in d.items() if f != eng[i])
            d[eng[i]] = i
    return order, full, free


PLAN = []


def rank_program(g, core, T, topo):
    rank = T.rank_of(core)
    if rank is None:
        return
    if not PLAN:
        o_ = build(); PLAN.append(o_); PLAN.append(plan(o_))
    ops, (order, pred, free) = PLAN
    Q = {"V": g.vector, "S": g.scalar, "P": g.tensor, "G": g, "Y": g.sync}
    cores = T.cores
    eng = [e for e in topo.engines(cores[0], cores[1]) if all(e in topo.engines(a, b) for a in cores for b in cores if a != b)]
    mask = sum(1 << e for e in eng)
    pos = {}; cnt = {}
    for i in order:
        e = ops[i]["eng"]; cnt[e] = cnt.get(e, 0) + 1; pos[i] = cnt[e]
    seen = {}; waits = {}; need = set()
    for i in order:
        e = ops[i]["eng"]; w = []
        if e == "R": continue
        best = {}
        for j in pred[i]:
            oj = ops[j]
            if oj["kind"] in COMP:
                if (j, i) in free: continue
                if pos[j] > seen.get((e, oj["eng"]), 0) and pos[j] > pos.get(best.get(oj["eng"]), 0): best[oj["eng"]] = j
            elif oj["kind"] != "send" and (e, j) not in seen:
                seen[(e, j)] = 1; w.append(j)
        for f, j in best.items():
            seen[(e, f)] = pos[j]; need.add(j); w.append(j)
        waits[i] = w
    semof = {}; num = {}; nd = 0; nr = 0
    for i in order:
        o = ops[i]
        if o["kind"] in COMP:
            if i in need:
                num[o["eng"]] = num.get(o["eng"], 0) + 1; semof[i] = (T.sem["e" + o["eng"]], num[o["eng"]])
        elif o["kind"] in ("load", "store"):
            semof[i] = (T.sem["d%d" % nd], 16); nd += 1
        elif o["kind"] == "recv":
            semof[i] = (T.sem["r%d" % nr], len(eng)); semof[o["after"][0]] = semof[i]; nr += 1

    def R(a):
        if not isinstance(a, Ap): return a
        v = T[a[0]][(a[4] if a[4] is not None else slice(None),) + a[1]]
        return v.indirect(R(a[5])) if a[5] is not None else v

    def hbm(name, idx):
        return T[name][:] if idx is None else T[name][:, idx[0]:idx[1]]

    def call(q, k, a):
        if k == "ts":
            return q.tensor_scalar(R(a[0]), R(a[1]), R(a[2]), R(a[3]), *[x for x in a[4:6] if x is not None])
        if k == "tt": return q.tensor_tensor(R(a[0]), R(a[1]), R(a[2]), a[3])
        if k == "tts": return [q.tensor_tensor(R(m[0]), R(m[1]), R(m[2]), m[3]) for m in a][-1]
        if k == "cp": return q.tensor_copy(R(a[0]), R(a[1]))
        if k == "mset": return q.memset(R(a[0]), a[1])
        if k == "scan": return q.tensor_tensor_scan(R(a[0]), R(a[1]), R(a[2]), 0.0, a[3], a[4])
        if k == "act": return q.activation(R(a[0]), R(a[1]), a[2], bias=R(a[3]), scale=R(a[4]), accum_out=R(a[5]))
        if k == "mm": return [q.matmul(R(m[0]), R(m[1]), R(m[2]), m[3], m[4]) for m in a][-1]
        if SCRATCH[a[0][0]][2] == I32: return q.iota(R(a[0]), a[1], a[2], a[3])
        return q.iota(R(a[0]), a[1], a[2], a[3], allow_small_or_imprecise_dtypes=True)

    sent = 0
    for i in order:
        o = ops[i]; k = o["kind"]; a = o["args"]
        if k == "recv": continue
        q = Q[o["eng"]]
        for j in waits[i]:
            q.wait_ge(*semof[j])
        if k == "many":
            for m in a: ins = call(q, m["kind"], m["args"])
        elif k in COMP: ins = call(q, k, a)
        elif k == "load":
            q.dma_start(R(a[0]), hbm(a[1], a[2])).then_inc(semof[i][0], 16); continue
        elif k == "store":
            if o["after"]: q.wait_ge(T.sem.sent, len(eng) * len(o["after"]))
            q.dma_start(hbm(a[1], a[2]), R(a[0])).then_inc(semof[i][0], 16); continue
        else:
            sent += len(eng); to = [topo.addr(cores[(rank + x[2]) % N]) for x in a]
            if not isinstance(a[0][0], Ap):
                g.remote_dma_fused([RemoteDMATransfer(dst_ids=[DstId(rid=to[0][0], pnc=to[0][1])], dma_engine_mask=mask, remote_sem=semof[i][0],
                                                      srcs=[R(x) for x in a[0][0]], dsts=[R(a[0][1])], alu_op=1)], local_sem=T.sem.sent)
            elif len(a) == 1:
                g.remote_dma(R(a[0][1]), R(a[0][0]), semof[i][0], T.sem.sent, to[0][1], to[0][0], mask)
            else:
                m = len(eng) // len(a)
                g.remote_dma_fused([RemoteDMATransfer(dst_ids=[DstId(rid=to[j][0], pnc=to[j][1])], dma_engine_mask=sum(1 << e for e in eng[j * m:j * m + m]),
                                                      remote_sem=semof[i][0], src=R(x[0]), dst=R(x[1])) for j, x in enumerate(a)], local_sem=T.sem.sent)
            continue
        if i in need: ins.then_inc(semof[i][0], 1)
    for i in order:
        if ops[i]["kind"] == "store": g.sync.wait_ge(*semof[i])
    g.wait_ge(T.sem.sent, sent)
